import numpy as np
import ml_dtypes


def mxq(x, axis, fmt="e4m3"):
    dtype, down = {"e4m3": (ml_dtypes.float8_e4m3fn, 7), "e5m2": (ml_dtypes.float8_e5m2, 14)}[fmt]
    v = np.moveaxis(np.asarray(x, np.float32).astype(ml_dtypes.bfloat16).astype(np.float64), axis, -1)
    blocks = v.reshape(v.shape[:-1] + (-1, 32))
    amax = np.abs(blocks).max(-1, keepdims=True)
    byte = np.maximum(np.where(amax > 0, np.frexp(amax)[1] - 1 + 127, 0) - down, 1)
    scale = np.exp2(byte - 127.0)
    codes = (blocks / scale).astype(np.float32).astype(dtype).astype(np.float64)
    return np.moveaxis((codes * scale).reshape(v.shape), -1, axis)


WIDE = False


def mx_kscale(k):
    if not WIDE:
        return np.ones(k)
    levels = np.array([10, -10, 5, -5, 0])
    if k % 512:
        return np.exp2(np.random.permutation(np.resize(levels, k // 32))).repeat(32)
    a = np.empty((k // 512, 16))
    for p in range(k // 512):
        a[p, :8] = np.random.permutation(np.resize(levels, 8))
        for g in range(8):
            far = levels[np.abs(levels - a[p, g]) >= 10]
            a[p, g + 8] = far[np.random.randint(len(far))]
    return np.exp2(a.ravel()).repeat(32)


def f64(x):
    return np.asarray(x).astype(np.float64)


def striped(idx):
    return np.tile(np.asarray(idx).reshape(-1, 16).T, (8, 1)).astype(np.uint16)


def unstriped(offs):
    return offs[:16].T.reshape(-1).astype(np.int64)


E2M1 = np.array([0.0, 0.5, 1.0, 1.5, 2.0, 3.0, 4.0, 6.0, -0.0, -0.5, -1.0, -1.5, -2.0, -3.0, -4.0, -6.0])


def pack_weight(w, fmt):
    k, n = w.shape
    w = f64(np.asarray(w, np.float32).astype(ml_dtypes.bfloat16)).reshape(k // 32, 32, n)
    amax = np.abs(w).max(1)
    if fmt == "e4m3":
        byte = np.frexp(amax)[1] - 1 + 127 - 7
    else:
        mant, ex = np.frexp(amax / 6.0)
        byte = np.where(mant > 0.5, ex, ex - 1) + 127
    byte = np.clip(np.where(amax > 0, byte, 1), 1, 254)
    scaled = (w * np.exp2(127.0 - byte)[:, None, :]).reshape(k, n).astype(np.float32)
    by_word = np.ascontiguousarray(scaled.reshape(k // 512, 128, 4, n).transpose(0, 1, 3, 2))
    if fmt == "e4m3":
        words = by_word.astype(ml_dtypes.float8_e4m3fn).view(np.uint8)
    else:
        c = by_word.astype(ml_dtypes.float4_e2m1fn).view(np.uint8) & 0xF
        words = (c[..., 0::2] | (c[..., 1::2] << 4)).reshape(k // 512, 128, 2 * n)
    return np.ascontiguousarray(words), np.ascontiguousarray(byte.astype(np.uint8).reshape(k // 512, 16, n))


def unpack_weight(words, scales, fmt):
    g, _, n = scales.shape
    words = np.ascontiguousarray(words).reshape(g, 128, n, -1)
    if fmt == "e4m3":
        vals = words.view(ml_dtypes.float8_e4m3fn).astype(np.float64)
    else:
        nib = np.empty((g, 128, n, 4), np.uint8)
        nib[..., 0::2] = words & 0xF
        nib[..., 1::2] = words >> 4
        vals = E2M1[nib]
    vals = vals * np.repeat(np.exp2(scales.astype(np.float64) - 127.0), 8, axis=1)[..., None]
    return vals.transpose(0, 1, 3, 2).reshape(g * 512, n)


B, N, T, D, NQ = 1, 512, 2048, 1024, 512
DV = 512


def sgn(shape):
    return np.random.uniform(0.5, 2.0, shape) * np.where(np.random.standard_normal(shape) < 0, -1.0, 1.0)


def setup_inputs():
    n = np.random.standard_normal
    idx = np.sort(np.random.permutation(T)[:B * N].reshape(B, N), axis=1).reshape(-1)
    s = mx_kscale(D)[:, None]
    u = mx_kscale(N)
    ut = np.ones(T)
    ut[idx] = u
    kp = pack_weight(n((D, T)) / s, "e2m1")
    return {
        "qT": (n((B, D, NQ)) * s * (1.00 / np.sqrt(D))).astype(np.float32),
        "k_words": np.ascontiguousarray(kp[0].reshape(1, 2, 128, T, 2).transpose(0, 2, 3, 1, 4)).reshape(1, 128, T, 4),
        "k_scales": kp[1],
        "vT": (n((DV, T)) / ut).astype(np.float32),
        "nb": np.tile(0.5 * n(2048), (128, 1)).astype(np.float32),
        "us": (sgn((B, N, 1)) * u[:, None]).astype(np.float32),
        "offs": striped(idx),
    }


def reference(qT, k_words, k_scales, vT, nb, us, offs):
    idx = unstriped(offs)
    pick = lambda x, which: x[:, which].reshape(x.shape[0], B, -1).transpose(1, 0, 2)
    k = unpack_weight(k_words.reshape(1, 128, T, 2, 2).transpose(0, 3, 1, 2, 4).reshape(2, 128, 2 * T), k_scales, "e2m1")
    kg = pick(k, idx)
    qq = mxq(f64(qT), 1, "e4m3")
    a = kg.transpose(0, 2, 1) @ qq
    y = np.square(np.maximum(a + pick(f64(nb), idx)[:, :1, :].transpose(0, 2, 1), 0.0)) * f64(us)
    wq = mxq(y, 1, "e4m3")
    o = wq.transpose(0, 2, 1) @ mxq(pick(f64(vT), idx).transpose(0, 2, 1), 1, "e4m3")
    ms = np.mean(np.square(o), axis=-1, keepdims=True)
    r_ = o / np.sqrt(ms + 1e-05)
    return r_

@@ -1,0 +1,229 @@
+from contextlib import ExitStack
+
+import concourse.mybir as mybir
+from concourse.masks import make_identity
+
+N, T, D, NQ, DV = 512, 2048, 1024, 512, 512
+EPS = 1e-05
+FLOPS = 2 * N * D * NQ + 2 * N * NQ * DV
+BYTES = 4 * D * NQ + 4 * 128 * T + 32 * T + 4 * DV * T + 4 * T + 4 * N + 2 * 128 * (N // 16) + 4 * NQ * DV
+
+F32 = mybir.dt.float32
+BF16 = mybir.dt.bfloat16
+I32 = mybir.dt.int32
+U32 = mybir.dt.uint32
+U16 = mybir.dt.uint16
+U8 = mybir.dt.uint8
+FP8X4 = mybir.dt.float8_e4m3fn_x4
+FP4X4 = mybir.dt.float4_e2m1fn_x4
+ACT = mybir.ActivationFunctionType
+ALU = mybir.AluOpType
+
+P = 128
+PACK = 4
+PASSES = D // (P * PACK)
+E_BLOCKS = DV // P
+Q_BLOCKS = NQ // P
+HALF = NQ // 2
+Q_ON_VECTOR = (224, 320)
+TINY = 2.0 ** -100
+
+
+def interleaved(dst, src):
+    return (dst.rearrange("p (c i) t -> p c t i", i=4), src.rearrange("p t (c i) -> p c t i", i=4))
+
+
+def tile_attend_mlpb_relu2_srt_kernel(tc, qT, k_words, k_scales, vT, nb, us, offs, out):
+    nc = tc.nc
+    with ExitStack() as ctx:
+        keep = ctx.enter_context(tc.tile_pool(name="keep", bufs=1))
+        stage = ctx.enter_context(tc.tile_pool(name="stage", bufs=1))
+        psum = ctx.enter_context(tc.psum_pool(name="psum", bufs=1))
+
+        def shared(shape, dtype, name, slot):
+            return stage.tile(shape, dtype, name=name, tag=slot, align_bytes=64)
+
+        us_sb = keep.tile([P, PACK], F32, name="us_sb")
+        nc.sync.dma_start(us_sb[:], us[0].rearrange("(p j) o -> p (j o)", j=PACK))
+        offsets = keep.tile([P, N // 16], U16, name="offsets")
+        nc.sync.dma_start(offsets[:], offs)
+
+        kw_win = shared([P, T], I32, "kw_win", "a")
+        ks_win = shared([P, PASSES, T], U8, "ks_win", "b")
+        nb_win = shared([P, T], F32, "nb_win", "d")
+        nc.vector.memset(ks_win[:].rearrange("p o t -> p (o t)").bitcast(I32), 0)
+        nc.vector.memset(nb_win[:], 0.0)
+
+        nc.sync.dma_start(kw_win[:], k_words[0].rearrange("p t b -> p (t b)").bitcast(I32))
+        for r in range(4):
+            nc.scalar.dma_start(ks_win[r:P:32, :, :].bitcast(I32),
+                              k_scales[:, r:16:4, :].rearrange("o f t -> f o t").bitcast(I32))
+        NB_ROW = 8
+        nc.scalar.dma_start(nb_win[NB_ROW:NB_ROW + 1, :], nb[0:1, :])
+
+        inv_root = keep.tile([P, PACK], F32, name="inv_root")
+        mag = keep.tile([P, PACK], F32, name="mag")
+        sgn = keep.tile([P, 2, 2], BF16, name="sgn")
+        nc.scalar.activation(inv_root[:], us_sb[:], ACT.Abs_reciprocal_sqrt, bias=TINY)
+        nc.scalar.activation(mag[:], us_sb[:], ACT.Abs)
+        nc.scalar.activation(sgn[:], us_sb[:].rearrange("p (h u) -> p u h", u=2), ACT.Sign)
+        rough = keep.tile([P, PACK], F32, name="rough")
+        miss = keep.tile([P, PACK], F32, name="miss")
+        root = keep.tile([P, PACK], F32, name="root")
+        nc.gpsimd.tensor_tensor(rough[:], mag[:], inv_root[:], ALU.mult)
+        nc.gpsimd.tensor_tensor(miss[:], rough[:], rough[:], ALU.mult)
+        nc.gpsimd.tensor_tensor(miss[:], mag[:], miss[:], ALU.subtract)
+        nc.gpsimd.tensor_tensor(miss[:], miss[:], inv_root[:], ALU.mult)
+        nc.gpsimd.tensor_scalar(miss[:], miss[:], 0.5, 0.0, ALU.mult, ALU.add)
+        nc.gpsimd.tensor_tensor(root[:], rough[:], miss[:], ALU.add)
+
+        q_raw = [shared([P, PACK, NQ], F32, "q_raw%d" % g, ("c", "e")[g]) for g in range(PASSES)]
+        for g in range(PASSES):
+            nc.sync.dma_start(q_raw[g][:], qT[0, g * 512:(g + 1) * 512, :].rearrange("(p j) q -> p j q", j=PACK))
+
+        ident = keep.tile([P, P], F32, name="ident")
+        make_identity(nc, ident[:])
+
+        ks_g = keep.tile([P, PASSES, N], U8, name="ks_g")
+        for o in range(PASSES):
+            nc.vector.tensor_copy(ks_g[:, o, :], ks_win[:, o, :].indirect(offsets[:]))
+        kw_g = shared([P, 2, 2, P], U32, "kw_g", "b")
+        nc.vector.tensor_copy(kw_g[:].rearrange("g u h m -> g m h u"), kw_win[:].bitcast(U32).indirect(offsets[:]))
+        nb_g = keep.tile([P, N], F32, name="nb_g")
+        nc.vector.tensor_copy(nb_g[:], nb_win[:].indirect(offsets[:]))
+        k_codes = keep.tile([P, PASSES, N], U16, name="k_codes", align_bytes=64)
+        nc.vector.tensor_copy(k_codes[:],
+                              kw_g[:].rearrange("g u h m -> g (u h m)").bitcast(U16).rearrange("g (c o) -> g o c", o=2))
+        k_sc = keep.tile([P, PASSES, 2, 2, P], U8, name="k_sc", align_bytes=64)
+        nc.vector.tensor_copy(k_sc[:].rearrange("g o u h m -> g o m h u"),
+                              ks_g[:].rearrange("g o (m h u) -> g o m h u", h=2, u=2))
+
+        slot_of = [2 * (t % 2) + t // 2 for t in range(PACK)]
+        nb_ps = psum.tile([P, PACK, P], F32, name="nb_ps", tag="turn3")
+        for t in range(PACK):
+            nc.tensor.transpose(nb_ps[:, t, :], nb_g[:, slot_of[t]:N:PACK], ident[:])
+        bias = keep.tile([P, PACK], F32, name="bias")
+        for t in range(PACK):
+            j = slot_of[t]
+            nc.scalar.activation(bias[:, t:t + 1], nb_ps[:, t, NB_ROW:NB_ROW + 1], ACT.Copy, scale=root[:, j:j + 1])
+
+        q_codes = keep.tile([P, PASSES, NQ], U32, name="q_codes", align_bytes=64)
+        q_sc = keep.tile([P, PASSES, NQ], U8, name="q_sc", align_bytes=64)
+        scores = [psum.tile([P, NQ], F32, name="score%d" % t, tag="acc%d" % t) for t in range(PACK)]
+        for g in range(PASSES):
+            q_bf = shared([P, NQ, PACK], BF16, "q_bf%d" % g, ("d", "f")[g])
+            cut = Q_ON_VECTOR[g]
+            dst, src = interleaved(q_bf[:, cut:, :], q_raw[g][:, :, cut:])
+            nc.scalar.copy(dst, src)
+            dst, src = interleaved(q_bf[:, :cut, :], q_raw[g][:, :, :cut])
+            nc.vector.tensor_copy(dst, src)
+            nc.vector.quantize_mx(out=q_codes[:, g, :].bitcast(FP8X4), scales=q_sc[:, g, :],
+                                  in_=q_bf[:].rearrange("p q t -> p (q t)"))
+            for t in range(PACK):
+                nc.tensor.matmul_mx(out=scores[t][:],
+                                    lhsT=k_codes[:, g, t * P:(t + 1) * P].bitcast(FP4X4),
+                                    lhsT_scale=k_sc[:, g, t // 2, t % 2, :],
+                                    rhs=q_codes[:, g, :].bitcast(FP8X4), rhs_scale=q_sc[:, g, :],
+                                    start=(g == 0), stop=(g == PASSES - 1))
+
+        v_win = []
+        for e in range(E_BLOCKS):
+            w = shared([P, T], F32, "v_win%d" % e, "abcd"[e])
+            nc.sync.dma_start(w[:], vT[e * P:(e + 1) * P, :])
+            v_win.append(w)
+        v_bf = keep.tile([P, DV * PACK], BF16, name="v_bf", align_bytes=64)
+        v_codes = keep.tile([P, DV], U32, name="v_codes", align_bytes=64)
+        v_sc = keep.tile([P, DV], U8, name="v_sc", align_bytes=64)
+
+        def values(e):
+            v_g = shared([P, 2, P, 2], BF16, "v_g%d" % e, "g%d" % e)
+            nc.vector.tensor_copy(v_g[:].rearrange("e u p h -> e p h u"), v_win[e][:].indirect(offsets[:]))
+            v_ps = psum.tile([P, 2, P], F32, name="v_ps%d" % e, tag="turn%d" % e)
+            for u in range(2):
+                nc.tensor.transpose(v_ps[:, u, :], v_g[:, u, :, :].rearrange("e p h -> e (p h)").bitcast(F32), ident[:])
+            nc.scalar.copy(v_bf[:, e * P * PACK:(e + 1) * P * PACK].bitcast(F32).rearrange("p (e u) -> p e u", u=2), v_ps[:].rearrange("p u e -> p e u"))
+
+        def quantise_values(lo, hi):
+            nc.vector.quantize_mx(out=v_codes[:, lo:hi].bitcast(FP8X4), scales=v_sc[:, lo:hi],
+                                  in_=v_bf[:, lo * PACK:hi * PACK])
+
+        y_codes = keep.tile([P, NQ], U32, name="y_codes", align_bytes=64)
+        y_sc = keep.tile([P, NQ], U8, name="y_sc", align_bytes=64)
+
+        def rectify(h):
+            cols = slice(h * HALF, (h + 1) * HALF)
+            r = shared([P, PACK, HALF], F32, "relu%d" % h, "relu")
+            for t in range(PACK):
+                j = slot_of[t]
+                nc.scalar.activation(r[:, t, :], scores[t][:, cols], ACT.Relu, bias=bias[:, t:t + 1],
+                                     scale=root[:, j:j + 1])
+            return r
+
+        def square(h, r):
+            y_mag = shared([P, HALF, PACK], BF16, "y_mag%d" % h, "g%d" % h)
+            dst, src = interleaved(y_mag[:], r[:])
+            nc.scalar.activation(dst, src, ACT.Square)
+            return y_mag
+
+        def signed(h, y_mag):
+            y_bf = shared([P, HALF, PACK], BF16, "y_bf%d" % h, "bc"[h])
+            nc.vector.tensor_tensor(y_bf[:], y_mag[:],
+                                    sgn[:].rearrange("p u h -> p (u h)").unsqueeze(1).to_broadcast([P, HALF, PACK]), ALU.mult)
+            return y_bf
+
+        def quantise_weights(h, y_bf):
+            cols = slice(h * HALF, (h + 1) * HALF)
+            nc.vector.quantize_mx(out=y_codes[:, cols].bitcast(FP8X4), scales=y_sc[:, cols],
+                                  in_=y_bf[:].rearrange("p q t -> p (q t)"))
+
+        r0 = rectify(0)
+        values(0)
+        m0 = square(0, r0)
+        r1 = rectify(1)
+        values(1)
+        m1 = square(1, r1)
+        quantise_weights(0, signed(0, m0))
+        quantise_values(0, 2 * P)
+
+        sums = [psum.tile([P, DV], F32, name="sum%d" % b, tag="acc%d" % b) for b in range(Q_BLOCKS)]
+
+        def product(b, lo, hi):
+            nc.tensor.matmul_mx(out=sums[b][:, lo:hi],
+                                lhsT=y_codes[:, b * P:(b + 1) * P].bitcast(FP8X4), lhsT_scale=y_sc[:, b * P:(b + 1) * P],
+                                rhs=v_codes[:, lo:hi].bitcast(FP8X4), rhs_scale=v_sc[:, lo:hi], start=True, stop=True)
+
+        EARLY = 2 * P
+        early_sq = keep.tile([P, Q_BLOCKS], F32, name="early_sq")
+        squares = keep.tile([P, DV], BF16, name="squares")
+
+        def early(b):
+            product(b, 0, EARLY)
+            nc.scalar.activation(squares[:, :EARLY], sums[b][:, :EARLY], ACT.Square, accum_out=early_sq[:, b:b + 1])
+
+        early(0)
+        early(1)
+        values(2)
+        quantise_weights(1, signed(1, m1))
+        quantise_values(2 * P, 3 * P)
+        early(2)
+        early(3)
+        early_ms = keep.tile([P, Q_BLOCKS], F32, name="early_ms")
+        nc.gpsimd.tensor_scalar(early_ms[:], early_sq[:], 1.0 / DV, EPS, ALU.mult, ALU.add)
+        for b in range(Q_BLOCKS):
+            product(b, EARLY, 3 * P)
+        values(3)
+        quantise_values(3 * P, DV)
+        late_sq = keep.tile([P, Q_BLOCKS], F32, name="late_sq")
+        rstd = keep.tile([P, Q_BLOCKS], F32, name="rstd")
+        for b in range(Q_BLOCKS):
+            product(b, 3 * P, DV)
+        for b in range(Q_BLOCKS):
+            nc.scalar.activation(squares[:, EARLY:], sums[b][:, EARLY:], ACT.Square, accum_out=late_sq[:, b:b + 1])
+            nc.scalar.activation(rstd[:, b:b + 1], late_sq[:, b:b + 1], ACT.Abs_reciprocal_sqrt,
+                                 bias=early_ms[:, b:b + 1], scale=1.0 / DV)
+            res = keep.tile([P, DV], F32, name="res%d" % b)
+            if b < Q_BLOCKS - 1:
+                nc.vector.tensor_scalar(res[:], sums[b][:], rstd[:, b:b + 1], None, ALU.mult)
+            else:
+                nc.scalar.activation(res[:], sums[b][:], ACT.Copy, scale=rstd[:, b:b + 1])
+            nc.sync.dma_start(out[0, b * P:(b + 1) * P, :], res[:])

@@ -25,7 +25,7 @@ PASSES = D // (P * PACK)
 E_BLOCKS = DV // P
 Q_BLOCKS = NQ // P
 HALF = NQ // 2
-Q_ON_VECTOR = (224, 320)
+Q_ON_VECTOR = (0, 128)
 TINY = 2.0 ** -100
 
 
@@ -43,7 +43,7 @@ def tile_attend_mlpb_relu2_srt_kernel(tc, qT, k_words, k_scales, vT, nb, us, off
         def shared(shape, dtype, name, slot):
             return stage.tile(shape, dtype, name=name, tag=slot, align_bytes=64)
 
-        us_sb = keep.tile([P, PACK], F32, name="us_sb")
+        us_sb = shared([P, PACK], F32, "us_sb", "c")
         nc.sync.dma_start(us_sb[:], us[0].rearrange("(p j) o -> p (j o)", j=PACK))
         offsets = keep.tile([P, N // 16], U16, name="offsets")
         nc.sync.dma_start(offsets[:], offs)
@@ -52,16 +52,19 @@ def tile_attend_mlpb_relu2_srt_kernel(tc, qT, k_words, k_scales, vT, nb, us, off
         ks_win = shared([P, PASSES, T], U8, "ks_win", "b")
         nb_win = shared([P, T], F32, "nb_win", "d")
         nc.vector.memset(ks_win[:].rearrange("p o t -> p (o t)").bitcast(I32), 0)
-        nc.vector.memset(nb_win[:], 0.0)
+        nc.gpsimd.memset(nb_win[:], 0.0)
 
         nc.sync.dma_start(kw_win[:], k_words[0].rearrange("p t b -> p (t b)").bitcast(I32))
         for r in range(4):
-            nc.scalar.dma_start(ks_win[r:P:32, :, :].bitcast(I32),
+            nc.sync.dma_start(ks_win[r:P:32, :, :].bitcast(I32),
                               k_scales[:, r:16:4, :].rearrange("o f t -> f o t").bitcast(I32))
         NB_ROW = 8
-        nc.scalar.dma_start(nb_win[NB_ROW:NB_ROW + 1, :], nb[0:1, :])
+        nc.sync.dma_start(nb_win[NB_ROW:NB_ROW + 1, :], nb[0:1, :])
 
-        inv_root = keep.tile([P, PACK], F32, name="inv_root")
+        ident = keep.tile([P, P], F32, name="ident")
+        make_identity(nc, ident[:])
+
+        inv_root = shared([P, PACK], F32, "inv_root", "e")
         mag = keep.tile([P, PACK], F32, name="mag")
         sgn = keep.tile([P, 2, 2], BF16, name="sgn")
         nc.scalar.activation(inv_root[:], us_sb[:], ACT.Abs_reciprocal_sqrt, bias=TINY)
@@ -81,16 +84,11 @@ def tile_attend_mlpb_relu2_srt_kernel(tc, qT, k_words, k_scales, vT, nb, us, off
         for g in range(PASSES):
             nc.sync.dma_start(q_raw[g][:], qT[0, g * 512:(g + 1) * 512, :].rearrange("(p j) q -> p j q", j=PACK))
 
-        ident = keep.tile([P, P], F32, name="ident")
-        make_identity(nc, ident[:])
-
+        kw_g = keep.tile([P, 2, 2, P], U32, name="kw_g")
+        nc.vector.tensor_copy(kw_g[:].rearrange("g u h m -> g m h u"), kw_win[:].bitcast(U32).indirect(offsets[:]))
         ks_g = keep.tile([P, PASSES, N], U8, name="ks_g")
         for o in range(PASSES):
             nc.vector.tensor_copy(ks_g[:, o, :], ks_win[:, o, :].indirect(offsets[:]))
-        kw_g = shared([P, 2, 2, P], U32, "kw_g", "b")
-        nc.vector.tensor_copy(kw_g[:].rearrange("g u h m -> g m h u"), kw_win[:].bitcast(U32).indirect(offsets[:]))
-        nb_g = keep.tile([P, N], F32, name="nb_g")
-        nc.vector.tensor_copy(nb_g[:], nb_win[:].indirect(offsets[:]))
         k_codes = keep.tile([P, PASSES, N], U16, name="k_codes", align_bytes=64)
         nc.vector.tensor_copy(k_codes[:],
                               kw_g[:].rearrange("g u h m -> g (u h m)").bitcast(U16).rearrange("g (c o) -> g o c", o=2))
@@ -99,6 +97,30 @@ def tile_attend_mlpb_relu2_srt_kernel(tc, qT, k_words, k_scales, vT, nb, us, off
                               ks_g[:].rearrange("g o (m h u) -> g o m h u", h=2, u=2))
 
         slot_of = [2 * (t % 2) + t // 2 for t in range(PACK)]
+        q_sc = keep.tile([P, PASSES, NQ], U8, name="q_sc", align_bytes=64)
+        scores = [psum.tile([P, NQ], F32, name="score%d" % t, tag="acc%d" % t) for t in range(PACK)]
+
+        def first_layer_pass(g):
+            q_bf = shared([P, NQ, PACK], BF16, "q_bf%d" % g, "q_bf%d" % g)
+            cut = Q_ON_VECTOR[g]
+            dst, src = interleaved(q_bf[:, cut:, :], q_raw[g][:, :, cut:])
+            nc.scalar.copy(dst, src)
+            if cut:
+                dst, src = interleaved(q_bf[:, :cut, :], q_raw[g][:, :, :cut])
+                nc.vector.tensor_copy(dst, src)
+            q_codes = shared([P, NQ], U32, "q_codes%d" % g, ("q_codes0", "d")[g])
+            nc.vector.quantize_mx(out=q_codes[:].bitcast(FP8X4), scales=q_sc[:, g, :],
+                                  in_=q_bf[:].rearrange("p q t -> p (q t)"))
+            for t in range(PACK):
+                nc.tensor.matmul_mx(out=scores[t][:],
+                                    lhsT=k_codes[:, g, t * P:(t + 1) * P].bitcast(FP4X4),
+                                    lhsT_scale=k_sc[:, g, t // 2, t % 2, :],
+                                    rhs=q_codes[:].bitcast(FP8X4), rhs_scale=q_sc[:, g, :],
+                                    start=(g == 0), stop=(g == PASSES - 1))
+
+        first_layer_pass(0)
+        nb_g = shared([P, N], F32, "nb_g", "q_bf0")
+        nc.vector.tensor_copy(nb_g[:], nb_win[:].indirect(offsets[:]))
         nb_ps = psum.tile([P, PACK, P], F32, name="nb_ps", tag="turn3")
         for t in range(PACK):
             nc.tensor.transpose(nb_ps[:, t, :], nb_g[:, slot_of[t]:N:PACK], ident[:])
@@ -106,67 +128,44 @@ def tile_attend_mlpb_relu2_srt_kernel(tc, qT, k_words, k_scales, vT, nb, us, off
         for t in range(PACK):
             j = slot_of[t]
             nc.scalar.activation(bias[:, t:t + 1], nb_ps[:, t, NB_ROW:NB_ROW + 1], ACT.Copy, scale=root[:, j:j + 1])
-
-        q_codes = keep.tile([P, PASSES, NQ], U32, name="q_codes", align_bytes=64)
-        q_sc = keep.tile([P, PASSES, NQ], U8, name="q_sc", align_bytes=64)
-        scores = [psum.tile([P, NQ], F32, name="score%d" % t, tag="acc%d" % t) for t in range(PACK)]
-        for g in range(PASSES):
-            q_bf = shared([P, NQ, PACK], BF16, "q_bf%d" % g, ("d", "f")[g])
-            cut = Q_ON_VECTOR[g]
-            dst, src = interleaved(q_bf[:, cut:, :], q_raw[g][:, :, cut:])
-            nc.scalar.copy(dst, src)
-            dst, src = interleaved(q_bf[:, :cut, :], q_raw[g][:, :, :cut])
-            nc.vector.tensor_copy(dst, src)
-            nc.vector.quantize_mx(out=q_codes[:, g, :].bitcast(FP8X4), scales=q_sc[:, g, :],
-                                  in_=q_bf[:].rearrange("p q t -> p (q t)"))
-            for t in range(PACK):
-                nc.tensor.matmul_mx(out=scores[t][:],
-                                    lhsT=k_codes[:, g, t * P:(t + 1) * P].bitcast(FP4X4),
-                                    lhsT_scale=k_sc[:, g, t // 2, t % 2, :],
-                                    rhs=q_codes[:, g, :].bitcast(FP8X4), rhs_scale=q_sc[:, g, :],
-                                    start=(g == 0), stop=(g == PASSES - 1))
+        first_layer_pass(1)
 
         v_win = []
         for e in range(E_BLOCKS):
-            w = shared([P, T], F32, "v_win%d" % e, "abcd"[e])
+            w = shared([P, T], F32, "v_win%d" % e, "abce"[e])
             nc.sync.dma_start(w[:], vT[e * P:(e + 1) * P, :])
             v_win.append(w)
-        v_bf = keep.tile([P, DV * PACK], BF16, name="v_bf", align_bytes=64)
-        v_codes = keep.tile([P, DV], U32, name="v_codes", align_bytes=64)
+        v_bf = [shared([P, 2, P * PACK], BF16, "v_bf%d" % i, ("b", "v_bf1")[i]) for i in range(2)]
         v_sc = keep.tile([P, DV], U8, name="v_sc", align_bytes=64)
+        y_codes = keep.tile([P, NQ], U32, name="y_codes", align_bytes=64)
+        y_sc = keep.tile([P, NQ], U8, name="y_sc", align_bytes=64)
 
         def values(e):
-            v_g = shared([P, 2, P, 2], BF16, "v_g%d" % e, "g%d" % e)
+            v_g = keep.tile([P, 2, P, 2], BF16, name="v_g%d" % e)
             nc.vector.tensor_copy(v_g[:].rearrange("e u p h -> e p h u"), v_win[e][:].indirect(offsets[:]))
             v_ps = psum.tile([P, 2, P], F32, name="v_ps%d" % e, tag="turn%d" % e)
             for u in range(2):
                 nc.tensor.transpose(v_ps[:, u, :], v_g[:, u, :, :].rearrange("e p h -> e (p h)").bitcast(F32), ident[:])
-            nc.scalar.copy(v_bf[:, e * P * PACK:(e + 1) * P * PACK].bitcast(F32).rearrange("p (e u) -> p e u", u=2), v_ps[:].rearrange("p u e -> p e u"))
+            return v_ps
 
-        def quantise_values(lo, hi):
-            nc.vector.quantize_mx(out=v_codes[:, lo:hi].bitcast(FP8X4), scales=v_sc[:, lo:hi],
-                                  in_=v_bf[:, lo * PACK:hi * PACK])
+        def copy_out(e, v_ps):
+            copy = nc.vector.tensor_copy if e < 2 else nc.scalar.copy
+            copy(v_bf[e // 2][:, e % 2, :].bitcast(F32).rearrange("p (e u) -> p e u", u=2),
+                 v_ps[:].rearrange("p u e -> p e u"))
 
-        y_codes = keep.tile([P, NQ], U32, name="y_codes", align_bytes=64)
-        y_sc = keep.tile([P, NQ], U8, name="y_sc", align_bytes=64)
+        def quantise_values(i):
+            cols = slice(i * 2 * P, (i + 1) * 2 * P)
+            nc.vector.quantize_mx(out=v_codes[:, cols].bitcast(FP8X4), scales=v_sc[:, cols],
+                                  in_=v_bf[i][:].rearrange("p e c -> p (e c)"))
 
-        def rectify(h):
-            cols = slice(h * HALF, (h + 1) * HALF)
-            r = shared([P, PACK, HALF], F32, "relu%d" % h, "relu")
-            for t in range(PACK):
-                j = slot_of[t]
-                nc.scalar.activation(r[:, t, :], scores[t][:, cols], ACT.Relu, bias=bias[:, t:t + 1],
-                                     scale=root[:, j:j + 1])
-            return r
-
-        def square(h, r):
-            y_mag = shared([P, HALF, PACK], BF16, "y_mag%d" % h, "g%d" % h)
-            dst, src = interleaved(y_mag[:], r[:])
+        def square(h):
+            y_mag = keep.tile([P, HALF, PACK], BF16, name="y_mag%d" % h)
+            dst, src = interleaved(y_mag[:], relu[:, :, h * HALF:(h + 1) * HALF])
             nc.scalar.activation(dst, src, ACT.Square)
             return y_mag
 
         def signed(h, y_mag):
-            y_bf = shared([P, HALF, PACK], BF16, "y_bf%d" % h, "bc"[h])
+            y_bf = shared([P, HALF, PACK], BF16, "y_bf%d" % h, "be"[h])
             nc.vector.tensor_tensor(y_bf[:], y_mag[:],
                                     sgn[:].rearrange("p u h -> p (u h)").unsqueeze(1).to_broadcast([P, HALF, PACK]), ALU.mult)
             return y_bf
@@ -176,54 +175,46 @@ def tile_attend_mlpb_relu2_srt_kernel(tc, qT, k_words, k_scales, vT, nb, us, off
             nc.vector.quantize_mx(out=y_codes[:, cols].bitcast(FP8X4), scales=y_sc[:, cols],
                                   in_=y_bf[:].rearrange("p q t -> p (q t)"))
 
-        r0 = rectify(0)
-        values(0)
-        m0 = square(0, r0)
-        r1 = rectify(1)
-        values(1)
-        m1 = square(1, r1)
+        relu = keep.tile([P, PACK, NQ], F32, name="relu")
+        for t in range(PACK):
+            j = slot_of[t]
+            nc.scalar.activation(relu[:, t, :], scores[t][:], ACT.Relu, bias=bias[:, t:t + 1], scale=root[:, j:j + 1])
+        m0 = square(0)
+        m1 = square(1)
+        turned = [values(0), values(1)]
+        copy_out(0, turned[0])
+        copy_out(1, turned[1])
+        copy_out(2, values(2))
+        v_codes = shared([P, DV], U32, "v_codes", "c")
+        quantise_values(0)
         quantise_weights(0, signed(0, m0))
-        quantise_values(0, 2 * P)
 
         sums = [psum.tile([P, DV], F32, name="sum%d" % b, tag="acc%d" % b) for b in range(Q_BLOCKS)]
+        squares = keep.tile([P, DV], BF16, name="squares")
 
-        def product(b, lo, hi):
+        def product(b, lo, hi, sum_sq):
             nc.tensor.matmul_mx(out=sums[b][:, lo:hi],
                                 lhsT=y_codes[:, b * P:(b + 1) * P].bitcast(FP8X4), lhsT_scale=y_sc[:, b * P:(b + 1) * P],
                                 rhs=v_codes[:, lo:hi].bitcast(FP8X4), rhs_scale=v_sc[:, lo:hi], start=True, stop=True)
+            nc.scalar.activation(squares[:, lo:hi], sums[b][:, lo:hi], ACT.Square, accum_out=sum_sq[:, b:b + 1])
 
         EARLY = 2 * P
-        early_sq = keep.tile([P, Q_BLOCKS], F32, name="early_sq")
-        squares = keep.tile([P, DV], BF16, name="squares")
-
-        def early(b):
-            product(b, 0, EARLY)
-            nc.scalar.activation(squares[:, :EARLY], sums[b][:, :EARLY], ACT.Square, accum_out=early_sq[:, b:b + 1])
-
-        early(0)
-        early(1)
-        values(2)
-        quantise_weights(1, signed(1, m1))
-        quantise_values(2 * P, 3 * P)
-        early(2)
-        early(3)
-        early_ms = keep.tile([P, Q_BLOCKS], F32, name="early_ms")
+        early_sq = keep.tile([P, 2], F32, name="early_sq")
+        early_ms = keep.tile([P, 2], F32, name="early_ms")
+        for b in range(2):
+            product(b, 0, EARLY, early_sq)
         nc.gpsimd.tensor_scalar(early_ms[:], early_sq[:], 1.0 / DV, EPS, ALU.mult, ALU.add)
-        for b in range(Q_BLOCKS):
-            product(b, EARLY, 3 * P)
-        values(3)
-        quantise_values(3 * P, DV)
+        copy_out(3, values(3))
+        y1 = signed(1, m1)
+        quantise_values(1)
+        quantise_weights(1, y1)
+
         late_sq = keep.tile([P, Q_BLOCKS], F32, name="late_sq")
         rstd = keep.tile([P, Q_BLOCKS], F32, name="rstd")
         for b in range(Q_BLOCKS):
-            product(b, 3 * P, DV)
-        for b in range(Q_BLOCKS):
-            nc.scalar.activation(squares[:, EARLY:], sums[b][:, EARLY:], ACT.Square, accum_out=late_sq[:, b:b + 1])
+            product(b, EARLY if b < 2 else 0, DV, late_sq)
             nc.scalar.activation(rstd[:, b:b + 1], late_sq[:, b:b + 1], ACT.Abs_reciprocal_sqrt,
-                                 bias=early_ms[:, b:b + 1], scale=1.0 / DV)
+                                 bias=early_ms[:, b:b + 1] if b < 2 else EPS, scale=1.0 / DV)
             res = keep.tile([P, DV], F32, name="res%d" % b)
-            if b < Q_BLOCKS - 1:
-                nc.vector.tensor_scalar(res[:], sums[b][:], rstd[:, b:b + 1], None, ALU.mult)
-            else:
-                nc.scalar.activation(res[:], sums[b][:], ACT.Copy, scale=rstd[:, b:b + 1])
+            nc.vector.tensor_scalar(res[:], sums[b][:], rstd[:, b:b + 1], None, ALU.mult)
             nc.sync.dma_start(out[0, b * P:(b + 1) * P, :], res[:])

@@ -25,7 +25,7 @@ PASSES = D // (P * PACK)
 E_BLOCKS = DV // P
 Q_BLOCKS = NQ // P
 HALF = NQ // 2
-Q_ON_VECTOR = (0, 128)
+Q_ON_VECTOR = (0, 192)
 TINY = 2.0 ** -100
 
 
@@ -38,69 +38,86 @@ def tile_attend_mlpb_relu2_srt_kernel(tc, qT, k_words, k_scales, vT, nb, us, off
     with ExitStack() as ctx:
         keep = ctx.enter_context(tc.tile_pool(name="keep", bufs=1))
         stage = ctx.enter_context(tc.tile_pool(name="stage", bufs=1))
+        turns = ctx.enter_context(tc.tile_pool(name="turns", bufs=1))
         psum = ctx.enter_context(tc.psum_pool(name="psum", bufs=1))
 
         def shared(shape, dtype, name, slot):
             return stage.tile(shape, dtype, name=name, tag=slot, align_bytes=64)
 
-        us_sb = shared([P, PACK], F32, "us_sb", "c")
+        def placed(shape, dtype, name, offset):
+            return turns.tile(shape, dtype, name=name, offset=offset, align_bytes=64)
+
+        us_sb = placed([P, PACK], F32, "us_sb", 0)
         nc.sync.dma_start(us_sb[:], us[0].rearrange("(p j) o -> p (j o)", j=PACK))
         offsets = keep.tile([P, N // 16], U16, name="offsets")
         nc.sync.dma_start(offsets[:], offs)
 
-        kw_win = shared([P, T], I32, "kw_win", "a")
-        ks_win = shared([P, PASSES, T], U8, "ks_win", "b")
+        kw_win = keep.tile([P, T], I32, name="kw_win")
+        ks_win = keep.tile([P, T], U8, name="ks_win")
         nb_win = shared([P, T], F32, "nb_win", "d")
-        nc.vector.memset(ks_win[:].rearrange("p o t -> p (o t)").bitcast(I32), 0)
-        nc.gpsimd.memset(nb_win[:], 0.0)
+        ident = keep.tile([P, P], F32, name="ident")
+        make_identity(nc, ident[:])
+        k_sc = [keep.tile([P, 2, 2, P], U8, name="k_sc%d" % g, align_bytes=64) for g in range(PASSES)]
+        nc.vector.memset(ks_win[:].bitcast(I32), 0)
+        nc.vector.memset(nb_win[:, :T // 2], 0.0)
+        nc.gpsimd.memset(nb_win[:, T // 2:], 0.0)
+        nc.vector.memset(k_sc[1][:].rearrange("g u h m -> g (u h m)").bitcast(I32), 0)
 
         nc.sync.dma_start(kw_win[:], k_words[0].rearrange("p t b -> p (t b)").bitcast(I32))
-        for r in range(4):
-            nc.sync.dma_start(ks_win[r:P:32, :, :].bitcast(I32),
-                              k_scales[:, r:16:4, :].rearrange("o f t -> f o t").bitcast(I32))
+        for quad in range(4):
+            nc.sync.dma_start(ks_win[32 * quad:32 * quad + 8, :].bitcast(I32),
+                              k_scales[:, 4 * quad:4 * quad + 4, :].bitcast(I32))
         NB_ROW = 8
         nc.sync.dma_start(nb_win[NB_ROW:NB_ROW + 1, :], nb[0:1, :])
 
-        ident = keep.tile([P, P], F32, name="ident")
-        make_identity(nc, ident[:])
-
-        inv_root = shared([P, PACK], F32, "inv_root", "e")
+        inv_root = placed([P, PACK], F32, "inv_root", 4 * T)
         mag = keep.tile([P, PACK], F32, name="mag")
         sgn = keep.tile([P, 2, 2], BF16, name="sgn")
         nc.scalar.activation(inv_root[:], us_sb[:], ACT.Abs_reciprocal_sqrt, bias=TINY)
         nc.scalar.activation(mag[:], us_sb[:], ACT.Abs)
         nc.scalar.activation(sgn[:], us_sb[:].rearrange("p (h u) -> p u h", u=2), ACT.Sign)
         rough = keep.tile([P, PACK], F32, name="rough")
+        gap = shared([P, PACK], F32, "gap", "a")
         miss = keep.tile([P, PACK], F32, name="miss")
         root = keep.tile([P, PACK], F32, name="root")
         nc.gpsimd.tensor_tensor(rough[:], mag[:], inv_root[:], ALU.mult)
         nc.gpsimd.tensor_tensor(miss[:], rough[:], rough[:], ALU.mult)
-        nc.gpsimd.tensor_tensor(miss[:], mag[:], miss[:], ALU.subtract)
-        nc.gpsimd.tensor_tensor(miss[:], miss[:], inv_root[:], ALU.mult)
+        nc.gpsimd.tensor_tensor(gap[:], mag[:], miss[:], ALU.subtract)
+        nc.gpsimd.tensor_tensor(miss[:], gap[:], inv_root[:], ALU.mult)
         nc.gpsimd.tensor_scalar(miss[:], miss[:], 0.5, 0.0, ALU.mult, ALU.add)
         nc.gpsimd.tensor_tensor(root[:], rough[:], miss[:], ALU.add)
 
-        q_raw = [shared([P, PACK, NQ], F32, "q_raw%d" % g, ("c", "e")[g]) for g in range(PASSES)]
+        q_raw = [placed([P, PACK, NQ], F32, "q_raw%d" % g, g * 4 * T) for g in range(PASSES)]
         for g in range(PASSES):
             nc.sync.dma_start(q_raw[g][:], qT[0, g * 512:(g + 1) * 512, :].rearrange("(p j) q -> p j q", j=PACK))
 
+        v_win = [shared([P, T], F32, "v_win0", "a")]
+        nc.sync.dma_start(v_win[0][:], vT[0:P, :])
+
         kw_g = keep.tile([P, 2, 2, P], U32, name="kw_g")
         nc.vector.tensor_copy(kw_g[:].rearrange("g u h m -> g m h u"), kw_win[:].bitcast(U32).indirect(offsets[:]))
-        ks_g = keep.tile([P, PASSES, N], U8, name="ks_g")
-        for o in range(PASSES):
-            nc.vector.tensor_copy(ks_g[:, o, :], ks_win[:, o, :].indirect(offsets[:]))
+        ks_g = shared([P, N], U8, "ks_g", "b")
+        nc.vector.tensor_copy(ks_g[:], ks_win[:].indirect(offsets[:]))
         k_codes = keep.tile([P, PASSES, N], U16, name="k_codes", align_bytes=64)
         nc.vector.tensor_copy(k_codes[:],
                               kw_g[:].rearrange("g u h m -> g (u h m)").bitcast(U16).rearrange("g (c o) -> g o c", o=2))
-        k_sc = keep.tile([P, PASSES, 2, 2, P], U8, name="k_sc", align_bytes=64)
-        nc.vector.tensor_copy(k_sc[:].rearrange("g o u h m -> g o m h u"),
-                              ks_g[:].rearrange("g o (m h u) -> g o m h u", h=2, u=2))
+        nc.vector.tensor_copy(k_sc[0][:].rearrange("g u h m -> g m h u"),
+                              ks_g[:].rearrange("g (m h u) -> g m h u", h=2, u=2))
+        for quad in range(4):
+            rows = 32 * quad
+            nc.sync.dma_start(k_sc[1][rows:rows + 4].rearrange("g u h m -> g (u h m)").bitcast(I32),
+                              k_sc[0][rows + 4:rows + 8].rearrange("g u h m -> g (u h m)").bitcast(I32))
 
         slot_of = [2 * (t % 2) + t // 2 for t in range(PACK)]
-        q_sc = keep.tile([P, PASSES, NQ], U8, name="q_sc", align_bytes=64)
-        scores = [psum.tile([P, NQ], F32, name="score%d" % t, tag="acc%d" % t) for t in range(PACK)]
+        nb_g = keep.tile([P, N], F32, name="nb_g")
+        nc.vector.tensor_copy(nb_g[:], nb_win[:].indirect(offsets[:]))
+        nb_ps = [psum.tile([P, 2, P], F32, name="nb_ps%d" % u, tag="acc%d" % (2 + u)) for u in range(2)]
+        for t in range(PACK):
+            nc.tensor.transpose(nb_ps[t // 2][:, t % 2, :], nb_g[:, slot_of[t]:N:PACK], ident[:])
 
-        def first_layer_pass(g):
+        q_sc = keep.tile([P, PASSES, NQ], U8, name="q_sc", align_bytes=64)
+        q_codes = []
+        for g in range(PASSES):
             q_bf = shared([P, NQ, PACK], BF16, "q_bf%d" % g, "q_bf%d" % g)
             cut = Q_ON_VECTOR[g]
             dst, src = interleaved(q_bf[:, cut:, :], q_raw[g][:, :, cut:])
@@ -108,48 +125,44 @@ def tile_attend_mlpb_relu2_srt_kernel(tc, qT, k_words, k_scales, vT, nb, us, off
             if cut:
                 dst, src = interleaved(q_bf[:, :cut, :], q_raw[g][:, :, :cut])
                 nc.vector.tensor_copy(dst, src)
-            q_codes = shared([P, NQ], U32, "q_codes%d" % g, ("q_codes0", "d")[g])
-            nc.vector.quantize_mx(out=q_codes[:].bitcast(FP8X4), scales=q_sc[:, g, :],
+            q_codes.append(shared([P, NQ], U32, "q_codes%d" % g, ("d", "q_codes1")[g]))
+            nc.vector.quantize_mx(out=q_codes[g][:].bitcast(FP8X4), scales=q_sc[:, g, :],
                                   in_=q_bf[:].rearrange("p q t -> p (q t)"))
-            for t in range(PACK):
+        bias = shared([P, 2, 2], F32, "bias", "q_bf1")
+        for u in range(2):
+            nc.vector.tensor_tensor(bias[:, u, :], nb_ps[u][:, :, NB_ROW], root[:, u:PACK:2], ALU.mult)
+
+        scores = [psum.tile([P, NQ], F32, name="score%d" % t, tag="acc%d" % t) for t in range(PACK)]
+        relu = keep.tile([P, PACK, NQ], F32, name="relu")
+        for t in range(PACK):
+            for g in range(PASSES):
                 nc.tensor.matmul_mx(out=scores[t][:],
                                     lhsT=k_codes[:, g, t * P:(t + 1) * P].bitcast(FP4X4),
-                                    lhsT_scale=k_sc[:, g, t // 2, t % 2, :],
-                                    rhs=q_codes[:].bitcast(FP8X4), rhs_scale=q_sc[:, g, :],
+                                    lhsT_scale=k_sc[g][:, t // 2, t % 2, :],
+                                    rhs=q_codes[g][:].bitcast(FP8X4), rhs_scale=q_sc[:, g, :],
                                     start=(g == 0), stop=(g == PASSES - 1))
-
-        first_layer_pass(0)
-        nb_g = shared([P, N], F32, "nb_g", "q_bf0")
-        nc.vector.tensor_copy(nb_g[:], nb_win[:].indirect(offsets[:]))
-        nb_ps = psum.tile([P, PACK, P], F32, name="nb_ps", tag="turn3")
-        for t in range(PACK):
-            nc.tensor.transpose(nb_ps[:, t, :], nb_g[:, slot_of[t]:N:PACK], ident[:])
-        bias = keep.tile([P, PACK], F32, name="bias")
-        for t in range(PACK):
             j = slot_of[t]
-            nc.scalar.activation(bias[:, t:t + 1], nb_ps[:, t, NB_ROW:NB_ROW + 1], ACT.Copy, scale=root[:, j:j + 1])
-        first_layer_pass(1)
+            nc.scalar.activation(relu[:, t, :], scores[t][:], ACT.Relu,
+                                 bias=bias[:, t // 2, t % 2:t % 2 + 1], scale=root[:, j:j + 1])
 
-        v_win = []
-        for e in range(E_BLOCKS):
-            w = shared([P, T], F32, "v_win%d" % e, "abce"[e])
+        for e in range(1, E_BLOCKS):
+            w = shared([P, T], F32, "v_win1", "b") if e == 1 else placed([P, T], F32, "v_win%d" % e, (e - 2) * 4 * T)
             nc.sync.dma_start(w[:], vT[e * P:(e + 1) * P, :])
             v_win.append(w)
         v_bf = [shared([P, 2, P * PACK], BF16, "v_bf%d" % i, ("b", "v_bf1")[i]) for i in range(2)]
         v_sc = keep.tile([P, DV], U8, name="v_sc", align_bytes=64)
-        y_codes = keep.tile([P, NQ], U32, name="y_codes", align_bytes=64)
         y_sc = keep.tile([P, NQ], U8, name="y_sc", align_bytes=64)
 
         def values(e):
-            v_g = keep.tile([P, 2, P, 2], BF16, name="v_g%d" % e)
+            v_g = shared([P, 2, P, 2], BF16, "v_g%d" % e, "g%d" % e)
             nc.vector.tensor_copy(v_g[:].rearrange("e u p h -> e p h u"), v_win[e][:].indirect(offsets[:]))
-            v_ps = psum.tile([P, 2, P], F32, name="v_ps%d" % e, tag="turn%d" % e)
+            v_ps = psum.tile([P, 2, P], F32, name="v_ps%d" % e, tag=("acc0", "acc1", "turn2", "turn3")[e])
             for u in range(2):
                 nc.tensor.transpose(v_ps[:, u, :], v_g[:, u, :, :].rearrange("e p h -> e (p h)").bitcast(F32), ident[:])
             return v_ps
 
         def copy_out(e, v_ps):
-            copy = nc.vector.tensor_copy if e < 2 else nc.scalar.copy
+            copy = nc.vector.tensor_copy if e == 0 else nc.scalar.copy
             copy(v_bf[e // 2][:, e % 2, :].bitcast(F32).rearrange("p (e u) -> p e u", u=2),
                  v_ps[:].rearrange("p u e -> p e u"))
 
@@ -159,13 +172,13 @@ def tile_attend_mlpb_relu2_srt_kernel(tc, qT, k_words, k_scales, vT, nb, us, off
                                   in_=v_bf[i][:].rearrange("p e c -> p (e c)"))
 
         def square(h):
-            y_mag = keep.tile([P, HALF, PACK], BF16, name="y_mag%d" % h)
+            y_mag = shared([P, HALF, PACK], BF16, "y_mag%d" % h, ("m", "g1")[h])
             dst, src = interleaved(y_mag[:], relu[:, :, h * HALF:(h + 1) * HALF])
             nc.scalar.activation(dst, src, ACT.Square)
             return y_mag
 
         def signed(h, y_mag):
-            y_bf = shared([P, HALF, PACK], BF16, "y_bf%d" % h, "be"[h])
+            y_bf = placed([P, HALF, PACK], BF16, "y_bf%d" % h, h * 4 * T)
             nc.vector.tensor_tensor(y_bf[:], y_mag[:],
                                     sgn[:].rearrange("p u h -> p (u h)").unsqueeze(1).to_broadcast([P, HALF, PACK]), ALU.mult)
             return y_bf
@@ -175,19 +188,19 @@ def tile_attend_mlpb_relu2_srt_kernel(tc, qT, k_words, k_scales, vT, nb, us, off
             nc.vector.quantize_mx(out=y_codes[:, cols].bitcast(FP8X4), scales=y_sc[:, cols],
                                   in_=y_bf[:].rearrange("p q t -> p (q t)"))
 
-        relu = keep.tile([P, PACK, NQ], F32, name="relu")
-        for t in range(PACK):
-            j = slot_of[t]
-            nc.scalar.activation(relu[:, t, :], scores[t][:], ACT.Relu, bias=bias[:, t:t + 1], scale=root[:, j:j + 1])
         m0 = square(0)
-        m1 = square(1)
         turned = [values(0), values(1)]
         copy_out(0, turned[0])
         copy_out(1, turned[1])
+        m1 = square(1)
         copy_out(2, values(2))
-        v_codes = shared([P, DV], U32, "v_codes", "c")
+        y0 = signed(0, m0)
+        v_codes = placed([P, DV], U32, "v_codes", T)
         quantise_values(0)
-        quantise_weights(0, signed(0, m0))
+        copy_out(3, values(3))
+        y_codes = placed([P, NQ], U32, "y_codes", 4 * T + T)
+        quantise_weights(0, y0)
+        y1 = signed(1, m1)
 
         sums = [psum.tile([P, DV], F32, name="sum%d" % b, tag="acc%d" % b) for b in range(Q_BLOCKS)]
         squares = keep.tile([P, DV], BF16, name="squares")
@@ -203,9 +216,7 @@ def tile_attend_mlpb_relu2_srt_kernel(tc, qT, k_words, k_scales, vT, nb, us, off
         early_ms = keep.tile([P, 2], F32, name="early_ms")
         for b in range(2):
             product(b, 0, EARLY, early_sq)
-        nc.gpsimd.tensor_scalar(early_ms[:], early_sq[:], 1.0 / DV, EPS, ALU.mult, ALU.add)
-        copy_out(3, values(3))
-        y1 = signed(1, m1)
+            nc.gpsimd.tensor_scalar(early_ms[:, b:b + 1], early_sq[:, b:b + 1], 1.0 / DV, EPS, ALU.mult, ALU.add)
         quantise_values(1)
         quantise_weights(1, y1)
 

@@ -25,7 +25,7 @@ PASSES = D // (P * PACK)
 E_BLOCKS = DV // P
 Q_BLOCKS = NQ // P
 HALF = NQ // 2
-Q_ON_VECTOR = (0, 192)
+Q_ON_VECTOR = (128, 256)
 TINY = 2.0 ** -100
 
 
@@ -47,7 +47,7 @@ def tile_attend_mlpb_relu2_srt_kernel(tc, qT, k_words, k_scales, vT, nb, us, off
         def placed(shape, dtype, name, offset):
             return turns.tile(shape, dtype, name=name, offset=offset, align_bytes=64)
 
-        us_sb = placed([P, PACK], F32, "us_sb", 0)
+        us_sb = keep.tile([P, PACK], F32, name="us_sb")
         nc.sync.dma_start(us_sb[:], us[0].rearrange("(p j) o -> p (j o)", j=PACK))
         offsets = keep.tile([P, N // 16], U16, name="offsets")
         nc.sync.dma_start(offsets[:], offs)
@@ -59,8 +59,7 @@ def tile_attend_mlpb_relu2_srt_kernel(tc, qT, k_words, k_scales, vT, nb, us, off
         make_identity(nc, ident[:])
         k_sc = [keep.tile([P, 2, 2, P], U8, name="k_sc%d" % g, align_bytes=64) for g in range(PASSES)]
         nc.vector.memset(ks_win[:].bitcast(I32), 0)
-        nc.vector.memset(nb_win[:, :T // 2], 0.0)
-        nc.gpsimd.memset(nb_win[:, T // 2:], 0.0)
+        nc.vector.memset(nb_win[:], 0.0)
         nc.vector.memset(k_sc[1][:].rearrange("g u h m -> g (u h m)").bitcast(I32), 0)
 
         nc.sync.dma_start(kw_win[:], k_words[0].rearrange("p t b -> p (t b)").bitcast(I32))
@@ -68,31 +67,29 @@ def tile_attend_mlpb_relu2_srt_kernel(tc, qT, k_words, k_scales, vT, nb, us, off
             nc.sync.dma_start(ks_win[32 * quad:32 * quad + 8, :].bitcast(I32),
                               k_scales[:, 4 * quad:4 * quad + 4, :].bitcast(I32))
         NB_ROW = 8
+        q_raw = [placed([P, PACK, NQ], F32, "q_raw%d" % g, g * 4 * T) for g in range(PASSES)]
+        q_rows = qT[0].rearrange("(g p j) q -> g p j q", g=PASSES, j=PACK)
+        nc.sync.dma_start(q_raw[0][:], q_rows[0])
         nc.sync.dma_start(nb_win[NB_ROW:NB_ROW + 1, :], nb[0:1, :])
+        nc.sync.dma_start(q_raw[1][:], q_rows[1])
+        v_win = [keep.tile([P, T], F32, name="v_win0")]
+        nc.sync.dma_start(v_win[0][:], vT[0:P, :])
 
-        inv_root = placed([P, PACK], F32, "inv_root", 4 * T)
+        inv_root = keep.tile([P, PACK], F32, name="inv_root")
         mag = keep.tile([P, PACK], F32, name="mag")
         sgn = keep.tile([P, 2, 2], BF16, name="sgn")
         nc.scalar.activation(inv_root[:], us_sb[:], ACT.Abs_reciprocal_sqrt, bias=TINY)
         nc.scalar.activation(mag[:], us_sb[:], ACT.Abs)
         nc.scalar.activation(sgn[:], us_sb[:].rearrange("p (h u) -> p u h", u=2), ACT.Sign)
         rough = keep.tile([P, PACK], F32, name="rough")
-        gap = shared([P, PACK], F32, "gap", "a")
         miss = keep.tile([P, PACK], F32, name="miss")
         root = keep.tile([P, PACK], F32, name="root")
         nc.gpsimd.tensor_tensor(rough[:], mag[:], inv_root[:], ALU.mult)
         nc.gpsimd.tensor_tensor(miss[:], rough[:], rough[:], ALU.mult)
-        nc.gpsimd.tensor_tensor(gap[:], mag[:], miss[:], ALU.subtract)
-        nc.gpsimd.tensor_tensor(miss[:], gap[:], inv_root[:], ALU.mult)
+        nc.gpsimd.tensor_tensor(miss[:], mag[:], miss[:], ALU.subtract)
+        nc.gpsimd.tensor_tensor(miss[:], miss[:], inv_root[:], ALU.mult)
         nc.gpsimd.tensor_scalar(miss[:], miss[:], 0.5, 0.0, ALU.mult, ALU.add)
         nc.gpsimd.tensor_tensor(root[:], rough[:], miss[:], ALU.add)
-
-        q_raw = [placed([P, PACK, NQ], F32, "q_raw%d" % g, g * 4 * T) for g in range(PASSES)]
-        for g in range(PASSES):
-            nc.sync.dma_start(q_raw[g][:], qT[0, g * 512:(g + 1) * 512, :].rearrange("(p j) q -> p j q", j=PACK))
-
-        v_win = [shared([P, T], F32, "v_win0", "a")]
-        nc.sync.dma_start(v_win[0][:], vT[0:P, :])
 
         kw_g = keep.tile([P, 2, 2, P], U32, name="kw_g")
         nc.vector.tensor_copy(kw_g[:].rearrange("g u h m -> g m h u"), kw_win[:].bitcast(U32).indirect(offsets[:]))
@@ -122,9 +119,8 @@ def tile_attend_mlpb_relu2_srt_kernel(tc, qT, k_words, k_scales, vT, nb, us, off
             cut = Q_ON_VECTOR[g]
             dst, src = interleaved(q_bf[:, cut:, :], q_raw[g][:, :, cut:])
             nc.scalar.copy(dst, src)
-            if cut:
-                dst, src = interleaved(q_bf[:, :cut, :], q_raw[g][:, :, :cut])
-                nc.vector.tensor_copy(dst, src)
+            dst, src = interleaved(q_bf[:, :cut, :], q_raw[g][:, :, :cut])
+            nc.vector.tensor_copy(dst, src)
             q_codes.append(shared([P, NQ], U32, "q_codes%d" % g, ("d", "q_codes1")[g]))
             nc.vector.quantize_mx(out=q_codes[g][:].bitcast(FP8X4), scales=q_sc[:, g, :],
                                   in_=q_bf[:].rearrange("p q t -> p (q t)"))
@@ -154,7 +150,7 @@ def tile_attend_mlpb_relu2_srt_kernel(tc, qT, k_words, k_scales, vT, nb, us, off
         y_sc = keep.tile([P, NQ], U8, name="y_sc", align_bytes=64)
 
         def values(e):
-            v_g = shared([P, 2, P, 2], BF16, "v_g%d" % e, "g%d" % e)
+            v_g = keep.tile([P, 2, P, 2], BF16, name="v_g%d" % e)
             nc.vector.tensor_copy(v_g[:].rearrange("e u p h -> e p h u"), v_win[e][:].indirect(offsets[:]))
             v_ps = psum.tile([P, 2, P], F32, name="v_ps%d" % e, tag=("acc0", "acc1", "turn2", "turn3")[e])
             for u in range(2):
@@ -162,7 +158,7 @@ def tile_attend_mlpb_relu2_srt_kernel(tc, qT, k_words, k_scales, vT, nb, us, off
             return v_ps
 
         def copy_out(e, v_ps):
-            copy = nc.vector.tensor_copy if e == 0 else nc.scalar.copy
+            copy = nc.vector.tensor_copy if e < 2 else nc.scalar.copy
             copy(v_bf[e // 2][:, e % 2, :].bitcast(F32).rearrange("p (e u) -> p e u", u=2),
                  v_ps[:].rearrange("p u e -> p e u"))
 
@@ -172,7 +168,7 @@ def tile_attend_mlpb_relu2_srt_kernel(tc, qT, k_words, k_scales, vT, nb, us, off
                                   in_=v_bf[i][:].rearrange("p e c -> p (e c)"))
 
         def square(h):
-            y_mag = shared([P, HALF, PACK], BF16, "y_mag%d" % h, ("m", "g1")[h])
+            y_mag = keep.tile([P, HALF, PACK], BF16, name="y_mag%d" % h)
             dst, src = interleaved(y_mag[:], relu[:, :, h * HALF:(h + 1) * HALF])
             nc.scalar.activation(dst, src, ACT.Square)
             return y_mag
@@ -227,5 +223,8 @@ def tile_attend_mlpb_relu2_srt_kernel(tc, qT, k_words, k_scales, vT, nb, us, off
             nc.scalar.activation(rstd[:, b:b + 1], late_sq[:, b:b + 1], ACT.Abs_reciprocal_sqrt,
                                  bias=early_ms[:, b:b + 1] if b < 2 else EPS, scale=1.0 / DV)
             res = keep.tile([P, DV], F32, name="res%d" % b)
-            nc.vector.tensor_scalar(res[:], sums[b][:], rstd[:, b:b + 1], None, ALU.mult)
-            nc.sync.dma_start(out[0, b * P:(b + 1) * P, :], res[:])
+            pieces = 2 if b == Q_BLOCKS - 1 else 1
+            for i in range(pieces):
+                cols = slice(i * DV // pieces, (i + 1) * DV // pieces)
+                nc.vector.tensor_scalar(res[:, cols], sums[b][:, cols], rstd[:, b:b + 1], None, ALU.mult)
+                nc.sync.dma_start(out[0, b * P:(b + 1) * P, cols], res[:, cols])

@@ -22,15 +22,20 @@ ALU = mybir.AluOpType
 P = 128
 PACK = 4
 PASSES = D // (P * PACK)
+QUADRANTS = 4
 E_BLOCKS = DV // P
 Q_BLOCKS = NQ // P
-HALF = NQ // 2
-Q_ON_VECTOR = (128, 256)
+Q_HALF = NQ // 2
+E_HALF = DV // 2
+WINDOW_BYTES = 4 * T
+Q_ON_VECTOR = (192, 320)
+NB_ROW = 8
 TINY = 2.0 ** -100
+SLOT_OF = [2 * (t % 2) + t // 2 for t in range(PACK)]
 
 
 def interleaved(dst, src):
-    return (dst.rearrange("p (c i) t -> p c t i", i=4), src.rearrange("p t (c i) -> p c t i", i=4))
+    return dst.rearrange("p (c i) t -> p c t i", i=4), src.rearrange("p t (c i) -> p c t i", i=4)
 
 
 def tile_attend_mlpb_relu2_srt_kernel(tc, qT, k_words, k_scales, vT, nb, us, offs, out):
@@ -41,33 +46,32 @@ def tile_attend_mlpb_relu2_srt_kernel(tc, qT, k_words, k_scales, vT, nb, us, off
         turns = ctx.enter_context(tc.tile_pool(name="turns", bufs=1))
         psum = ctx.enter_context(tc.psum_pool(name="psum", bufs=1))
 
-        def shared(shape, dtype, name, slot):
-            return stage.tile(shape, dtype, name=name, tag=slot, align_bytes=64)
+        def shared(shape, dtype, name, tag):
+            return stage.tile(shape, dtype, name=name, tag=tag, align_bytes=64)
 
         def placed(shape, dtype, name, offset):
             return turns.tile(shape, dtype, name=name, offset=offset, align_bytes=64)
 
-        us_sb = keep.tile([P, PACK], F32, name="us_sb")
-        nc.sync.dma_start(us_sb[:], us[0].rearrange("(p j) o -> p (j o)", j=PACK))
         offsets = keep.tile([P, N // 16], U16, name="offsets")
         nc.sync.dma_start(offsets[:], offs)
 
         kw_win = keep.tile([P, T], I32, name="kw_win")
         ks_win = keep.tile([P, T], U8, name="ks_win")
-        nb_win = shared([P, T], F32, "nb_win", "d")
+        nb_win = shared([P, T], F32, "nb_win", "nb_then_codes")
         ident = keep.tile([P, P], F32, name="ident")
         make_identity(nc, ident[:])
         k_sc = [keep.tile([P, 2, 2, P], U8, name="k_sc%d" % g, align_bytes=64) for g in range(PASSES)]
         nc.vector.memset(ks_win[:].bitcast(I32), 0)
         nc.vector.memset(nb_win[:], 0.0)
-        nc.vector.memset(k_sc[1][:].rearrange("g u h m -> g (u h m)").bitcast(I32), 0)
+        nc.vector.memset(k_sc[1][:].rearrange("p u h m -> p (u h m)").bitcast(I32), 0)
 
         nc.sync.dma_start(kw_win[:], k_words[0].rearrange("p t b -> p (t b)").bitcast(I32))
-        for quad in range(4):
+        us_sb = keep.tile([P, PACK], F32, name="us_sb")
+        nc.sync.dma_start(us_sb[:], us[0].rearrange("(p j) o -> p (j o)", j=PACK))
+        for quad in range(QUADRANTS):
             nc.sync.dma_start(ks_win[32 * quad:32 * quad + 8, :].bitcast(I32),
                               k_scales[:, 4 * quad:4 * quad + 4, :].bitcast(I32))
-        NB_ROW = 8
-        q_raw = [placed([P, PACK, NQ], F32, "q_raw%d" % g, g * 4 * T) for g in range(PASSES)]
+        q_raw = [placed([P, PACK, NQ], F32, "q_raw%d" % g, g * WINDOW_BYTES) for g in range(PASSES)]
         q_rows = qT[0].rearrange("(g p j) q -> g p j q", g=PASSES, j=PACK)
         nc.sync.dma_start(q_raw[0][:], q_rows[0])
         nc.sync.dma_start(nb_win[NB_ROW:NB_ROW + 1, :], nb[0:1, :])
@@ -82,35 +86,34 @@ def tile_attend_mlpb_relu2_srt_kernel(tc, qT, k_words, k_scales, vT, nb, us, off
         nc.scalar.activation(mag[:], us_sb[:], ACT.Abs)
         nc.scalar.activation(sgn[:], us_sb[:].rearrange("p (h u) -> p u h", u=2), ACT.Sign)
         rough = keep.tile([P, PACK], F32, name="rough")
-        miss = keep.tile([P, PACK], F32, name="miss")
+        step = keep.tile([P, PACK], F32, name="step")
         root = keep.tile([P, PACK], F32, name="root")
         nc.gpsimd.tensor_tensor(rough[:], mag[:], inv_root[:], ALU.mult)
-        nc.gpsimd.tensor_tensor(miss[:], rough[:], rough[:], ALU.mult)
-        nc.gpsimd.tensor_tensor(miss[:], mag[:], miss[:], ALU.subtract)
-        nc.gpsimd.tensor_tensor(miss[:], miss[:], inv_root[:], ALU.mult)
-        nc.gpsimd.tensor_scalar(miss[:], miss[:], 0.5, 0.0, ALU.mult, ALU.add)
-        nc.gpsimd.tensor_tensor(root[:], rough[:], miss[:], ALU.add)
+        nc.gpsimd.tensor_tensor(step[:], rough[:], rough[:], ALU.mult)
+        nc.gpsimd.tensor_tensor(step[:], mag[:], step[:], ALU.subtract)
+        nc.gpsimd.tensor_tensor(step[:], step[:], inv_root[:], ALU.mult)
+        nc.gpsimd.tensor_scalar(step[:], step[:], 0.5, 0.0, ALU.mult, ALU.add)
+        nc.gpsimd.tensor_tensor(root[:], rough[:], step[:], ALU.add)
 
         kw_g = keep.tile([P, 2, 2, P], U32, name="kw_g")
-        nc.vector.tensor_copy(kw_g[:].rearrange("g u h m -> g m h u"), kw_win[:].bitcast(U32).indirect(offsets[:]))
-        ks_g = shared([P, N], U8, "ks_g", "b")
+        nc.vector.tensor_copy(kw_g[:].rearrange("p u h m -> p m h u"), kw_win[:].bitcast(U32).indirect(offsets[:]))
+        ks_g = shared([P, N], U8, "ks_g", "scales_then_values")
         nc.vector.tensor_copy(ks_g[:], ks_win[:].indirect(offsets[:]))
         k_codes = keep.tile([P, PASSES, N], U16, name="k_codes", align_bytes=64)
         nc.vector.tensor_copy(k_codes[:],
-                              kw_g[:].rearrange("g u h m -> g (u h m)").bitcast(U16).rearrange("g (c o) -> g o c", o=2))
-        nc.vector.tensor_copy(k_sc[0][:].rearrange("g u h m -> g m h u"),
-                              ks_g[:].rearrange("g (m h u) -> g m h u", h=2, u=2))
-        for quad in range(4):
-            rows = 32 * quad
-            nc.sync.dma_start(k_sc[1][rows:rows + 4].rearrange("g u h m -> g (u h m)").bitcast(I32),
-                              k_sc[0][rows + 4:rows + 8].rearrange("g u h m -> g (u h m)").bitcast(I32))
+                              kw_g[:].rearrange("p u h m -> p (u h m)").bitcast(U16).rearrange("p (c g) -> p g c", g=2))
+        nc.vector.tensor_copy(k_sc[0][:].rearrange("p u h m -> p m h u"),
+                              ks_g[:].rearrange("p (m h u) -> p m h u", h=2, u=2))
+        for quad in range(QUADRANTS):
+            row = 32 * quad
+            nc.sync.dma_start(k_sc[1][row:row + 4].rearrange("p u h m -> p (u h m)").bitcast(I32),
+                              k_sc[0][row + 4:row + 8].rearrange("p u h m -> p (u h m)").bitcast(I32))
 
-        slot_of = [2 * (t % 2) + t // 2 for t in range(PACK)]
         nb_g = keep.tile([P, N], F32, name="nb_g")
         nc.vector.tensor_copy(nb_g[:], nb_win[:].indirect(offsets[:]))
         nb_ps = [psum.tile([P, 2, P], F32, name="nb_ps%d" % u, tag="acc%d" % (2 + u)) for u in range(2)]
         for t in range(PACK):
-            nc.tensor.transpose(nb_ps[t // 2][:, t % 2, :], nb_g[:, slot_of[t]:N:PACK], ident[:])
+            nc.tensor.transpose(nb_ps[t // 2][:, t % 2, :], nb_g[:, SLOT_OF[t]:N:PACK], ident[:])
 
         q_sc = keep.tile([P, PASSES, NQ], U8, name="q_sc", align_bytes=64)
         q_codes = []
@@ -121,7 +124,7 @@ def tile_attend_mlpb_relu2_srt_kernel(tc, qT, k_words, k_scales, vT, nb, us, off
             nc.scalar.copy(dst, src)
             dst, src = interleaved(q_bf[:, :cut, :], q_raw[g][:, :, :cut])
             nc.vector.tensor_copy(dst, src)
-            q_codes.append(shared([P, NQ], U32, "q_codes%d" % g, ("d", "q_codes1")[g]))
+            q_codes.append(shared([P, NQ], U32, "q_codes%d" % g, ("nb_then_codes", "q_codes1")[g]))
             nc.vector.quantize_mx(out=q_codes[g][:].bitcast(FP8X4), scales=q_sc[:, g, :],
                                   in_=q_bf[:].rearrange("p q t -> p (q t)"))
         bias = shared([P, 2, 2], F32, "bias", "q_bf1")
@@ -131,30 +134,31 @@ def tile_attend_mlpb_relu2_srt_kernel(tc, qT, k_words, k_scales, vT, nb, us, off
         scores = [psum.tile([P, NQ], F32, name="score%d" % t, tag="acc%d" % t) for t in range(PACK)]
         relu = keep.tile([P, PACK, NQ], F32, name="relu")
         for t in range(PACK):
+            u, h = divmod(t, 2)
             for g in range(PASSES):
                 nc.tensor.matmul_mx(out=scores[t][:],
                                     lhsT=k_codes[:, g, t * P:(t + 1) * P].bitcast(FP4X4),
-                                    lhsT_scale=k_sc[g][:, t // 2, t % 2, :],
+                                    lhsT_scale=k_sc[g][:, u, h, :],
                                     rhs=q_codes[g][:].bitcast(FP8X4), rhs_scale=q_sc[:, g, :],
                                     start=(g == 0), stop=(g == PASSES - 1))
-            j = slot_of[t]
             nc.scalar.activation(relu[:, t, :], scores[t][:], ACT.Relu,
-                                 bias=bias[:, t // 2, t % 2:t % 2 + 1], scale=root[:, j:j + 1])
+                                 bias=bias[:, u, h:h + 1], scale=root[:, SLOT_OF[t]:SLOT_OF[t] + 1])
 
+        v_win.append(shared([P, T], F32, "v_win1", "scales_then_values"))
+        v_win.append(placed([P, T], F32, "v_win2", 0))
+        v_win.append(placed([P, T], F32, "v_win3", WINDOW_BYTES))
         for e in range(1, E_BLOCKS):
-            w = shared([P, T], F32, "v_win1", "b") if e == 1 else placed([P, T], F32, "v_win%d" % e, (e - 2) * 4 * T)
-            nc.sync.dma_start(w[:], vT[e * P:(e + 1) * P, :])
-            v_win.append(w)
-        v_bf = [shared([P, 2, P * PACK], BF16, "v_bf%d" % i, ("b", "v_bf1")[i]) for i in range(2)]
+            nc.sync.dma_start(v_win[e][:], vT[e * P:(e + 1) * P, :])
+        v_bf = [shared([P, 2, P * PACK], BF16, "v_bf%d" % i, ("scales_then_values", "v_bf1")[i]) for i in range(2)]
         v_sc = keep.tile([P, DV], U8, name="v_sc", align_bytes=64)
         y_sc = keep.tile([P, NQ], U8, name="y_sc", align_bytes=64)
 
-        def values(e):
+        def gather_and_turn(e):
             v_g = keep.tile([P, 2, P, 2], BF16, name="v_g%d" % e)
-            nc.vector.tensor_copy(v_g[:].rearrange("e u p h -> e p h u"), v_win[e][:].indirect(offsets[:]))
+            nc.vector.tensor_copy(v_g[:].rearrange("e u m h -> e m h u"), v_win[e][:].indirect(offsets[:]))
             v_ps = psum.tile([P, 2, P], F32, name="v_ps%d" % e, tag=("acc0", "acc1", "turn2", "turn3")[e])
             for u in range(2):
-                nc.tensor.transpose(v_ps[:, u, :], v_g[:, u, :, :].rearrange("e p h -> e (p h)").bitcast(F32), ident[:])
+                nc.tensor.transpose(v_ps[:, u, :], v_g[:, u, :, :].rearrange("e m h -> e (m h)").bitcast(F32), ident[:])
             return v_ps
 
         def copy_out(e, v_ps):
@@ -163,40 +167,41 @@ def tile_attend_mlpb_relu2_srt_kernel(tc, qT, k_words, k_scales, vT, nb, us, off
                  v_ps[:].rearrange("p u e -> p e u"))
 
         def quantise_values(i):
-            cols = slice(i * 2 * P, (i + 1) * 2 * P)
+            cols = slice(i * E_HALF, (i + 1) * E_HALF)
             nc.vector.quantize_mx(out=v_codes[:, cols].bitcast(FP8X4), scales=v_sc[:, cols],
                                   in_=v_bf[i][:].rearrange("p e c -> p (e c)"))
 
-        def square(h):
-            y_mag = keep.tile([P, HALF, PACK], BF16, name="y_mag%d" % h)
-            dst, src = interleaved(y_mag[:], relu[:, :, h * HALF:(h + 1) * HALF])
+        def square(i):
+            y_mag = keep.tile([P, Q_HALF, PACK], BF16, name="y_mag%d" % i)
+            dst, src = interleaved(y_mag[:], relu[:, :, i * Q_HALF:(i + 1) * Q_HALF])
             nc.scalar.activation(dst, src, ACT.Square)
             return y_mag
 
-        def signed(h, y_mag):
-            y_bf = placed([P, HALF, PACK], BF16, "y_bf%d" % h, h * 4 * T)
-            nc.vector.tensor_tensor(y_bf[:], y_mag[:],
-                                    sgn[:].rearrange("p u h -> p (u h)").unsqueeze(1).to_broadcast([P, HALF, PACK]), ALU.mult)
+        def signed(i, y_mag):
+            y_bf = placed([P, Q_HALF, PACK], BF16, "y_bf%d" % i, i * WINDOW_BYTES)
+            signs = sgn[:].rearrange("p u h -> p (u h)").unsqueeze(1).to_broadcast([P, Q_HALF, PACK])
+            nc.vector.tensor_tensor(y_bf[:], y_mag[:], signs, ALU.mult)
             return y_bf
 
-        def quantise_weights(h, y_bf):
-            cols = slice(h * HALF, (h + 1) * HALF)
+        def quantise_y(i, y_bf):
+            cols = slice(i * Q_HALF, (i + 1) * Q_HALF)
             nc.vector.quantize_mx(out=y_codes[:, cols].bitcast(FP8X4), scales=y_sc[:, cols],
                                   in_=y_bf[:].rearrange("p q t -> p (q t)"))
 
-        m0 = square(0)
-        turned = [values(0), values(1)]
+        y_bf_bytes = 2 * Q_HALF * PACK
+        y_mag0 = square(0)
+        turned = [gather_and_turn(0), gather_and_turn(1)]
         copy_out(0, turned[0])
         copy_out(1, turned[1])
-        m1 = square(1)
-        copy_out(2, values(2))
-        y0 = signed(0, m0)
-        v_codes = placed([P, DV], U32, "v_codes", T)
+        y_mag1 = square(1)
+        copy_out(2, gather_and_turn(2))
+        y_bf0 = signed(0, y_mag0)
+        v_codes = placed([P, DV], U32, "v_codes", y_bf_bytes)
         quantise_values(0)
-        copy_out(3, values(3))
-        y_codes = placed([P, NQ], U32, "y_codes", 4 * T + T)
-        quantise_weights(0, y0)
-        y1 = signed(1, m1)
+        copy_out(3, gather_and_turn(3))
+        y_codes = placed([P, NQ], U32, "y_codes", WINDOW_BYTES + y_bf_bytes)
+        quantise_y(0, y_bf0)
+        y_bf1 = signed(1, y_mag1)
 
         sums = [psum.tile([P, DV], F32, name="sum%d" % b, tag="acc%d" % b) for b in range(Q_BLOCKS)]
         squares = keep.tile([P, DV], BF16, name="squares")
@@ -207,21 +212,22 @@ def tile_attend_mlpb_relu2_srt_kernel(tc, qT, k_words, k_scales, vT, nb, us, off
                                 rhs=v_codes[:, lo:hi].bitcast(FP8X4), rhs_scale=v_sc[:, lo:hi], start=True, stop=True)
             nc.scalar.activation(squares[:, lo:hi], sums[b][:, lo:hi], ACT.Square, accum_out=sum_sq[:, b:b + 1])
 
-        EARLY = 2 * P
-        early_sq = keep.tile([P, 2], F32, name="early_sq")
-        early_ms = keep.tile([P, 2], F32, name="early_ms")
-        for b in range(2):
-            product(b, 0, EARLY, early_sq)
+        early_blocks = Q_HALF // P
+        early_sq = keep.tile([P, early_blocks], F32, name="early_sq")
+        early_ms = keep.tile([P, early_blocks], F32, name="early_ms")
+        for b in range(early_blocks):
+            product(b, 0, E_HALF, early_sq)
             nc.gpsimd.tensor_scalar(early_ms[:, b:b + 1], early_sq[:, b:b + 1], 1.0 / DV, EPS, ALU.mult, ALU.add)
         quantise_values(1)
-        quantise_weights(1, y1)
+        quantise_y(1, y_bf1)
 
         late_sq = keep.tile([P, Q_BLOCKS], F32, name="late_sq")
         rstd = keep.tile([P, Q_BLOCKS], F32, name="rstd")
         for b in range(Q_BLOCKS):
-            product(b, EARLY if b < 2 else 0, DV, late_sq)
+            early = b < early_blocks
+            product(b, E_HALF if early else 0, DV, late_sq)
             nc.scalar.activation(rstd[:, b:b + 1], late_sq[:, b:b + 1], ACT.Abs_reciprocal_sqrt,
-                                 bias=early_ms[:, b:b + 1] if b < 2 else EPS, scale=1.0 / DV)
+                                 bias=early_ms[:, b:b + 1] if early else EPS, scale=1.0 / DV)
             res = keep.tile([P, DV], F32, name="res%d" % b)
             pieces = 2 if b == Q_BLOCKS - 1 else 1
             for i in range(pieces):

@@ -28,10 +28,10 @@ Q_BLOCKS = NQ // P
 Q_HALF = NQ // 2
 E_HALF = DV // 2
 WINDOW_BYTES = 4 * T
-Q_ON_VECTOR = (192, 320)
-NB_ROW = 8
+Q_ON_VECTOR = (224, 256)
+NB_ROW = P - 1
+KS_ROW = 96
 TINY = 2.0 ** -100
-SLOT_OF = [2 * (t % 2) + t // 2 for t in range(PACK)]
 
 
 def interleaved(dst, src):
@@ -42,49 +42,55 @@ def tile_attend_mlpb_relu2_srt_kernel(tc, qT, k_words, k_scales, vT, nb, us, off
     nc = tc.nc
     with ExitStack() as ctx:
         keep = ctx.enter_context(tc.tile_pool(name="keep", bufs=1))
-        stage = ctx.enter_context(tc.tile_pool(name="stage", bufs=1))
         turns = ctx.enter_context(tc.tile_pool(name="turns", bufs=1))
         psum = ctx.enter_context(tc.psum_pool(name="psum", bufs=1))
-
-        def shared(shape, dtype, name, tag):
-            return stage.tile(shape, dtype, name=name, tag=tag, align_bytes=64)
 
         def placed(shape, dtype, name, offset):
             return turns.tile(shape, dtype, name=name, offset=offset, align_bytes=64)
 
         offsets = keep.tile([P, N // 16], U16, name="offsets")
         nc.sync.dma_start(offsets[:], offs)
-
-        kw_win = keep.tile([P, T], I32, name="kw_win")
         ks_win = keep.tile([P, T], U8, name="ks_win")
-        nb_win = shared([P, T], F32, "nb_win", "nb_then_codes")
-        ident = keep.tile([P, P], F32, name="ident")
-        make_identity(nc, ident[:])
-        k_sc = [keep.tile([P, 2, 2, P], U8, name="k_sc%d" % g, align_bytes=64) for g in range(PASSES)]
-        nc.vector.memset(ks_win[:].bitcast(I32), 0)
-        nc.vector.memset(nb_win[:], 0.0)
-        nc.vector.memset(k_sc[1][:].rearrange("p u h m -> p (u h m)").bitcast(I32), 0)
-
-        nc.sync.dma_start(kw_win[:], k_words[0].rearrange("p t b -> p (t b)").bitcast(I32))
+        nb_win = keep.tile([P, T], F32, name="nb_win")
         us_sb = keep.tile([P, PACK], F32, name="us_sb")
+        nc.sync.dma_start(ks_win[KS_ROW:P, :].bitcast(I32), k_scales.rearrange("g f t -> f g t").bitcast(I32))
+        nc.sync.dma_start(nb_win[NB_ROW:P, :], nb[0:1, :])
         nc.sync.dma_start(us_sb[:], us[0].rearrange("(p j) o -> p (j o)", j=PACK))
-        for quad in range(QUADRANTS):
-            nc.sync.dma_start(ks_win[32 * quad:32 * quad + 8, :].bitcast(I32),
-                              k_scales[:, 4 * quad:4 * quad + 4, :].bitcast(I32))
-        q_raw = [placed([P, PACK, NQ], F32, "q_raw%d" % g, g * WINDOW_BYTES) for g in range(PASSES)]
+        q_raw = [keep.tile([P, PACK, NQ], F32, name="q_raw%d" % g) for g in range(PASSES)]
         q_rows = qT[0].rearrange("(g p j) q -> g p j q", g=PASSES, j=PACK)
         nc.sync.dma_start(q_raw[0][:], q_rows[0])
-        nc.sync.dma_start(nb_win[NB_ROW:NB_ROW + 1, :], nb[0:1, :])
+        kw_win = keep.tile([P, T], I32, name="kw_win")
+        nc.sync.dma_start(kw_win[:], k_words[0].rearrange("p t b -> p (t b)").bitcast(I32))
+
+        k_sc = keep.tile([P, PASSES, N], U8, name="k_sc", align_bytes=64)
+        nc.vector.memset(ks_win[0:KS_ROW, :].bitcast(I32), 0)
+        nc.gpsimd.memset(nb_win[0:NB_ROW, :].bitcast(I32), 0)
+        nc.vector.memset(k_sc[:].rearrange("p g c -> p (g c)").bitcast(I32), 0)
+        ident = keep.tile([P, P], F32, name="ident")
+        make_identity(nc, ident[:])
+
+        ks_g = keep.tile([P, N], U8, name="ks_g")
+        nc.vector.tensor_copy(ks_g[:], ks_win[:].indirect(offsets[:]))
+        ks_d = keep.tile([P, PACK, P], U8, name="ks_d")
+        nc.vector.tensor_copy(ks_d[:].rearrange("p t m -> p m t"), ks_g[:].rearrange("p (m t) -> p m t", t=PACK))
+        for quad in range(QUADRANTS):
+            row = KS_ROW + 8 * quad
+            nc.sync.dma_start(k_sc[32 * quad:32 * quad + 4].rearrange("p g c -> p (g c)").bitcast(I32),
+                              ks_d[row:row + 8].rearrange("p t m -> p (t m)").bitcast(I32))
+
         nc.sync.dma_start(q_raw[1][:], q_rows[1])
         v_win = [keep.tile([P, T], F32, name="v_win0")]
-        nc.sync.dma_start(v_win[0][:], vT[0:P, :])
+        for e in range(1, E_BLOCKS):
+            v_win.append(placed([P, T], F32, "v_win%d" % e, (e - 1) * WINDOW_BYTES))
+        for e in range(E_BLOCKS):
+            nc.sync.dma_start(v_win[e][:], vT[e * P:(e + 1) * P, :])
 
         inv_root = keep.tile([P, PACK], F32, name="inv_root")
         mag = keep.tile([P, PACK], F32, name="mag")
-        sgn = keep.tile([P, 2, 2], BF16, name="sgn")
+        sgn = keep.tile([P, PACK], BF16, name="sgn")
         nc.scalar.activation(inv_root[:], us_sb[:], ACT.Abs_reciprocal_sqrt, bias=TINY)
         nc.scalar.activation(mag[:], us_sb[:], ACT.Abs)
-        nc.scalar.activation(sgn[:], us_sb[:].rearrange("p (h u) -> p u h", u=2), ACT.Sign)
+        nc.scalar.activation(sgn[:], us_sb[:], ACT.Sign)
         rough = keep.tile([P, PACK], F32, name="rough")
         step = keep.tile([P, PACK], F32, name="step")
         root = keep.tile([P, PACK], F32, name="root")
@@ -95,141 +101,146 @@ def tile_attend_mlpb_relu2_srt_kernel(tc, qT, k_words, k_scales, vT, nb, us, off
         nc.gpsimd.tensor_scalar(step[:], step[:], 0.5, 0.0, ALU.mult, ALU.add)
         nc.gpsimd.tensor_tensor(root[:], rough[:], step[:], ALU.add)
 
-        kw_g = keep.tile([P, 2, 2, P], U32, name="kw_g")
-        nc.vector.tensor_copy(kw_g[:].rearrange("p u h m -> p m h u"), kw_win[:].bitcast(U32).indirect(offsets[:]))
-        ks_g = shared([P, N], U8, "ks_g", "scales_then_values")
-        nc.vector.tensor_copy(ks_g[:], ks_win[:].indirect(offsets[:]))
-        k_codes = keep.tile([P, PASSES, N], U16, name="k_codes", align_bytes=64)
-        nc.vector.tensor_copy(k_codes[:],
-                              kw_g[:].rearrange("p u h m -> p (u h m)").bitcast(U16).rearrange("p (c g) -> p g c", g=2))
-        nc.vector.tensor_copy(k_sc[0][:].rearrange("p u h m -> p m h u"),
-                              ks_g[:].rearrange("p (m h u) -> p m h u", h=2, u=2))
-        for quad in range(QUADRANTS):
-            row = 32 * quad
-            nc.sync.dma_start(k_sc[1][row:row + 4].rearrange("p u h m -> p (u h m)").bitcast(I32),
-                              k_sc[0][row + 4:row + 8].rearrange("p u h m -> p (u h m)").bitcast(I32))
-
         nb_g = keep.tile([P, N], F32, name="nb_g")
         nc.vector.tensor_copy(nb_g[:], nb_win[:].indirect(offsets[:]))
-        nb_ps = [psum.tile([P, 2, P], F32, name="nb_ps%d" % u, tag="acc%d" % (2 + u)) for u in range(2)]
+        nb_ps = psum.tile([P, PACK, P], F32, name="nb_ps", tag="turn3")
         for t in range(PACK):
-            nc.tensor.transpose(nb_ps[t // 2][:, t % 2, :], nb_g[:, SLOT_OF[t]:N:PACK], ident[:])
+            nc.tensor.transpose(nb_ps[:, t, :], nb_g[:, t:N:PACK], ident[:])
+        bias = keep.tile([P, PACK], F32, name="bias")
+        for t in range(PACK):
+            nc.scalar.activation(bias[:, t:t + 1], nb_ps[:, t, NB_ROW:P], ACT.Copy, scale=root[:, t:t + 1])
 
         q_sc = keep.tile([P, PASSES, NQ], U8, name="q_sc", align_bytes=64)
-        q_codes = []
-        for g in range(PASSES):
-            q_bf = shared([P, NQ, PACK], BF16, "q_bf%d" % g, "q_bf%d" % g)
+
+        def cast_queries(g):
+            q_bf = keep.tile([P, NQ, PACK], BF16, name="q_bf%d" % g, align_bytes=64)
             cut = Q_ON_VECTOR[g]
             dst, src = interleaved(q_bf[:, cut:, :], q_raw[g][:, :, cut:])
             nc.scalar.copy(dst, src)
-            dst, src = interleaved(q_bf[:, :cut, :], q_raw[g][:, :, :cut])
-            nc.vector.tensor_copy(dst, src)
-            q_codes.append(shared([P, NQ], U32, "q_codes%d" % g, ("nb_then_codes", "q_codes1")[g]))
-            nc.vector.quantize_mx(out=q_codes[g][:].bitcast(FP8X4), scales=q_sc[:, g, :],
+            if cut:
+                dst, src = interleaved(q_bf[:, :cut, :], q_raw[g][:, :, :cut])
+                nc.vector.tensor_copy(dst, src)
+            return q_bf
+
+        def quantise_queries(g, q_bf, codes):
+            nc.vector.quantize_mx(out=codes[:].bitcast(FP8X4), scales=q_sc[:, g, :],
                                   in_=q_bf[:].rearrange("p q t -> p (q t)"))
-        bias = shared([P, 2, 2], F32, "bias", "q_bf1")
-        for u in range(2):
-            nc.vector.tensor_tensor(bias[:, u, :], nb_ps[u][:, :, NB_ROW], root[:, u:PACK:2], ALU.mult)
+
+        q_codes = [keep.tile([P, NQ], U32, name="q_codes%d" % g, align_bytes=64) for g in range(PASSES)]
+        quantise_queries(0, cast_queries(0), q_codes[0])
+
+        kw_g = keep.tile([P, PACK, P], U32, name="kw_g")
+        nc.vector.tensor_copy(kw_g[:].rearrange("p t m -> p m t"), kw_win[:].bitcast(U32).indirect(offsets[:]))
+        k_codes = [keep.tile([P, N], U16, name="k_codes%d" % g, align_bytes=64) for g in range(PASSES)]
+        halves = kw_g[:].rearrange("p t m -> p (t m)").bitcast(U16).rearrange("p (c g) -> p g c", g=2)
+        for g in range(PASSES):
+            nc.vector.tensor_copy(k_codes[g][:], halves[:, g, :])
+        quantise_queries(1, cast_queries(1), q_codes[1])
 
         scores = [psum.tile([P, NQ], F32, name="score%d" % t, tag="acc%d" % t) for t in range(PACK)]
-        relu = keep.tile([P, PACK, NQ], F32, name="relu")
-        for t in range(PACK):
-            u, h = divmod(t, 2)
-            for g in range(PASSES):
+        for g in range(PASSES):
+            for t in range(PACK):
                 nc.tensor.matmul_mx(out=scores[t][:],
-                                    lhsT=k_codes[:, g, t * P:(t + 1) * P].bitcast(FP4X4),
-                                    lhsT_scale=k_sc[g][:, u, h, :],
+                                    lhsT=k_codes[g][:, t * P:(t + 1) * P].bitcast(FP4X4),
+                                    lhsT_scale=k_sc[:, g, t * P:(t + 1) * P],
                                     rhs=q_codes[g][:].bitcast(FP8X4), rhs_scale=q_sc[:, g, :],
                                     start=(g == 0), stop=(g == PASSES - 1))
-            nc.scalar.activation(relu[:, t, :], scores[t][:], ACT.Relu,
-                                 bias=bias[:, u, h:h + 1], scale=root[:, SLOT_OF[t]:SLOT_OF[t] + 1])
 
-        v_win.append(shared([P, T], F32, "v_win1", "scales_then_values"))
-        v_win.append(placed([P, T], F32, "v_win2", 0))
-        v_win.append(placed([P, T], F32, "v_win3", WINDOW_BYTES))
-        for e in range(1, E_BLOCKS):
-            nc.sync.dma_start(v_win[e][:], vT[e * P:(e + 1) * P, :])
-        v_bf = [shared([P, 2, P * PACK], BF16, "v_bf%d" % i, ("scales_then_values", "v_bf1")[i]) for i in range(2)]
+        v_bf = [keep.tile([P, 2, P * PACK], BF16, name="v_bf%d" % i, tag="v_bf%d" % i, align_bytes=64) for i in range(2)]
         v_sc = keep.tile([P, DV], U8, name="v_sc", align_bytes=64)
         y_sc = keep.tile([P, NQ], U8, name="y_sc", align_bytes=64)
 
         def gather_and_turn(e):
-            v_g = keep.tile([P, 2, P, 2], BF16, name="v_g%d" % e)
-            nc.vector.tensor_copy(v_g[:].rearrange("e u m h -> e m h u"), v_win[e][:].indirect(offsets[:]))
-            v_ps = psum.tile([P, 2, P], F32, name="v_ps%d" % e, tag=("acc0", "acc1", "turn2", "turn3")[e])
+            v_g = keep.tile([P, N], BF16, name="v_g%d" % e)
+            nc.vector.tensor_copy(v_g[:], v_win[e][:].indirect(offsets[:]))
+            v_ps = psum.tile([P, 2, P], F32, name="v_ps%d" % e, tag="turn%d" % e)
             for u in range(2):
-                nc.tensor.transpose(v_ps[:, u, :], v_g[:, u, :, :].rearrange("e m h -> e (m h)").bitcast(F32), ident[:])
-            return v_ps
-
-        def copy_out(e, v_ps):
+                nc.tensor.transpose(v_ps[:, u, :], v_g[:].bitcast(F32)[:, u:N // 2:2], ident[:])
             copy = nc.vector.tensor_copy if e < 2 else nc.scalar.copy
             copy(v_bf[e // 2][:, e % 2, :].bitcast(F32).rearrange("p (e u) -> p e u", u=2),
                  v_ps[:].rearrange("p u e -> p e u"))
 
-        def quantise_values(i):
-            cols = slice(i * E_HALF, (i + 1) * E_HALF)
-            nc.vector.quantize_mx(out=v_codes[:, cols].bitcast(FP8X4), scales=v_sc[:, cols],
+        def quantise_values(i, codes):
+            nc.vector.quantize_mx(out=codes[:].bitcast(FP8X4), scales=v_sc[:, i * E_HALF:(i + 1) * E_HALF],
                                   in_=v_bf[i][:].rearrange("p e c -> p (e c)"))
 
         def square(i):
+            relu = keep.tile([P, PACK, Q_HALF], F32, name="relu%d" % i, tag="relu")
+            for t in range(PACK):
+                nc.scalar.activation(relu[:, t, :], scores[t][:, i * Q_HALF:(i + 1) * Q_HALF], ACT.Relu,
+                                     bias=bias[:, t:t + 1], scale=root[:, t:t + 1])
             y_mag = keep.tile([P, Q_HALF, PACK], BF16, name="y_mag%d" % i)
-            dst, src = interleaved(y_mag[:], relu[:, :, i * Q_HALF:(i + 1) * Q_HALF])
+            dst, src = interleaved(y_mag[:], relu[:])
             nc.scalar.activation(dst, src, ACT.Square)
             return y_mag
 
         def signed(i, y_mag):
-            y_bf = placed([P, Q_HALF, PACK], BF16, "y_bf%d" % i, i * WINDOW_BYTES)
-            signs = sgn[:].rearrange("p u h -> p (u h)").unsqueeze(1).to_broadcast([P, Q_HALF, PACK])
+            y_bf = placed([P, Q_HALF, PACK], BF16, "y_bf%d" % i, 2 * i * WINDOW_BYTES)
+            signs = sgn[:].unsqueeze(1).to_broadcast([P, Q_HALF, PACK])
             nc.vector.tensor_tensor(y_bf[:], y_mag[:], signs, ALU.mult)
             return y_bf
 
-        def quantise_y(i, y_bf):
-            cols = slice(i * Q_HALF, (i + 1) * Q_HALF)
-            nc.vector.quantize_mx(out=y_codes[:, cols].bitcast(FP8X4), scales=y_sc[:, cols],
+        def quantise_y(i, y_bf, codes):
+            nc.vector.quantize_mx(out=codes[:].bitcast(FP8X4), scales=y_sc[:, i * Q_HALF:(i + 1) * Q_HALF],
                                   in_=y_bf[:].rearrange("p q t -> p (q t)"))
 
-        y_bf_bytes = 2 * Q_HALF * PACK
-        y_mag0 = square(0)
-        turned = [gather_and_turn(0), gather_and_turn(1)]
-        copy_out(0, turned[0])
-        copy_out(1, turned[1])
-        y_mag1 = square(1)
-        copy_out(2, gather_and_turn(2))
-        y_bf0 = signed(0, y_mag0)
-        v_codes = placed([P, DV], U32, "v_codes", y_bf_bytes)
-        quantise_values(0)
-        copy_out(3, gather_and_turn(3))
-        y_codes = placed([P, NQ], U32, "y_codes", WINDOW_BYTES + y_bf_bytes)
-        quantise_y(0, y_bf0)
-        y_bf1 = signed(1, y_mag1)
+        y_mag = [square(0), square(1)]
+        gather_and_turn(0)
+        gather_and_turn(1)
+        y_bf0 = signed(0, y_mag[0])
+        gather_and_turn(2)
+        y_codes = [placed([P, Q_HALF], U32, "y_codes0", WINDOW_BYTES + 4 * E_HALF)]
+        quantise_y(0, y_bf0, y_codes[0])
+        v_codes = [placed([P, E_HALF], U32, "v_codes0", WINDOW_BYTES)]
+        quantise_values(0, v_codes[0])
 
         sums = [psum.tile([P, DV], F32, name="sum%d" % b, tag="acc%d" % b) for b in range(Q_BLOCKS)]
         squares = keep.tile([P, DV], BF16, name="squares")
+        half_blocks = Q_HALF // P
+        early_blocks = Q_BLOCKS - 1
 
-        def product(b, lo, hi, sum_sq):
-            nc.tensor.matmul_mx(out=sums[b][:, lo:hi],
-                                lhsT=y_codes[:, b * P:(b + 1) * P].bitcast(FP8X4), lhsT_scale=y_sc[:, b * P:(b + 1) * P],
-                                rhs=v_codes[:, lo:hi].bitcast(FP8X4), rhs_scale=v_sc[:, lo:hi], start=True, stop=True)
+        def product(b, i):
+            cols = slice(b % half_blocks * P, (b % half_blocks + 1) * P)
+            nc.tensor.matmul_mx(out=sums[b][:, i * E_HALF:(i + 1) * E_HALF],
+                                lhsT=y_codes[b // half_blocks][:, cols].bitcast(FP8X4), lhsT_scale=y_sc[:, b * P:(b + 1) * P],
+                                rhs=v_codes[i][:].bitcast(FP8X4), rhs_scale=v_sc[:, i * E_HALF:(i + 1) * E_HALF],
+                                start=True, stop=True)
+
+        def sum_squares(b, lo, hi, sum_sq):
             nc.scalar.activation(squares[:, lo:hi], sums[b][:, lo:hi], ACT.Square, accum_out=sum_sq[:, b:b + 1])
 
-        early_blocks = Q_HALF // P
         early_sq = keep.tile([P, early_blocks], F32, name="early_sq")
         early_ms = keep.tile([P, early_blocks], F32, name="early_ms")
-        for b in range(early_blocks):
-            product(b, 0, E_HALF, early_sq)
-            nc.gpsimd.tensor_scalar(early_ms[:, b:b + 1], early_sq[:, b:b + 1], 1.0 / DV, EPS, ALU.mult, ALU.add)
-        quantise_values(1)
-        quantise_y(1, y_bf1)
+
+        def early_product(b):
+            product(b, 0)
+            if b < early_blocks:
+                sum_squares(b, 0, E_HALF, early_sq)
+                nc.gpsimd.tensor_scalar(early_ms[:, b:b + 1], early_sq[:, b:b + 1], 1.0 / DV, EPS, ALU.mult, ALU.add)
+
+        for b in range(half_blocks):
+            early_product(b)
+
+        gather_and_turn(3)
+        y_bf1 = signed(1, y_mag[1])
+        y_codes.append(keep.tile([P, Q_HALF], U32, name="y_codes1", align_bytes=64))
+        quantise_y(1, y_bf1, y_codes[1])
+        for b in range(half_blocks, Q_BLOCKS):
+            early_product(b)
+        v_codes.append(keep.tile([P, E_HALF], U32, name="v_codes1", align_bytes=64))
+        quantise_values(1, v_codes[1])
 
         late_sq = keep.tile([P, Q_BLOCKS], F32, name="late_sq")
         rstd = keep.tile([P, Q_BLOCKS], F32, name="rstd")
         for b in range(Q_BLOCKS):
+            product(b, 1)
+        for b in range(Q_BLOCKS):
             early = b < early_blocks
-            product(b, E_HALF if early else 0, DV, late_sq)
+            sum_squares(b, E_HALF if early else 0, DV, late_sq)
             nc.scalar.activation(rstd[:, b:b + 1], late_sq[:, b:b + 1], ACT.Abs_reciprocal_sqrt,
                                  bias=early_ms[:, b:b + 1] if early else EPS, scale=1.0 / DV)
             res = keep.tile([P, DV], F32, name="res%d" % b)
-            pieces = 2 if b == Q_BLOCKS - 1 else 1
+            pieces = 2 if b in (0, Q_BLOCKS - 1) else 1
             for i in range(pieces):
                 cols = slice(i * DV // pieces, (i + 1) * DV // pieces)
                 nc.vector.tensor_scalar(res[:, cols], sums[b][:, cols], rstd[:, b:b + 1], None, ALU.mult)

@@ -25,10 +25,10 @@ PASSES = D // (P * PACK)
 QUADRANTS = 4
 E_BLOCKS = DV // P
 Q_BLOCKS = NQ // P
-Q_HALF = NQ // 2
 E_HALF = DV // 2
 WINDOW_BYTES = 4 * T
-Q_ON_VECTOR = (224, 256)
+Y_CUTS = (0, 256, 512)
+Q_ON_VECTOR = (224, 320)
 NB_ROW = P - 1
 KS_ROW = 96
 TINY = 2.0 ** -100
@@ -129,6 +129,11 @@ def tile_attend_mlpb_relu2_srt_kernel(tc, qT, k_words, k_scales, vT, nb, us, off
         q_codes = [keep.tile([P, NQ], U32, name="q_codes%d" % g, align_bytes=64) for g in range(PASSES)]
         quantise_queries(0, cast_queries(0), q_codes[0])
 
+        warm = psum.tile([P, NQ], F32, name="warm", tag="turn0")
+        for i in range(2):
+            nc.tensor.matmul_mx(out=warm[:], lhsT=q_codes[0][:, 0:P].bitcast(FP8X4), lhsT_scale=q_sc[:, 0, 0:P],
+                                rhs=q_codes[0][:].bitcast(FP8X4), rhs_scale=q_sc[:, 0, :], start=True, stop=True)
+
         kw_g = keep.tile([P, PACK, P], U32, name="kw_g")
         nc.vector.tensor_copy(kw_g[:].rearrange("p t m -> p m t"), kw_win[:].bitcast(U32).indirect(offsets[:]))
         k_codes = [keep.tile([P, N], U16, name="k_codes%d" % g, align_bytes=64) for g in range(PASSES)]
@@ -146,102 +151,110 @@ def tile_attend_mlpb_relu2_srt_kernel(tc, qT, k_words, k_scales, vT, nb, us, off
                                     rhs=q_codes[g][:].bitcast(FP8X4), rhs_scale=q_sc[:, g, :],
                                     start=(g == 0), stop=(g == PASSES - 1))
 
-        v_bf = [keep.tile([P, 2, P * PACK], BF16, name="v_bf%d" % i, tag="v_bf%d" % i, align_bytes=64) for i in range(2)]
         v_sc = keep.tile([P, DV], U8, name="v_sc", align_bytes=64)
         y_sc = keep.tile([P, NQ], U8, name="y_sc", align_bytes=64)
 
-        def gather_and_turn(e):
+        def gather(e):
             v_g = keep.tile([P, N], BF16, name="v_g%d" % e)
             nc.vector.tensor_copy(v_g[:], v_win[e][:].indirect(offsets[:]))
+            return v_g
+
+        def turn(e, v_g, dst):
             v_ps = psum.tile([P, 2, P], F32, name="v_ps%d" % e, tag="turn%d" % e)
             for u in range(2):
                 nc.tensor.transpose(v_ps[:, u, :], v_g[:].bitcast(F32)[:, u:N // 2:2], ident[:])
-            copy = nc.vector.tensor_copy if e < 2 else nc.scalar.copy
-            copy(v_bf[e // 2][:, e % 2, :].bitcast(F32).rearrange("p (e u) -> p e u", u=2),
+            copy = nc.vector.tensor_copy if e == 0 else nc.scalar.copy
+            copy(dst.bitcast(F32).rearrange("p (e u) -> p e u", u=2),
                  v_ps[:].rearrange("p u e -> p e u"))
 
-        def quantise_values(i, codes):
-            nc.vector.quantize_mx(out=codes[:].bitcast(FP8X4), scales=v_sc[:, i * E_HALF:(i + 1) * E_HALF],
-                                  in_=v_bf[i][:].rearrange("p e c -> p (e c)"))
+        def quantise_values(lo, hi, v_bf):
+            cols = slice(lo * P, hi * P)
+            nc.vector.quantize_mx(out=v_codes[:, cols].bitcast(FP8X4), scales=v_sc[:, cols],
+                                  in_=v_bf)
 
         def square(i):
-            relu = keep.tile([P, PACK, Q_HALF], F32, name="relu%d" % i, tag="relu")
+            lo, hi = Y_CUTS[i], Y_CUTS[i + 1]
+            relu = keep.tile([P, PACK, hi - lo], F32, name="relu%d" % i, tag="relu")
             for t in range(PACK):
-                nc.scalar.activation(relu[:, t, :], scores[t][:, i * Q_HALF:(i + 1) * Q_HALF], ACT.Relu,
+                nc.scalar.activation(relu[:, t, :], scores[t][:, lo:hi], ACT.Relu,
                                      bias=bias[:, t:t + 1], scale=root[:, t:t + 1])
-            y_mag = keep.tile([P, Q_HALF, PACK], BF16, name="y_mag%d" % i)
+            y_mag = keep.tile([P, hi - lo, PACK], BF16, name="y_mag%d" % i)
             dst, src = interleaved(y_mag[:], relu[:])
             nc.scalar.activation(dst, src, ACT.Square)
             return y_mag
 
-        def signed(i, y_mag):
-            y_bf = placed([P, Q_HALF, PACK], BF16, "y_bf%d" % i, 2 * i * WINDOW_BYTES)
-            signs = sgn[:].unsqueeze(1).to_broadcast([P, Q_HALF, PACK])
-            nc.vector.tensor_tensor(y_bf[:], y_mag[:], signs, ALU.mult)
+        def signed(i):
+            width = Y_CUTS[i + 1] - Y_CUTS[i]
+            y_bf = placed([P, width, PACK], BF16, "y_bf%d" % i, 2 * i * WINDOW_BYTES + WINDOW_BYTES // 2)
+            signs = sgn[:].unsqueeze(1).to_broadcast([P, width, PACK])
+            nc.vector.tensor_tensor(y_bf[:], y_mag[i][:], signs, ALU.mult)
             return y_bf
 
-        def quantise_y(i, y_bf, codes):
-            nc.vector.quantize_mx(out=codes[:].bitcast(FP8X4), scales=y_sc[:, i * Q_HALF:(i + 1) * Q_HALF],
+        def quantise_y(i, y_bf):
+            cols = slice(Y_CUTS[i], Y_CUTS[i + 1])
+            nc.vector.quantize_mx(out=y_codes[:, cols].bitcast(FP8X4), scales=y_sc[:, cols],
                                   in_=y_bf[:].rearrange("p q t -> p (q t)"))
 
-        y_mag = [square(0), square(1)]
-        gather_and_turn(0)
-        gather_and_turn(1)
-        y_bf0 = signed(0, y_mag[0])
-        gather_and_turn(2)
-        y_codes = [placed([P, Q_HALF], U32, "y_codes0", WINDOW_BYTES + 4 * E_HALF)]
-        quantise_y(0, y_bf0, y_codes[0])
-        v_codes = [placed([P, E_HALF], U32, "v_codes0", WINDOW_BYTES)]
-        quantise_values(0, v_codes[0])
+        y_mag = [square(i) for i in range(len(Y_CUTS) - 1)]
+        v_bf01 = keep.tile([P, 2 * N], BF16, name="v_bf01", align_bytes=64)
+        turn(0, gather(0), v_bf01[:, :N])
+        turn(1, gather(1), v_bf01[:, N:])
+        y_bf0 = signed(0)
+        v_g2 = gather(2)
+        y_codes = placed([P, NQ], U32, "y_codes", WINDOW_BYTES)
+        quantise_y(0, y_bf0)
+        v_codes = placed([P, DV], U32, "v_codes", WINDOW_BYTES + WINDOW_BYTES // 2)
+        quantise_values(0, 2, v_bf01[:])
 
         sums = [psum.tile([P, DV], F32, name="sum%d" % b, tag="acc%d" % b) for b in range(Q_BLOCKS)]
         squares = keep.tile([P, DV], BF16, name="squares")
-        half_blocks = Q_HALF // P
-        early_blocks = Q_BLOCKS - 1
+        early_blocks = Y_CUTS[-2] // P
 
-        def product(b, i):
-            cols = slice(b % half_blocks * P, (b % half_blocks + 1) * P)
-            nc.tensor.matmul_mx(out=sums[b][:, i * E_HALF:(i + 1) * E_HALF],
-                                lhsT=y_codes[b // half_blocks][:, cols].bitcast(FP8X4), lhsT_scale=y_sc[:, b * P:(b + 1) * P],
-                                rhs=v_codes[i][:].bitcast(FP8X4), rhs_scale=v_sc[:, i * E_HALF:(i + 1) * E_HALF],
-                                start=True, stop=True)
+        def product(b, lo, hi):
+            rows = slice(b * P, (b + 1) * P)
+            nc.tensor.matmul_mx(out=sums[b][:, lo:hi], lhsT=y_codes[:, rows].bitcast(FP8X4), lhsT_scale=y_sc[:, rows],
+                                rhs=v_codes[:, lo:hi].bitcast(FP8X4), rhs_scale=v_sc[:, lo:hi], start=True, stop=True)
 
         def sum_squares(b, lo, hi, sum_sq):
-            nc.scalar.activation(squares[:, lo:hi], sums[b][:, lo:hi], ACT.Square, accum_out=sum_sq[:, b:b + 1])
+            nc.scalar.activation(squares[:, 0:hi - lo], sums[b][:, lo:hi], ACT.Square, accum_out=sum_sq[:, b:b + 1])
 
-        early_sq = keep.tile([P, early_blocks], F32, name="early_sq")
-        early_ms = keep.tile([P, early_blocks], F32, name="early_ms")
+        cuts = (0, 2 * P, 3 * P, DV)
+        part_sq = [keep.tile([P, Q_BLOCKS], F32, name="part_sq%d" % i) for i in range(3)]
+        part_ms = [keep.tile([P, early_blocks], F32, name="part_ms%d" % i) for i in range(2)]
 
-        def early_product(b):
-            product(b, 0)
-            if b < early_blocks:
-                sum_squares(b, 0, E_HALF, early_sq)
-                nc.gpsimd.tensor_scalar(early_ms[:, b:b + 1], early_sq[:, b:b + 1], 1.0 / DV, EPS, ALU.mult, ALU.add)
+        def early_part(i):
+            for b in range(early_blocks):
+                product(b, cuts[i], cuts[i + 1])
+                sum_squares(b, cuts[i], cuts[i + 1], part_sq[i])
+                nc.gpsimd.tensor_scalar(part_ms[i][:, b:b + 1], part_sq[i][:, b:b + 1], 1.0 / DV,
+                                        part_ms[0][:, b:b + 1] if i else EPS, ALU.mult, ALU.add)
 
-        for b in range(half_blocks):
-            early_product(b)
+        early_part(0)
+        v_g3 = gather(3)
+        v_bf2 = placed([P, N], BF16, "v_bf2", 2 * WINDOW_BYTES)
+        turn(2, v_g2, v_bf2[:])
+        v_bf3 = keep.tile([P, N], BF16, name="v_bf3", align_bytes=64)
+        turn(3, v_g3, v_bf3[:])
+        y_bf1 = signed(1)
+        quantise_values(2, 3, v_bf2[:])
+        early_part(1)
+        quantise_y(1, y_bf1)
+        quantise_values(3, 4, v_bf3[:])
 
-        gather_and_turn(3)
-        y_bf1 = signed(1, y_mag[1])
-        y_codes.append(keep.tile([P, Q_HALF], U32, name="y_codes1", align_bytes=64))
-        quantise_y(1, y_bf1, y_codes[1])
-        for b in range(half_blocks, Q_BLOCKS):
-            early_product(b)
-        v_codes.append(keep.tile([P, E_HALF], U32, name="v_codes1", align_bytes=64))
-        quantise_values(1, v_codes[1])
-
-        late_sq = keep.tile([P, Q_BLOCKS], F32, name="late_sq")
         rstd = keep.tile([P, Q_BLOCKS], F32, name="rstd")
         for b in range(Q_BLOCKS):
-            product(b, 1)
+            product(b, cuts[2] if b < early_blocks else 0, DV)
         for b in range(Q_BLOCKS):
             early = b < early_blocks
-            sum_squares(b, E_HALF if early else 0, DV, late_sq)
-            nc.scalar.activation(rstd[:, b:b + 1], late_sq[:, b:b + 1], ACT.Abs_reciprocal_sqrt,
-                                 bias=early_ms[:, b:b + 1] if early else EPS, scale=1.0 / DV)
+            sum_squares(b, cuts[2] if early else 0, DV, part_sq[2])
+            nc.scalar.activation(rstd[:, b:b + 1], part_sq[2][:, b:b + 1], ACT.Abs_reciprocal_sqrt,
+                                 bias=part_ms[1][:, b:b + 1] if early else EPS, scale=1.0 / DV)
             res = keep.tile([P, DV], F32, name="res%d" % b)
             pieces = 2 if b in (0, Q_BLOCKS - 1) else 1
             for i in range(pieces):
                 cols = slice(i * DV // pieces, (i + 1) * DV // pieces)
-                nc.vector.tensor_scalar(res[:, cols], sums[b][:, cols], rstd[:, b:b + 1], None, ALU.mult)
+                if b == Q_BLOCKS - 1:
+                    nc.scalar.activation(res[:, cols], sums[b][:, cols], ACT.Copy, scale=rstd[:, b:b + 1])
+                else:
+                    nc.vector.tensor_scalar(res[:, cols], sums[b][:, cols], rstd[:, b:b + 1], None, ALU.mult)
                 nc.sync.dma_start(out[0, b * P:(b + 1) * P, cols], res[:, cols])

@@ -129,11 +129,6 @@ def tile_attend_mlpb_relu2_srt_kernel(tc, qT, k_words, k_scales, vT, nb, us, off
         q_codes = [keep.tile([P, NQ], U32, name="q_codes%d" % g, align_bytes=64) for g in range(PASSES)]
         quantise_queries(0, cast_queries(0), q_codes[0])
 
-        warm = psum.tile([P, NQ], F32, name="warm", tag="turn0")
-        for i in range(2):
-            nc.tensor.matmul_mx(out=warm[:], lhsT=q_codes[0][:, 0:P].bitcast(FP8X4), lhsT_scale=q_sc[:, 0, 0:P],
-                                rhs=q_codes[0][:].bitcast(FP8X4), rhs_scale=q_sc[:, 0, :], start=True, stop=True)
-
         kw_g = keep.tile([P, PACK, P], U32, name="kw_g")
         nc.vector.tensor_copy(kw_g[:].rearrange("p t m -> p m t"), kw_win[:].bitcast(U32).indirect(offsets[:]))
         k_codes = [keep.tile([P, N], U16, name="k_codes%d" % g, align_bytes=64) for g in range(PASSES)]
@@ -222,14 +217,14 @@ def tile_attend_mlpb_relu2_srt_kernel(tc, qT, k_words, k_scales, vT, nb, us, off
         part_sq = [keep.tile([P, Q_BLOCKS], F32, name="part_sq%d" % i) for i in range(3)]
         part_ms = [keep.tile([P, early_blocks], F32, name="part_ms%d" % i) for i in range(2)]
 
-        def early_part(i):
-            for b in range(early_blocks):
+        def early_part(i, blocks):
+            for b in range(blocks):
                 product(b, cuts[i], cuts[i + 1])
                 sum_squares(b, cuts[i], cuts[i + 1], part_sq[i])
                 nc.gpsimd.tensor_scalar(part_ms[i][:, b:b + 1], part_sq[i][:, b:b + 1], 1.0 / DV,
                                         part_ms[0][:, b:b + 1] if i else EPS, ALU.mult, ALU.add)
 
-        early_part(0)
+        early_part(0, early_blocks)
         v_g3 = gather(3)
         v_bf2 = placed([P, N], BF16, "v_bf2", 2 * WINDOW_BYTES)
         turn(2, v_g2, v_bf2[:])
@@ -237,24 +232,39 @@ def tile_attend_mlpb_relu2_srt_kernel(tc, qT, k_words, k_scales, vT, nb, us, off
         turn(3, v_g3, v_bf3[:])
         y_bf1 = signed(1)
         quantise_values(2, 3, v_bf2[:])
-        early_part(1)
+        early_part(1, 1)
         quantise_y(1, y_bf1)
+        last = Q_BLOCKS - 1
+        for i in range(2):
+            product(last, cuts[i], cuts[i + 1])
         quantise_values(3, 4, v_bf3[:])
 
         rstd = keep.tile([P, Q_BLOCKS], F32, name="rstd")
-        for b in range(Q_BLOCKS):
-            product(b, cuts[2] if b < early_blocks else 0, DV)
+        done = (2, 1, 0, 2)
+        for b in (0, last, 1, 2):
+            product(b, cuts[done[b]], DV)
+        stats = keep.tile([P, 6], F32, name="stats")
+        mean_var = keep.tile([P, 2], F32, name="mean_var")
+        last_ms = keep.tile([P, 1], F32, name="last_ms")
+        nc.vector.bn_stats(stats[:], sums[last][:])
         for b in range(Q_BLOCKS):
             early = b < early_blocks
-            sum_squares(b, cuts[2] if early else 0, DV, part_sq[2])
-            nc.scalar.activation(rstd[:, b:b + 1], part_sq[2][:, b:b + 1], ACT.Abs_reciprocal_sqrt,
-                                 bias=part_ms[1][:, b:b + 1] if early else EPS, scale=1.0 / DV)
+            if b == last:
+                nc.scalar.activation(rstd[:, b:b + 1], last_ms[:], ACT.Abs_reciprocal_sqrt, bias=EPS)
+            else:
+                sum_squares(b, cuts[done[b]], DV, part_sq[2])
+                nc.scalar.activation(rstd[:, b:b + 1], part_sq[2][:, b:b + 1], ACT.Abs_reciprocal_sqrt,
+                                     bias=part_ms[done[b] - 1][:, b:b + 1] if early else EPS, scale=1.0 / DV)
             res = keep.tile([P, DV], F32, name="res%d" % b)
-            pieces = 2 if b in (0, Q_BLOCKS - 1) else 1
+            pieces = 2
             for i in range(pieces):
                 cols = slice(i * DV // pieces, (i + 1) * DV // pieces)
-                if b == Q_BLOCKS - 1:
+                if b == last:
                     nc.scalar.activation(res[:, cols], sums[b][:, cols], ACT.Copy, scale=rstd[:, b:b + 1])
+                    nc.scalar.dma_start(out[0, b * P:(b + 1) * P, cols], res[:, cols])
                 else:
                     nc.vector.tensor_scalar(res[:, cols], sums[b][:, cols], rstd[:, b:b + 1], None, ALU.mult)
-                nc.sync.dma_start(out[0, b * P:(b + 1) * P, cols], res[:, cols])
+                    nc.sync.dma_start(out[0, b * P:(b + 1) * P, cols], res[:, cols])
+            if b == 0:
+                nc.vector.bn_aggr(mean_var[:], stats[:])
+                nc.gpsimd.tensor_scalar(last_ms[:], mean_var[:, 0:1], mean_var[:, 0:1], mean_var[:, 1:2], ALU.mult, ALU.add)

@@ -87,10 +87,9 @@ def tile_attend_mlpb_relu2_srt_kernel(tc, qT, k_words, k_scales, vT, nb, us, off
 
         inv_root = keep.tile([P, PACK], F32, name="inv_root")
         mag = keep.tile([P, PACK], F32, name="mag")
-        sgn = keep.tile([P, PACK], BF16, name="sgn")
+        signs = keep.tile([P, NQ // 2, PACK], BF16, name="signs")
         nc.scalar.activation(inv_root[:], us_sb[:], ACT.Abs_reciprocal_sqrt, bias=TINY)
         nc.scalar.activation(mag[:], us_sb[:], ACT.Abs)
-        nc.scalar.activation(sgn[:], us_sb[:], ACT.Sign)
         rough = keep.tile([P, PACK], F32, name="rough")
         step = keep.tile([P, PACK], F32, name="step")
         root = keep.tile([P, PACK], F32, name="root")
@@ -109,6 +108,7 @@ def tile_attend_mlpb_relu2_srt_kernel(tc, qT, k_words, k_scales, vT, nb, us, off
         bias = keep.tile([P, PACK], F32, name="bias")
         for t in range(PACK):
             nc.scalar.activation(bias[:, t:t + 1], nb_ps[:, t, NB_ROW:P], ACT.Copy, scale=root[:, t:t + 1])
+        nc.scalar.activation(signs[:], us_sb[:].unsqueeze(1).to_broadcast([P, NQ // 2, PACK]), ACT.Sign)
 
         q_sc = keep.tile([P, PASSES, NQ], U8, name="q_sc", align_bytes=64)
 
@@ -181,8 +181,7 @@ def tile_attend_mlpb_relu2_srt_kernel(tc, qT, k_words, k_scales, vT, nb, us, off
         def signed(i):
             width = Y_CUTS[i + 1] - Y_CUTS[i]
             y_bf = placed([P, width, PACK], BF16, "y_bf%d" % i, 2 * i * WINDOW_BYTES + WINDOW_BYTES // 2)
-            signs = sgn[:].unsqueeze(1).to_broadcast([P, width, PACK])
-            nc.vector.tensor_tensor(y_bf[:], y_mag[i][:], signs, ALU.mult)
+            nc.vector.tensor_tensor(y_bf[:], y_mag[i][:], signs[:], ALU.mult)
             return y_bf
 
         def quantise_y(i, y_bf):
@@ -235,12 +234,11 @@ def tile_attend_mlpb_relu2_srt_kernel(tc, qT, k_words, k_scales, vT, nb, us, off
         early_part(1, 1)
         quantise_y(1, y_bf1)
         last = Q_BLOCKS - 1
-        for i in range(2):
-            product(last, cuts[i], cuts[i + 1])
+        product(last, cuts[0], cuts[1])
         quantise_values(3, 4, v_bf3[:])
 
         rstd = keep.tile([P, Q_BLOCKS], F32, name="rstd")
-        done = (2, 1, 0, 2)
+        done = (2, 1, 0, 1)
         for b in (0, last, 1, 2):
             product(b, cuts[done[b]], DV)
         stats = keep.tile([P, 6], F32, name="stats")

@@ -28,7 +28,8 @@ Q_BLOCKS = NQ // P
 E_HALF = DV // 2
 WINDOW_BYTES = 4 * T
 Y_CUTS = (0, 256, 512)
-Q_ON_VECTOR = (224, 320)
+Q_HALF = NQ // 2
+Q_ON_VECTOR = ((0, 160), (224, 96))
 NB_ROW = P - 1
 KS_ROW = 96
 TINY = 2.0 ** -100
@@ -61,6 +62,7 @@ def tile_attend_mlpb_relu2_srt_kernel(tc, qT, k_words, k_scales, vT, nb, us, off
         nc.sync.dma_start(q_raw[0][:], q_rows[0])
         kw_win = keep.tile([P, T], I32, name="kw_win")
         nc.sync.dma_start(kw_win[:], k_words[0].rearrange("p t b -> p (t b)").bitcast(I32))
+        nc.sync.dma_start(q_raw[1][:], q_rows[1])
 
         k_sc = keep.tile([P, PASSES, N], U8, name="k_sc", align_bytes=64)
         nc.vector.memset(ks_win[0:KS_ROW, :].bitcast(I32), 0)
@@ -78,7 +80,6 @@ def tile_attend_mlpb_relu2_srt_kernel(tc, qT, k_words, k_scales, vT, nb, us, off
             nc.sync.dma_start(k_sc[32 * quad:32 * quad + 4].rearrange("p g c -> p (g c)").bitcast(I32),
                               ks_d[row:row + 8].rearrange("p t m -> p (t m)").bitcast(I32))
 
-        nc.sync.dma_start(q_raw[1][:], q_rows[1])
         v_win = [keep.tile([P, T], F32, name="v_win0")]
         for e in range(1, E_BLOCKS):
             v_win.append(placed([P, T], F32, "v_win%d" % e, (e - 1) * WINDOW_BYTES))
@@ -110,24 +111,26 @@ def tile_attend_mlpb_relu2_srt_kernel(tc, qT, k_words, k_scales, vT, nb, us, off
             nc.scalar.activation(bias[:, t:t + 1], nb_ps[:, t, NB_ROW:P], ACT.Copy, scale=root[:, t:t + 1])
         nc.scalar.activation(signs[:], us_sb[:].unsqueeze(1).to_broadcast([P, NQ // 2, PACK]), ACT.Sign)
 
-        q_sc = keep.tile([P, PASSES, NQ], U8, name="q_sc", align_bytes=64)
-
-        def cast_queries(g):
-            q_bf = keep.tile([P, NQ, PACK], BF16, name="q_bf%d" % g, align_bytes=64)
-            cut = Q_ON_VECTOR[g]
-            dst, src = interleaved(q_bf[:, cut:, :], q_raw[g][:, :, cut:])
+        def cast_queries(h, g):
+            q_bf = keep.tile([P, Q_HALF, PACK], BF16, name="q_bf%d%d" % (h, g), align_bytes=64)
+            raw = q_raw[g][:, :, h * Q_HALF:(h + 1) * Q_HALF]
+            cut = Q_ON_VECTOR[h][g]
+            dst, src = interleaved(q_bf[:, cut:, :], raw[:, :, cut:])
             nc.scalar.copy(dst, src)
             if cut:
-                dst, src = interleaved(q_bf[:, :cut, :], q_raw[g][:, :, :cut])
+                dst, src = interleaved(q_bf[:, :cut, :], raw[:, :, :cut])
                 nc.vector.tensor_copy(dst, src)
             return q_bf
 
-        def quantise_queries(g, q_bf, codes):
-            nc.vector.quantize_mx(out=codes[:].bitcast(FP8X4), scales=q_sc[:, g, :],
+        def quantise_queries(h, g, q_bf):
+            codes = keep.tile([P, Q_HALF], U32, name="q_codes%d%d" % (h, g), align_bytes=64)
+            scales = keep.tile([P, Q_HALF], U8, name="q_sc%d%d" % (h, g), align_bytes=64)
+            nc.vector.quantize_mx(out=codes[:].bitcast(FP8X4), scales=scales[:],
                                   in_=q_bf[:].rearrange("p q t -> p (q t)"))
+            return codes, scales
 
-        q_codes = [keep.tile([P, NQ], U32, name="q_codes%d" % g, align_bytes=64) for g in range(PASSES)]
-        quantise_queries(0, cast_queries(0), q_codes[0])
+        q_bf0 = [cast_queries(h, 0) for h in range(2)]
+        q_mx0 = [quantise_queries(h, 0, q_bf0[h]) for h in range(2)]
 
         kw_g = keep.tile([P, PACK, P], U32, name="kw_g")
         nc.vector.tensor_copy(kw_g[:].rearrange("p t m -> p m t"), kw_win[:].bitcast(U32).indirect(offsets[:]))
@@ -135,16 +138,43 @@ def tile_attend_mlpb_relu2_srt_kernel(tc, qT, k_words, k_scales, vT, nb, us, off
         halves = kw_g[:].rearrange("p t m -> p (t m)").bitcast(U16).rearrange("p (c g) -> p g c", g=2)
         for g in range(PASSES):
             nc.vector.tensor_copy(k_codes[g][:], halves[:, g, :])
-        quantise_queries(1, cast_queries(1), q_codes[1])
+        q_bf1 = [cast_queries(h, 1) for h in range(2)]
+        q_mx1 = [quantise_queries(h, 1, q_bf1[h]) for h in range(2)]
 
         scores = [psum.tile([P, NQ], F32, name="score%d" % t, tag="acc%d" % t) for t in range(PACK)]
-        for g in range(PASSES):
-            for t in range(PACK):
-                nc.tensor.matmul_mx(out=scores[t][:],
-                                    lhsT=k_codes[g][:, t * P:(t + 1) * P].bitcast(FP4X4),
-                                    lhsT_scale=k_sc[:, g, t * P:(t + 1) * P],
-                                    rhs=q_codes[g][:].bitcast(FP8X4), rhs_scale=q_sc[:, g, :],
-                                    start=(g == 0), stop=(g == PASSES - 1))
+        spare = [psum.tile([P, P], F32, name="spare%d" % t, tag="turn%d" % t) for t in range(PACK)]
+
+        def score_pass(dst, t, g, q_mx, c):
+            codes, scales = q_mx
+            nc.tensor.matmul_mx(out=dst, lhsT=k_codes[g][:, t * P:(t + 1) * P].bitcast(FP4X4),
+                                lhsT_scale=k_sc[:, g, t * P:(t + 1) * P],
+                                rhs=codes[:, c:c + P].bitcast(FP8X4), rhs_scale=scales[:, c:c + P],
+                                start=(g == 0), stop=(g == PASSES - 1))
+
+        def rectify(dst, src, t):
+            nc.scalar.activation(dst, src, ACT.Relu, bias=bias[:, t:t + 1], scale=root[:, t:t + 1])
+
+        def square(h, relu):
+            y_abs = keep.tile([P, Q_HALF, PACK], BF16, name="y_mag%d" % h)
+            dst, src = interleaved(y_abs[:], relu[:])
+            nc.scalar.activation(dst, src, ACT.Square)
+            return y_abs
+
+        first = [(t, c, scores[t][:, :P] if c == 0 else spare[t][:]) for c in (0, P) for t in range(PACK)]
+        for t, c, dst in first:
+            score_pass(dst, t, 0, q_mx0[0], c)
+        relu = keep.tile([P, PACK, Q_HALF], F32, name="relu0", tag="relu")
+        for t, c, dst in first:
+            score_pass(dst, t, 1, q_mx1[0], c)
+            rectify(relu[:, t, c:c + P], dst, t)
+        y_mag = [square(0, relu)]
+        relu = keep.tile([P, PACK, Q_HALF], F32, name="relu1", tag="relu")
+        for t in range(PACK):
+            for c in (0, P):
+                score_pass(scores[t][:, Q_HALF + c:Q_HALF + c + P], t, 0, q_mx0[1], c)
+                score_pass(scores[t][:, Q_HALF + c:Q_HALF + c + P], t, 1, q_mx1[1], c)
+            rectify(relu[:, t, :], scores[t][:, Q_HALF:], t)
+        y_mag.append(square(1, relu))
 
         v_sc = keep.tile([P, DV], U8, name="v_sc", align_bytes=64)
         y_sc = keep.tile([P, NQ], U8, name="y_sc", align_bytes=64)
@@ -167,17 +197,6 @@ def tile_attend_mlpb_relu2_srt_kernel(tc, qT, k_words, k_scales, vT, nb, us, off
             nc.vector.quantize_mx(out=v_codes[:, cols].bitcast(FP8X4), scales=v_sc[:, cols],
                                   in_=v_bf)
 
-        def square(i):
-            lo, hi = Y_CUTS[i], Y_CUTS[i + 1]
-            relu = keep.tile([P, PACK, hi - lo], F32, name="relu%d" % i, tag="relu")
-            for t in range(PACK):
-                nc.scalar.activation(relu[:, t, :], scores[t][:, lo:hi], ACT.Relu,
-                                     bias=bias[:, t:t + 1], scale=root[:, t:t + 1])
-            y_mag = keep.tile([P, hi - lo, PACK], BF16, name="y_mag%d" % i)
-            dst, src = interleaved(y_mag[:], relu[:])
-            nc.scalar.activation(dst, src, ACT.Square)
-            return y_mag
-
         def signed(i):
             width = Y_CUTS[i + 1] - Y_CUTS[i]
             y_bf = placed([P, width, PACK], BF16, "y_bf%d" % i, 2 * i * WINDOW_BYTES + WINDOW_BYTES // 2)
@@ -189,7 +208,6 @@ def tile_attend_mlpb_relu2_srt_kernel(tc, qT, k_words, k_scales, vT, nb, us, off
             nc.vector.quantize_mx(out=y_codes[:, cols].bitcast(FP8X4), scales=y_sc[:, cols],
                                   in_=y_bf[:].rearrange("p q t -> p (q t)"))
 
-        y_mag = [square(i) for i in range(len(Y_CUTS) - 1)]
         v_bf01 = keep.tile([P, 2 * N], BF16, name="v_bf01", align_bytes=64)
         turn(0, gather(0), v_bf01[:, :N])
         turn(1, gather(1), v_bf01[:, N:])

@@ -155,7 +155,7 @@ def tile_attend_mlpb_relu2_srt_kernel(tc, qT, k_words, k_scales, vT, nb, us, off
             nc.scalar.activation(dst, src, ACT.Relu, bias=bias[:, t:t + 1], scale=root[:, t:t + 1])
 
         def square(h, relu):
-            y_abs = keep.tile([P, Q_HALF, PACK], BF16, name="y_mag%d" % h)
+            y_abs = placed([P, Q_HALF, PACK], BF16, "y_mag%d" % h, (4 - h) * WINDOW_BYTES + WINDOW_BYTES // 4)
             dst, src = interleaved(y_abs[:], relu[:])
             nc.scalar.activation(dst, src, ACT.Square)
             return y_abs
@@ -174,13 +174,12 @@ def tile_attend_mlpb_relu2_srt_kernel(tc, qT, k_words, k_scales, vT, nb, us, off
                 score_pass(scores[t][:, Q_HALF + c:Q_HALF + c + P], t, 0, q_mx0[1], c)
                 score_pass(scores[t][:, Q_HALF + c:Q_HALF + c + P], t, 1, q_mx1[1], c)
             rectify(relu[:, t, :], scores[t][:, Q_HALF:], t)
-        y_mag.append(square(1, relu))
 
         v_sc = keep.tile([P, DV], U8, name="v_sc", align_bytes=64)
         y_sc = keep.tile([P, NQ], U8, name="y_sc", align_bytes=64)
 
         def gather(e):
-            v_g = keep.tile([P, N], BF16, name="v_g%d" % e)
+            v_g = placed([P, N], BF16, "v_g%d" % e, 3 * WINDOW_BYTES + e * WINDOW_BYTES // 4)
             nc.vector.tensor_copy(v_g[:], v_win[e][:].indirect(offsets[:]))
             return v_g
 
@@ -188,9 +187,7 @@ def tile_attend_mlpb_relu2_srt_kernel(tc, qT, k_words, k_scales, vT, nb, us, off
             v_ps = psum.tile([P, 2, P], F32, name="v_ps%d" % e, tag="turn%d" % e)
             for u in range(2):
                 nc.tensor.transpose(v_ps[:, u, :], v_g[:].bitcast(F32)[:, u:N // 2:2], ident[:])
-            copy = nc.vector.tensor_copy if e == 0 else nc.scalar.copy
-            copy(dst.bitcast(F32).rearrange("p (e u) -> p e u", u=2),
-                 v_ps[:].rearrange("p u e -> p e u"))
+            nc.scalar.copy(dst.bitcast(F32).rearrange("p (e u) -> p e u", u=2), v_ps[:].rearrange("p u e -> p e u"))
 
         def quantise_values(lo, hi, v_bf):
             cols = slice(lo * P, hi * P)
@@ -211,6 +208,7 @@ def tile_attend_mlpb_relu2_srt_kernel(tc, qT, k_words, k_scales, vT, nb, us, off
         v_bf01 = keep.tile([P, 2 * N], BF16, name="v_bf01", align_bytes=64)
         turn(0, gather(0), v_bf01[:, :N])
         turn(1, gather(1), v_bf01[:, N:])
+        y_mag.append(square(1, relu))
         y_bf0 = signed(0)
         v_g2 = gather(2)
         y_codes = placed([P, NQ], U32, "y_codes", WINDOW_BYTES)

@@ -27,7 +27,6 @@ E_BLOCKS = DV // P
 Q_BLOCKS = NQ // P
 E_HALF = DV // 2
 WINDOW_BYTES = 4 * T
-Y_CUTS = (0, 256, 512)
 Q_HALF = NQ // 2
 Q_ON_VECTOR = ((0, 160), (224, 96))
 NB_ROW = P - 1
@@ -80,15 +79,13 @@ def tile_attend_mlpb_relu2_srt_kernel(tc, qT, k_words, k_scales, vT, nb, us, off
             nc.sync.dma_start(k_sc[32 * quad:32 * quad + 4].rearrange("p g c -> p (g c)").bitcast(I32),
                               ks_d[row:row + 8].rearrange("p t m -> p (t m)").bitcast(I32))
 
-        v_win = [keep.tile([P, T], F32, name="v_win0")]
-        for e in range(1, E_BLOCKS):
-            v_win.append(placed([P, T], F32, "v_win%d" % e, (e - 1) * WINDOW_BYTES))
+        v_win = [placed([P, T], F32, "v_win%d" % e, e * WINDOW_BYTES) for e in range(E_BLOCKS)]
         for e in range(E_BLOCKS):
             nc.sync.dma_start(v_win[e][:], vT[e * P:(e + 1) * P, :])
 
         inv_root = keep.tile([P, PACK], F32, name="inv_root")
         mag = keep.tile([P, PACK], F32, name="mag")
-        signs = keep.tile([P, NQ // 2, PACK], BF16, name="signs")
+        signs = keep.tile([P, P, PACK], BF16, name="signs")
         nc.scalar.activation(inv_root[:], us_sb[:], ACT.Abs_reciprocal_sqrt, bias=TINY)
         nc.scalar.activation(mag[:], us_sb[:], ACT.Abs)
         rough = keep.tile([P, PACK], F32, name="rough")
@@ -109,7 +106,7 @@ def tile_attend_mlpb_relu2_srt_kernel(tc, qT, k_words, k_scales, vT, nb, us, off
         bias = keep.tile([P, PACK], F32, name="bias")
         for t in range(PACK):
             nc.scalar.activation(bias[:, t:t + 1], nb_ps[:, t, NB_ROW:P], ACT.Copy, scale=root[:, t:t + 1])
-        nc.scalar.activation(signs[:], us_sb[:].unsqueeze(1).to_broadcast([P, NQ // 2, PACK]), ACT.Sign)
+        nc.scalar.activation(signs[:], us_sb[:].unsqueeze(1).to_broadcast([P, P, PACK]), ACT.Sign)
 
         def cast_queries(h, g):
             q_bf = keep.tile([P, Q_HALF, PACK], BF16, name="q_bf%d%d" % (h, g), align_bytes=64)
@@ -154,32 +151,35 @@ def tile_attend_mlpb_relu2_srt_kernel(tc, qT, k_words, k_scales, vT, nb, us, off
         def rectify(dst, src, t):
             nc.scalar.activation(dst, src, ACT.Relu, bias=bias[:, t:t + 1], scale=root[:, t:t + 1])
 
-        def square(h, relu):
-            y_abs = placed([P, Q_HALF, PACK], BF16, "y_mag%d" % h, (4 - h) * WINDOW_BYTES + WINDOW_BYTES // 4)
-            dst, src = interleaved(y_abs[:], relu[:])
+        def square(b, relu):
+            y_abs = keep.tile([P, P, PACK], BF16, name="y_mag%d" % b)
+            dst, src = interleaved(y_abs[:], relu[:, :, b % 2 * P:(b % 2 + 1) * P])
             nc.scalar.activation(dst, src, ACT.Square)
             return y_abs
 
         first = [(t, c, scores[t][:, :P] if c == 0 else spare[t][:]) for c in (0, P) for t in range(PACK)]
         for t, c, dst in first:
             score_pass(dst, t, 0, q_mx0[0], c)
-        relu = keep.tile([P, PACK, Q_HALF], F32, name="relu0", tag="relu")
+        relu = [keep.tile([P, PACK, Q_HALF], F32, name="relu%d" % h) for h in range(2)]
+        y_mag = []
         for t, c, dst in first:
             score_pass(dst, t, 1, q_mx1[0], c)
-            rectify(relu[:, t, c:c + P], dst, t)
-        y_mag = [square(0, relu)]
-        relu = keep.tile([P, PACK, Q_HALF], F32, name="relu1", tag="relu")
+            rectify(relu[0][:, t, c:c + P], dst, t)
+            if t == PACK - 1:
+                y_mag.append(square(c // P, relu[0]))
         for t in range(PACK):
             for c in (0, P):
                 score_pass(scores[t][:, Q_HALF + c:Q_HALF + c + P], t, 0, q_mx0[1], c)
                 score_pass(scores[t][:, Q_HALF + c:Q_HALF + c + P], t, 1, q_mx1[1], c)
-            rectify(relu[:, t, :], scores[t][:, Q_HALF:], t)
+            rectify(relu[1][:, t, :], scores[t][:, Q_HALF:], t)
+        y_mag.append(square(2, relu[1]))
 
         v_sc = keep.tile([P, DV], U8, name="v_sc", align_bytes=64)
         y_sc = keep.tile([P, NQ], U8, name="y_sc", align_bytes=64)
+        y_codes = keep.tile([P, NQ], U32, name="y_codes", align_bytes=64)
 
         def gather(e):
-            v_g = placed([P, N], BF16, "v_g%d" % e, 3 * WINDOW_BYTES + e * WINDOW_BYTES // 4)
+            v_g = keep.tile([P, N], BF16, name="v_g%d" % e)
             nc.vector.tensor_copy(v_g[:], v_win[e][:].indirect(offsets[:]))
             return v_g
 
@@ -190,85 +190,102 @@ def tile_attend_mlpb_relu2_srt_kernel(tc, qT, k_words, k_scales, vT, nb, us, off
             nc.scalar.copy(dst.bitcast(F32).rearrange("p (e u) -> p e u", u=2), v_ps[:].rearrange("p u e -> p e u"))
 
         def quantise_values(lo, hi, v_bf):
-            cols = slice(lo * P, hi * P)
-            nc.vector.quantize_mx(out=v_codes[:, cols].bitcast(FP8X4), scales=v_sc[:, cols],
-                                  in_=v_bf)
+            first = lo // 2 * E_HALF
+            nc.vector.quantize_mx(out=v_codes[lo // 2][:, lo * P - first:hi * P - first].bitcast(FP8X4),
+                                  scales=v_sc[:, lo * P:hi * P], in_=v_bf)
 
-        def signed(i):
-            width = Y_CUTS[i + 1] - Y_CUTS[i]
-            y_bf = placed([P, width, PACK], BF16, "y_bf%d" % i, 2 * i * WINDOW_BYTES + WINDOW_BYTES // 2)
-            nc.vector.tensor_tensor(y_bf[:], y_mag[i][:], signs[:], ALU.mult)
+        def signed(b):
+            if b == Q_BLOCKS - 1:
+                y_bf = placed([P, P, PACK], BF16, "y_bf%d" % b, b * WINDOW_BYTES)
+            else:
+                y_bf = keep.tile([P, P, PACK], BF16, name="y_bf%d" % b, align_bytes=64)
+            nc.vector.tensor_tensor(y_bf[:], y_mag[b][:], signs[:], ALU.mult)
             return y_bf
 
-        def quantise_y(i, y_bf):
-            cols = slice(Y_CUTS[i], Y_CUTS[i + 1])
+        def quantise_y(b, y_bf):
+            cols = slice(b * P, (b + 1) * P)
             nc.vector.quantize_mx(out=y_codes[:, cols].bitcast(FP8X4), scales=y_sc[:, cols],
                                   in_=y_bf[:].rearrange("p q t -> p (q t)"))
 
         v_bf01 = keep.tile([P, 2 * N], BF16, name="v_bf01", align_bytes=64)
         turn(0, gather(0), v_bf01[:, :N])
+        quantise_y(0, signed(0))
         turn(1, gather(1), v_bf01[:, N:])
-        y_mag.append(square(1, relu))
-        y_bf0 = signed(0)
+        quantise_y(1, signed(1))
+        y_mag.append(square(3, relu[1]))
+        warm = psum.tile([P, N], F32, name="warm", tag="turn0")
+
+        def warm_up(b):
+            rows = slice(b * P, (b + 1) * P)
+            nc.tensor.matmul_mx(out=warm[:], lhsT=y_codes[:, rows].bitcast(FP8X4), lhsT_scale=y_sc[:, rows],
+                                rhs=k_codes[0][:].bitcast(FP4X4), rhs_scale=k_sc[:, 0, :], start=True, stop=True)
+
+        warm_up(1)
+        warm_up(1)
         v_g2 = gather(2)
-        y_codes = placed([P, NQ], U32, "y_codes", WINDOW_BYTES)
-        quantise_y(0, y_bf0)
-        v_codes = placed([P, DV], U32, "v_codes", WINDOW_BYTES + WINDOW_BYTES // 2)
+        v_bf2 = keep.tile([P, N], BF16, name="v_bf2", align_bytes=64)
+        turn(2, v_g2, v_bf2[:])
+        y_bf2 = signed(2)
+        v_codes = [placed([P, E_HALF], U32, "v_codes0", 2 * WINDOW_BYTES + WINDOW_BYTES // 2)]
         quantise_values(0, 2, v_bf01[:])
+        quantise_y(2, y_bf2)
 
         sums = [psum.tile([P, DV], F32, name="sum%d" % b, tag="acc%d" % b) for b in range(Q_BLOCKS)]
         squares = keep.tile([P, DV], BF16, name="squares")
-        early_blocks = Y_CUTS[-2] // P
+        last = Q_BLOCKS - 1
 
         def product(b, lo, hi):
             rows = slice(b * P, (b + 1) * P)
+            half = lo // E_HALF
             nc.tensor.matmul_mx(out=sums[b][:, lo:hi], lhsT=y_codes[:, rows].bitcast(FP8X4), lhsT_scale=y_sc[:, rows],
-                                rhs=v_codes[:, lo:hi].bitcast(FP8X4), rhs_scale=v_sc[:, lo:hi], start=True, stop=True)
+                                rhs=v_codes[half][:, lo - half * E_HALF:hi - half * E_HALF].bitcast(FP8X4),
+                                rhs_scale=v_sc[:, lo:hi], start=True, stop=True)
 
         def sum_squares(b, lo, hi, sum_sq):
             nc.scalar.activation(squares[:, 0:hi - lo], sums[b][:, lo:hi], ACT.Square, accum_out=sum_sq[:, b:b + 1])
 
         cuts = (0, 2 * P, 3 * P, DV)
         part_sq = [keep.tile([P, Q_BLOCKS], F32, name="part_sq%d" % i) for i in range(3)]
-        part_ms = [keep.tile([P, early_blocks], F32, name="part_ms%d" % i) for i in range(2)]
+        part_ms = [keep.tile([P, last], F32, name="part_ms%d" % i) for i in range(2)]
 
-        def early_part(i, blocks):
-            for b in range(blocks):
-                product(b, cuts[i], cuts[i + 1])
-                sum_squares(b, cuts[i], cuts[i + 1], part_sq[i])
-                nc.gpsimd.tensor_scalar(part_ms[i][:, b:b + 1], part_sq[i][:, b:b + 1], 1.0 / DV,
-                                        part_ms[0][:, b:b + 1] if i else EPS, ALU.mult, ALU.add)
+        def early_sum(i, b):
+            sum_squares(b, cuts[i], cuts[i + 1], part_sq[i])
+            nc.gpsimd.tensor_scalar(part_ms[i][:, b:b + 1], part_sq[i][:, b:b + 1], 1.0 / DV,
+                                    part_ms[0][:, b:b + 1] if i else EPS, ALU.mult, ALU.add)
 
-        early_part(0, early_blocks)
+        for b in range(last):
+            product(b, cuts[0], cuts[1])
+            early_sum(0, b)
+        warm_up(2)
         v_g3 = gather(3)
-        v_bf2 = placed([P, N], BF16, "v_bf2", 2 * WINDOW_BYTES)
-        turn(2, v_g2, v_bf2[:])
         v_bf3 = keep.tile([P, N], BF16, name="v_bf3", align_bytes=64)
         turn(3, v_g3, v_bf3[:])
-        y_bf1 = signed(1)
+        y_bf3 = signed(3)
+        v_codes.append(placed([P, E_HALF], U32, "v_codes1", 3 * WINDOW_BYTES + WINDOW_BYTES // 2))
         quantise_values(2, 3, v_bf2[:])
-        early_part(1, 1)
-        quantise_y(1, y_bf1)
-        last = Q_BLOCKS - 1
+        quantise_y(3, y_bf3)
+        product(0, cuts[1], cuts[2])
+        early_sum(1, 0)
         product(last, cuts[0], cuts[1])
+        for b in (last, 1, 2):
+            product(b, cuts[1], cuts[2])
         quantise_values(3, 4, v_bf3[:])
 
         rstd = keep.tile([P, Q_BLOCKS], F32, name="rstd")
-        done = (2, 1, 0, 1)
         for b in (0, last, 1, 2):
-            product(b, cuts[done[b]], DV)
+            product(b, cuts[2], DV)
         stats = keep.tile([P, 6], F32, name="stats")
         mean_var = keep.tile([P, 2], F32, name="mean_var")
         last_ms = keep.tile([P, 1], F32, name="last_ms")
         nc.vector.bn_stats(stats[:], sums[last][:])
         for b in range(Q_BLOCKS):
-            early = b < early_blocks
             if b == last:
                 nc.scalar.activation(rstd[:, b:b + 1], last_ms[:], ACT.Abs_reciprocal_sqrt, bias=EPS)
             else:
-                sum_squares(b, cuts[done[b]], DV, part_sq[2])
+                done = 2 if b == 0 else 1
+                sum_squares(b, cuts[done], DV, part_sq[2])
                 nc.scalar.activation(rstd[:, b:b + 1], part_sq[2][:, b:b + 1], ACT.Abs_reciprocal_sqrt,
-                                     bias=part_ms[done[b] - 1][:, b:b + 1] if early else EPS, scale=1.0 / DV)
+                                     bias=part_ms[done - 1][:, b:b + 1], scale=1.0 / DV)
             res = keep.tile([P, DV], F32, name="res%d" % b)
             pieces = 2
             for i in range(pieces):

@@ -61,7 +61,6 @@ def tile_attend_mlpb_relu2_srt_kernel(tc, qT, k_words, k_scales, vT, nb, us, off
         nc.sync.dma_start(q_raw[0][:], q_rows[0])
         kw_win = keep.tile([P, T], I32, name="kw_win")
         nc.sync.dma_start(kw_win[:], k_words[0].rearrange("p t b -> p (t b)").bitcast(I32))
-        nc.sync.dma_start(q_raw[1][:], q_rows[1])
 
         k_sc = keep.tile([P, PASSES, N], U8, name="k_sc", align_bytes=64)
         nc.vector.memset(ks_win[0:KS_ROW, :].bitcast(I32), 0)
@@ -79,6 +78,7 @@ def tile_attend_mlpb_relu2_srt_kernel(tc, qT, k_words, k_scales, vT, nb, us, off
             nc.sync.dma_start(k_sc[32 * quad:32 * quad + 4].rearrange("p g c -> p (g c)").bitcast(I32),
                               ks_d[row:row + 8].rearrange("p t m -> p (t m)").bitcast(I32))
 
+        nc.sync.dma_start(q_raw[1][:], q_rows[1])
         v_win = [placed([P, T], F32, "v_win%d" % e, e * WINDOW_BYTES) for e in range(E_BLOCKS)]
         for e in range(E_BLOCKS):
             nc.sync.dma_start(v_win[e][:], vT[e * P:(e + 1) * P, :])
@@ -195,7 +195,7 @@ def tile_attend_mlpb_relu2_srt_kernel(tc, qT, k_words, k_scales, vT, nb, us, off
                                   scales=v_sc[:, lo * P:hi * P], in_=v_bf)
 
         def signed(b):
-            if b == Q_BLOCKS - 1:
+            if b >= 1:
                 y_bf = placed([P, P, PACK], BF16, "y_bf%d" % b, b * WINDOW_BYTES)
             else:
                 y_bf = keep.tile([P, P, PACK], BF16, name="y_bf%d" % b, align_bytes=64)

@@ -213,15 +213,6 @@ def tile_attend_mlpb_relu2_srt_kernel(tc, qT, k_words, k_scales, vT, nb, us, off
         turn(1, gather(1), v_bf01[:, N:])
         quantise_y(1, signed(1))
         y_mag.append(square(3, relu[1]))
-        warm = psum.tile([P, N], F32, name="warm", tag="turn0")
-
-        def warm_up(b):
-            rows = slice(b * P, (b + 1) * P)
-            nc.tensor.matmul_mx(out=warm[:], lhsT=y_codes[:, rows].bitcast(FP8X4), lhsT_scale=y_sc[:, rows],
-                                rhs=k_codes[0][:].bitcast(FP4X4), rhs_scale=k_sc[:, 0, :], start=True, stop=True)
-
-        warm_up(1)
-        warm_up(1)
         v_g2 = gather(2)
         v_bf2 = keep.tile([P, N], BF16, name="v_bf2", align_bytes=64)
         turn(2, v_g2, v_bf2[:])
@@ -256,7 +247,6 @@ def tile_attend_mlpb_relu2_srt_kernel(tc, qT, k_words, k_scales, vT, nb, us, off
         for b in range(last):
             product(b, cuts[0], cuts[1])
             early_sum(0, b)
-        warm_up(2)
         v_g3 = gather(3)
         v_bf3 = keep.tile([P, N], BF16, name="v_bf3", align_bytes=64)
         turn(3, v_g3, v_bf3[:])

@@ -23,15 +23,15 @@ P = 128
 PACK = 4
 PASSES = D // (P * PACK)
 QUADRANTS = 4
-E_BLOCKS = DV // P
-Q_BLOCKS = NQ // P
-E_HALF = DV // 2
+BLOCKS = 4
+LAST = BLOCKS - 1
 WINDOW_BYTES = 4 * T
 Q_HALF = NQ // 2
-Q_ON_VECTOR = ((0, 160), (224, 96))
 NB_ROW = P - 1
-KS_ROW = 96
+KS_ROW = 32
 TINY = 2.0 ** -100
+PER_COLUMN = 16
+LAST_ON_VECTOR = 288
 
 
 def interleaved(dst, src):
@@ -48,14 +48,15 @@ def tile_attend_mlpb_relu2_srt_kernel(tc, qT, k_words, k_scales, vT, nb, us, off
         def placed(shape, dtype, name, offset):
             return turns.tile(shape, dtype, name=name, offset=offset, align_bytes=64)
 
-        offsets = keep.tile([P, N // 16], U16, name="offsets")
-        nc.sync.dma_start(offsets[:], offs)
+        offsets = keep.tile([P, N // PER_COLUMN], U16, name="offsets")
         ks_win = keep.tile([P, T], U8, name="ks_win")
         nb_win = keep.tile([P, T], F32, name="nb_win")
         us_sb = keep.tile([P, PACK], F32, name="us_sb")
-        nc.sync.dma_start(ks_win[KS_ROW:P, :].bitcast(I32), k_scales.rearrange("g f t -> f g t").bitcast(I32))
         nc.sync.dma_start(nb_win[NB_ROW:P, :], nb[0:1, :])
         nc.sync.dma_start(us_sb[:], us[0].rearrange("(p j) o -> p (j o)", j=PACK))
+        nc.sync.dma_start(ks_win[KS_ROW:KS_ROW + 32, :].bitcast(I32),
+                          k_scales.rearrange("g f t -> f g t").bitcast(I32))
+        nc.sync.dma_start(offsets[:], offs)
         q_raw = [keep.tile([P, PACK, NQ], F32, name="q_raw%d" % g) for g in range(PASSES)]
         q_rows = qT[0].rearrange("(g p j) q -> g p j q", g=PASSES, j=PACK)
         nc.sync.dma_start(q_raw[0][:], q_rows[0])
@@ -64,30 +65,31 @@ def tile_attend_mlpb_relu2_srt_kernel(tc, qT, k_words, k_scales, vT, nb, us, off
 
         k_sc = keep.tile([P, PASSES, N], U8, name="k_sc", align_bytes=64)
         nc.vector.memset(ks_win[0:KS_ROW, :].bitcast(I32), 0)
+        nc.vector.memset(ks_win[KS_ROW + 32:P, :].bitcast(I32), 0)
         nc.gpsimd.memset(nb_win[0:NB_ROW, :].bitcast(I32), 0)
         nc.vector.memset(k_sc[:].rearrange("p g c -> p (g c)").bitcast(I32), 0)
         ident = keep.tile([P, P], F32, name="ident")
         make_identity(nc, ident[:])
 
-        ks_g = keep.tile([P, N], U8, name="ks_g")
-        nc.vector.tensor_copy(ks_g[:], ks_win[:].indirect(offsets[:]))
-        ks_d = keep.tile([P, PACK, P], U8, name="ks_d")
-        nc.vector.tensor_copy(ks_d[:].rearrange("p t m -> p m t"), ks_g[:].rearrange("p (m t) -> p m t", t=PACK))
+        ks_g = keep.tile([P, PACK, P], U8, name="ks_g")
+        nc.vector.tensor_copy(ks_g[:].rearrange("p t m -> p m t"), ks_win[:].indirect(offsets[:]))
         for quad in range(QUADRANTS):
             row = KS_ROW + 8 * quad
             nc.sync.dma_start(k_sc[32 * quad:32 * quad + 4].rearrange("p g c -> p (g c)").bitcast(I32),
-                              ks_d[row:row + 8].rearrange("p t m -> p (t m)").bitcast(I32))
+                              ks_g[row:row + 8].rearrange("p t m -> p (t m)").bitcast(I32))
 
         nc.sync.dma_start(q_raw[1][:], q_rows[1])
-        v_win = [placed([P, T], F32, "v_win%d" % e, e * WINDOW_BYTES) for e in range(E_BLOCKS)]
-        for e in range(E_BLOCKS):
+        v_win = [placed([P, T], F32, "v_win%d" % e, e * WINDOW_BYTES) for e in range(BLOCKS)]
+        for e in range(BLOCKS):
             nc.sync.dma_start(v_win[e][:], vT[e * P:(e + 1) * P, :])
 
         inv_root = keep.tile([P, PACK], F32, name="inv_root")
         mag = keep.tile([P, PACK], F32, name="mag")
         signs = keep.tile([P, P, PACK], BF16, name="signs")
-        nc.scalar.activation(inv_root[:], us_sb[:], ACT.Abs_reciprocal_sqrt, bias=TINY)
-        nc.scalar.activation(mag[:], us_sb[:], ACT.Abs)
+        nc.vector.scalar_tensor_tensor(mag[:], us_sb[:], -1.0, us_sb[:], ALU.mult, ALU.max)
+        positive = keep.tile([P, PACK], F32, name="positive")
+        nc.vector.tensor_scalar(positive[:], us_sb[:], 0.0, None, ALU.is_ge)
+        nc.scalar.activation(inv_root[:], mag[:], ACT.Abs_reciprocal_sqrt, bias=TINY)
         rough = keep.tile([P, PACK], F32, name="rough")
         step = keep.tile([P, PACK], F32, name="step")
         root = keep.tile([P, PACK], F32, name="root")
@@ -106,28 +108,24 @@ def tile_attend_mlpb_relu2_srt_kernel(tc, qT, k_words, k_scales, vT, nb, us, off
         bias = keep.tile([P, PACK], F32, name="bias")
         for t in range(PACK):
             nc.scalar.activation(bias[:, t:t + 1], nb_ps[:, t, NB_ROW:P], ACT.Copy, scale=root[:, t:t + 1])
-        nc.scalar.activation(signs[:], us_sb[:].unsqueeze(1).to_broadcast([P, P, PACK]), ACT.Sign)
+        nc.scalar.activation(signs[:], positive[:].unsqueeze(1).to_broadcast([P, P, PACK]), ACT.Copy, bias=-1.0, scale=2.0)
 
-        def cast_queries(h, g):
-            q_bf = keep.tile([P, Q_HALF, PACK], BF16, name="q_bf%d%d" % (h, g), align_bytes=64)
-            raw = q_raw[g][:, :, h * Q_HALF:(h + 1) * Q_HALF]
-            cut = Q_ON_VECTOR[h][g]
-            dst, src = interleaved(q_bf[:, cut:, :], raw[:, :, cut:])
-            nc.scalar.copy(dst, src)
-            if cut:
-                dst, src = interleaved(q_bf[:, :cut, :], raw[:, :, :cut])
-                nc.vector.tensor_copy(dst, src)
-            return q_bf
+        q_bf = [keep.tile([P, NQ * PACK], BF16, name="q_bf%d" % g, align_bytes=64) for g in range(PASSES)]
+        q_codes = [keep.tile([P, NQ], U32, name="q_codes%d" % g, align_bytes=64) for g in range(PASSES)]
+        q_sc = [keep.tile([P, NQ], U8, name="q_sc%d" % g, align_bytes=64) for g in range(PASSES)]
 
-        def quantise_queries(h, g, q_bf):
-            codes = keep.tile([P, Q_HALF], U32, name="q_codes%d%d" % (h, g), align_bytes=64)
-            scales = keep.tile([P, Q_HALF], U8, name="q_sc%d%d" % (h, g), align_bytes=64)
-            nc.vector.quantize_mx(out=codes[:].bitcast(FP8X4), scales=scales[:],
-                                  in_=q_bf[:].rearrange("p q t -> p (q t)"))
-            return codes, scales
+        def cast_queries(copy, g, lo, hi):
+            dst = q_bf[g][:, lo * PACK:hi * PACK].rearrange("p (c t) -> p c t", t=PACK)
+            copy(*interleaved(dst, q_raw[g][:, :, lo:hi]))
 
-        q_bf0 = [cast_queries(h, 0) for h in range(2)]
-        q_mx0 = [quantise_queries(h, 0, q_bf0[h]) for h in range(2)]
+        def quantise_queries(g, lo, hi):
+            nc.vector.quantize_mx(out=q_codes[g][:, lo:hi].bitcast(FP8X4), scales=q_sc[g][:, lo:hi],
+                                  in_=q_bf[g][:, lo * PACK:hi * PACK])
+
+        cast_queries(nc.scalar.copy, 0, 0, Q_HALF)
+        cast_queries(nc.vector.tensor_copy, 0, Q_HALF, NQ)
+        quantise_queries(0, 0, Q_HALF)
+        quantise_queries(0, Q_HALF, NQ)
 
         kw_g = keep.tile([P, PACK, P], U32, name="kw_g")
         nc.vector.tensor_copy(kw_g[:].rearrange("p t m -> p m t"), kw_win[:].bitcast(U32).indirect(offsets[:]))
@@ -135,44 +133,32 @@ def tile_attend_mlpb_relu2_srt_kernel(tc, qT, k_words, k_scales, vT, nb, us, off
         halves = kw_g[:].rearrange("p t m -> p (t m)").bitcast(U16).rearrange("p (c g) -> p g c", g=2)
         for g in range(PASSES):
             nc.vector.tensor_copy(k_codes[g][:], halves[:, g, :])
-        q_bf1 = [cast_queries(h, 1) for h in range(2)]
-        q_mx1 = [quantise_queries(h, 1, q_bf1[h]) for h in range(2)]
+
+        for b in range(BLOCKS):
+            cast_queries(nc.scalar.copy if b % 2 else nc.vector.tensor_copy, 1, b * P, (b + 1) * P)
+        quantise_queries(1, 0, P)
+        quantise_queries(1, P, Q_HALF)
+        quantise_queries(1, Q_HALF, NQ)
 
         scores = [psum.tile([P, NQ], F32, name="score%d" % t, tag="acc%d" % t) for t in range(PACK)]
         spare = [psum.tile([P, P], F32, name="spare%d" % t, tag="turn%d" % t) for t in range(PACK)]
 
-        def score_pass(dst, t, g, q_mx, c):
-            codes, scales = q_mx
+        def score_pass(dst, t, g, lo, hi):
             nc.tensor.matmul_mx(out=dst, lhsT=k_codes[g][:, t * P:(t + 1) * P].bitcast(FP4X4),
                                 lhsT_scale=k_sc[:, g, t * P:(t + 1) * P],
-                                rhs=codes[:, c:c + P].bitcast(FP8X4), rhs_scale=scales[:, c:c + P],
+                                rhs=q_codes[g][:, lo:hi].bitcast(FP8X4), rhs_scale=q_sc[g][:, lo:hi],
                                 start=(g == 0), stop=(g == PASSES - 1))
 
         def rectify(dst, src, t):
             nc.scalar.activation(dst, src, ACT.Relu, bias=bias[:, t:t + 1], scale=root[:, t:t + 1])
 
-        def square(b, relu):
+        relu = [keep.tile([P, PACK, Q_HALF], F32, name="relu%d" % h) for h in range(2)]
+
+        def square(b):
             y_abs = keep.tile([P, P, PACK], BF16, name="y_mag%d" % b)
-            dst, src = interleaved(y_abs[:], relu[:, :, b % 2 * P:(b % 2 + 1) * P])
+            dst, src = interleaved(y_abs[:], relu[b // 2][:, :, b % 2 * P:(b % 2 + 1) * P])
             nc.scalar.activation(dst, src, ACT.Square)
             return y_abs
-
-        first = [(t, c, scores[t][:, :P] if c == 0 else spare[t][:]) for c in (0, P) for t in range(PACK)]
-        for t, c, dst in first:
-            score_pass(dst, t, 0, q_mx0[0], c)
-        relu = [keep.tile([P, PACK, Q_HALF], F32, name="relu%d" % h) for h in range(2)]
-        y_mag = []
-        for t, c, dst in first:
-            score_pass(dst, t, 1, q_mx1[0], c)
-            rectify(relu[0][:, t, c:c + P], dst, t)
-            if t == PACK - 1:
-                y_mag.append(square(c // P, relu[0]))
-        for t in range(PACK):
-            for c in (0, P):
-                score_pass(scores[t][:, Q_HALF + c:Q_HALF + c + P], t, 0, q_mx0[1], c)
-                score_pass(scores[t][:, Q_HALF + c:Q_HALF + c + P], t, 1, q_mx1[1], c)
-            rectify(relu[1][:, t, :], scores[t][:, Q_HALF:], t)
-        y_mag.append(square(2, relu[1]))
 
         v_sc = keep.tile([P, DV], U8, name="v_sc", align_bytes=64)
         y_sc = keep.tile([P, NQ], U8, name="y_sc", align_bytes=64)
@@ -180,26 +166,27 @@ def tile_attend_mlpb_relu2_srt_kernel(tc, qT, k_words, k_scales, vT, nb, us, off
 
         def gather(e):
             v_g = keep.tile([P, N], BF16, name="v_g%d" % e)
-            nc.vector.tensor_copy(v_g[:], v_win[e][:].indirect(offsets[:]))
+            cut = LAST_ON_VECTOR if e == LAST else N
+            nc.vector.tensor_copy(v_g[:, :cut], v_win[e][:].indirect(offsets[:, :cut // PER_COLUMN]))
+            if cut < N:
+                nc.scalar.activation(v_g[:, cut:], v_win[e][:].indirect(offsets[:, cut // PER_COLUMN:]), ACT.Copy)
             return v_g
 
-        def turn(e, v_g, dst):
+        def turn(e, v_g):
             v_ps = psum.tile([P, 2, P], F32, name="v_ps%d" % e, tag="turn%d" % e)
             for u in range(2):
                 nc.tensor.transpose(v_ps[:, u, :], v_g[:].bitcast(F32)[:, u:N // 2:2], ident[:])
+            return v_ps
+
+        def copy_out(dst, v_ps):
             nc.scalar.copy(dst.bitcast(F32).rearrange("p (e u) -> p e u", u=2), v_ps[:].rearrange("p u e -> p e u"))
 
         def quantise_values(lo, hi, v_bf):
-            first = lo // 2 * E_HALF
-            nc.vector.quantize_mx(out=v_codes[lo // 2][:, lo * P - first:hi * P - first].bitcast(FP8X4),
-                                  scales=v_sc[:, lo * P:hi * P], in_=v_bf)
+            nc.vector.quantize_mx(out=v_codes[lo // 2][:, lo % 2 * P:(hi - lo // 2 * 2) * P].bitcast(FP8X4), scales=v_sc[:, lo * P:hi * P], in_=v_bf)
 
-        def signed(b):
-            if b >= 1:
-                y_bf = placed([P, P, PACK], BF16, "y_bf%d" % b, b * WINDOW_BYTES)
-            else:
-                y_bf = keep.tile([P, P, PACK], BF16, name="y_bf%d" % b, align_bytes=64)
-            nc.vector.tensor_tensor(y_bf[:], y_mag[b][:], signs[:], ALU.mult)
+        def signed(b, y_abs):
+            y_bf = placed([P, P, PACK], BF16, "y_bf%d" % b, b * WINDOW_BYTES)
+            nc.vector.tensor_tensor(y_bf[:], y_abs[:], signs[:], ALU.mult)
             return y_bf
 
         def quantise_y(b, y_bf):
@@ -207,85 +194,100 @@ def tile_attend_mlpb_relu2_srt_kernel(tc, qT, k_words, k_scales, vT, nb, us, off
             nc.vector.quantize_mx(out=y_codes[:, cols].bitcast(FP8X4), scales=y_sc[:, cols],
                                   in_=y_bf[:].rearrange("p q t -> p (q t)"))
 
+        first = [(t, c, scores[t][:, :P] if c == 0 else spare[t][:]) for c in (0, P) for t in range(PACK)]
+        for t, c, dst in first:
+            score_pass(dst, t, 0, c, c + P)
+        for t, c, dst in first[:PACK]:
+            score_pass(dst, t, 1, c, c + P)
+            rectify(relu[0][:, t, c:c + P], dst, t)
+        y_abs0 = square(0)
+        for t, c, dst in first[PACK:]:
+            score_pass(dst, t, 1, c, c + P)
+            rectify(relu[0][:, t, c:c + P], dst, t)
         v_bf01 = keep.tile([P, 2 * N], BF16, name="v_bf01", align_bytes=64)
-        turn(0, gather(0), v_bf01[:, :N])
-        quantise_y(0, signed(0))
-        turn(1, gather(1), v_bf01[:, N:])
-        quantise_y(1, signed(1))
-        y_mag.append(square(3, relu[1]))
-        v_g2 = gather(2)
+        copy_out(v_bf01[:, :N], turn(0, gather(0)))
+        quantise_y(0, signed(0, y_abs0))
+        y_abs1 = square(1)
+        for t in range(PACK):
+            for g in range(PASSES):
+                score_pass(scores[t][:, Q_HALF:], t, g, Q_HALF, NQ)
+            rectify(relu[1][:, t, :], scores[t][:, Q_HALF:], t)
+        copy_out(v_bf01[:, N:], turn(1, gather(1)))
+        quantise_y(1, signed(1, y_abs1))
+        y_abs2 = square(2)
+        y_abs3 = square(3)
         v_bf2 = keep.tile([P, N], BF16, name="v_bf2", align_bytes=64)
-        turn(2, v_g2, v_bf2[:])
-        y_bf2 = signed(2)
-        v_codes = [placed([P, E_HALF], U32, "v_codes0", 2 * WINDOW_BYTES + WINDOW_BYTES // 2)]
+        copy_out(v_bf2[:], turn(2, gather(2)))
+        y_bf2 = signed(2, y_abs2)
+        v_codes = [placed([P, 2 * P], U32, "v_codes0", 2 * WINDOW_BYTES + WINDOW_BYTES // 2)]
         quantise_values(0, 2, v_bf01[:])
         quantise_y(2, y_bf2)
 
-        sums = [psum.tile([P, DV], F32, name="sum%d" % b, tag="acc%d" % b) for b in range(Q_BLOCKS)]
-        squares = keep.tile([P, DV], BF16, name="squares")
-        last = Q_BLOCKS - 1
+        sums = [psum.tile([P, DV], F32, name="sum%d" % b, tag="acc%d" % b) for b in range(BLOCKS)]
+        ends = [psum.tile([P, P], F32, name="end%d" % b, tag="turn%d" % b) for b in range(2)]
+
+        def sums_at(b, lo, hi):
+            return ends[b][:] if b < 2 and lo == 3 * P else sums[b][:, lo:hi]
+
+        squares = keep.tile([P, BLOCKS, DV], BF16, name="squares")
+        cuts = (0, 2 * P, 3 * P, DV)
+        tail = LAST * WINDOW_BYTES
 
         def product(b, lo, hi):
             rows = slice(b * P, (b + 1) * P)
-            half = lo // E_HALF
-            nc.tensor.matmul_mx(out=sums[b][:, lo:hi], lhsT=y_codes[:, rows].bitcast(FP8X4), lhsT_scale=y_sc[:, rows],
-                                rhs=v_codes[half][:, lo - half * E_HALF:hi - half * E_HALF].bitcast(FP8X4),
+            nc.tensor.matmul_mx(out=sums_at(b, lo, hi), lhsT=y_codes[:, rows].bitcast(FP8X4), lhsT_scale=y_sc[:, rows],
+                                rhs=v_codes[lo // (2 * P)][:, lo % (2 * P):hi - lo // (2 * P) * 2 * P].bitcast(FP8X4),
                                 rhs_scale=v_sc[:, lo:hi], start=True, stop=True)
 
-        def sum_squares(b, lo, hi, sum_sq):
-            nc.scalar.activation(squares[:, 0:hi - lo], sums[b][:, lo:hi], ACT.Square, accum_out=sum_sq[:, b:b + 1])
+        def sum_squares(b, lo, hi, offset=None):
+            name = "sum_sq%d_%d" % (b, lo)
+            sum_sq = keep.tile([P, 1], F32, name=name) if offset is None else placed([P, 1], F32, name, offset)
+            nc.scalar.activation(squares[:, b, lo:hi], sums_at(b, lo, hi), ACT.Square, accum_out=sum_sq[:])
+            return sum_sq
 
-        cuts = (0, 2 * P, 3 * P, DV)
-        part_sq = [keep.tile([P, Q_BLOCKS], F32, name="part_sq%d" % i) for i in range(3)]
-        part_ms = [keep.tile([P, last], F32, name="part_ms%d" % i) for i in range(2)]
+        mean_sq = [EPS] * BLOCKS
 
-        def early_sum(i, b):
-            sum_squares(b, cuts[i], cuts[i + 1], part_sq[i])
-            nc.gpsimd.tensor_scalar(part_ms[i][:, b:b + 1], part_sq[i][:, b:b + 1], 1.0 / DV,
-                                    part_ms[0][:, b:b + 1] if i else EPS, ALU.mult, ALU.add)
+        def early_sum(b, lo, hi, offset=None):
+            sum_sq = sum_squares(b, lo, hi, offset)
+            so_far = keep.tile([P, 1], F32, name="mean_sq%d_%d" % (b, lo))
+            nc.gpsimd.tensor_scalar(so_far[:], sum_sq[:], 1.0 / DV, mean_sq[b], ALU.mult, ALU.add)
+            mean_sq[b] = so_far[:]
 
-        for b in range(last):
+        for b in range(LAST):
             product(b, cuts[0], cuts[1])
-            early_sum(0, b)
-        v_g3 = gather(3)
-        v_bf3 = keep.tile([P, N], BF16, name="v_bf3", align_bytes=64)
-        turn(3, v_g3, v_bf3[:])
-        y_bf3 = signed(3)
-        v_codes.append(placed([P, E_HALF], U32, "v_codes1", 3 * WINDOW_BYTES + WINDOW_BYTES // 2))
-        quantise_values(2, 3, v_bf2[:])
-        quantise_y(3, y_bf3)
-        product(0, cuts[1], cuts[2])
-        early_sum(1, 0)
-        product(last, cuts[0], cuts[1])
-        for b in (last, 1, 2):
-            product(b, cuts[1], cuts[2])
-        quantise_values(3, 4, v_bf3[:])
 
-        rstd = keep.tile([P, Q_BLOCKS], F32, name="rstd")
-        for b in (0, last, 1, 2):
+        v_g3 = gather(LAST)
+        for b in range(2):
+            early_sum(b, cuts[0], cuts[1], tail + WINDOW_BYTES // 4 + 64 * b)
+        v_bf3 = keep.tile([P, N], BF16, name="v_bf3", align_bytes=64)
+        copy_out(v_bf3[:], turn(LAST, v_g3))
+        v_codes.append(placed([P, 2 * P], U32, "v_codes1", tail + WINDOW_BYTES // 2))
+        quantise_values(2, 3, v_bf2[:])
+        quantise_y(LAST, signed(LAST, y_abs3))
+        for b in range(2):
+            product(b, cuts[1], cuts[2])
+            early_sum(b, cuts[1], cuts[2])
+        quantise_values(3, 4, v_bf3[:])
+        for b in range(2):
             product(b, cuts[2], DV)
-        stats = keep.tile([P, 6], F32, name="stats")
-        mean_var = keep.tile([P, 2], F32, name="mean_var")
-        last_ms = keep.tile([P, 1], F32, name="last_ms")
-        nc.vector.bn_stats(stats[:], sums[last][:])
-        for b in range(Q_BLOCKS):
-            if b == last:
-                nc.scalar.activation(rstd[:, b:b + 1], last_ms[:], ACT.Abs_reciprocal_sqrt, bias=EPS)
-            else:
-                done = 2 if b == 0 else 1
-                sum_squares(b, cuts[done], DV, part_sq[2])
-                nc.scalar.activation(rstd[:, b:b + 1], part_sq[2][:, b:b + 1], ACT.Abs_reciprocal_sqrt,
-                                     bias=part_ms[done - 1][:, b:b + 1], scale=1.0 / DV)
+        product(2, cuts[1], DV)
+        product(LAST, cuts[0], cuts[1])
+        product(LAST, cuts[1], DV)
+
+        def finish(b, sum_sq):
+            rstd = keep.tile([P, 1], F32, name="rstd%d" % b)
+            nc.scalar.activation(rstd[:], sum_sq[:], ACT.Abs_reciprocal_sqrt, bias=mean_sq[b], scale=1.0 / DV)
             res = keep.tile([P, DV], F32, name="res%d" % b)
-            pieces = 2
-            for i in range(pieces):
-                cols = slice(i * DV // pieces, (i + 1) * DV // pieces)
-                if b == last:
-                    nc.scalar.activation(res[:, cols], sums[b][:, cols], ACT.Copy, scale=rstd[:, b:b + 1])
-                    nc.scalar.dma_start(out[0, b * P:(b + 1) * P, cols], res[:, cols])
-                else:
-                    nc.vector.tensor_scalar(res[:, cols], sums[b][:, cols], rstd[:, b:b + 1], None, ALU.mult)
-                    nc.sync.dma_start(out[0, b * P:(b + 1) * P, cols], res[:, cols])
-            if b == 0:
-                nc.vector.bn_aggr(mean_var[:], stats[:])
-                nc.gpsimd.tensor_scalar(last_ms[:], mean_var[:, 0:1], mean_var[:, 0:1], mean_var[:, 1:2], ALU.mult, ALU.add)
+            for i in range(2):
+                cols = slice(i * DV // 2, (i + 1) * DV // 2)
+                for lo, hi in ((cuts[1], cuts[2]), (cuts[2], DV)) if i and b < 2 else ((cols.start, cols.stop),):
+                    nc.vector.tensor_scalar(res[:, lo:hi], sums_at(b, lo, hi), rstd[:], None, ALU.mult)
+                nc.sync.dma_start(out[0, b * P:(b + 1) * P, cols], res[:, cols])
+
+        last_sq = [sum_squares(b, cuts[2], DV, 64 * b) for b in range(2)]
+        for b in range(2):
+            finish(b, last_sq[b])
+        last_sq = sum_squares(2, 0, DV, 0)
+        early_sum(LAST, cuts[0], cuts[1], 64)
+        finish(2, last_sq)
+        finish(LAST, sum_squares(LAST, cuts[1], DV))

@@ -29,9 +29,10 @@ WINDOW_BYTES = 4 * T
 Q_HALF = NQ // 2
 NB_ROW = P - 1
 KS_ROW = 32
+NB_ZEROED_BY_VECTOR = 768
 TINY = 2.0 ** -100
 PER_COLUMN = 16
-LAST_ON_VECTOR = 288
+ON_VECTOR = (N, N, 352, 288)
 
 
 def interleaved(dst, src):
@@ -52,10 +53,10 @@ def tile_attend_mlpb_relu2_srt_kernel(tc, qT, k_words, k_scales, vT, nb, us, off
         ks_win = keep.tile([P, T], U8, name="ks_win")
         nb_win = keep.tile([P, T], F32, name="nb_win")
         us_sb = keep.tile([P, PACK], F32, name="us_sb")
-        nc.sync.dma_start(nb_win[NB_ROW:P, :], nb[0:1, :])
-        nc.sync.dma_start(us_sb[:], us[0].rearrange("(p j) o -> p (j o)", j=PACK))
         nc.sync.dma_start(ks_win[KS_ROW:KS_ROW + 32, :].bitcast(I32),
                           k_scales.rearrange("g f t -> f g t").bitcast(I32))
+        nc.sync.dma_start(nb_win[NB_ROW:P, :], nb[0:1, :])
+        nc.sync.dma_start(us_sb[:], us[0].rearrange("(p j) o -> p (j o)", j=PACK))
         nc.sync.dma_start(offsets[:], offs)
         q_raw = [keep.tile([P, PACK, NQ], F32, name="q_raw%d" % g) for g in range(PASSES)]
         q_rows = qT[0].rearrange("(g p j) q -> g p j q", g=PASSES, j=PACK)
@@ -66,8 +67,9 @@ def tile_attend_mlpb_relu2_srt_kernel(tc, qT, k_words, k_scales, vT, nb, us, off
         k_sc = keep.tile([P, PASSES, N], U8, name="k_sc", align_bytes=64)
         nc.vector.memset(ks_win[0:KS_ROW, :].bitcast(I32), 0)
         nc.vector.memset(ks_win[KS_ROW + 32:P, :].bitcast(I32), 0)
-        nc.gpsimd.memset(nb_win[0:NB_ROW, :].bitcast(I32), 0)
         nc.vector.memset(k_sc[:].rearrange("p g c -> p (g c)").bitcast(I32), 0)
+        nc.vector.memset(nb_win[0:NB_ROW, :NB_ZEROED_BY_VECTOR].bitcast(I32), 0)
+        nc.gpsimd.memset(nb_win[0:NB_ROW, NB_ZEROED_BY_VECTOR:].bitcast(I32), 0)
         ident = keep.tile([P, P], F32, name="ident")
         make_identity(nc, ident[:])
 
@@ -154,8 +156,9 @@ def tile_attend_mlpb_relu2_srt_kernel(tc, qT, k_words, k_scales, vT, nb, us, off
 
         relu = [keep.tile([P, PACK, Q_HALF], F32, name="relu%d" % h) for h in range(2)]
 
-        def square(b):
-            y_abs = keep.tile([P, P, PACK], BF16, name="y_mag%d" % b)
+        def square(b, offset=None):
+            name = "y_mag%d" % b
+            y_abs = keep.tile([P, P, PACK], BF16, name=name) if offset is None else placed([P, P, PACK], BF16, name, offset)
             dst, src = interleaved(y_abs[:], relu[b // 2][:, :, b % 2 * P:(b % 2 + 1) * P])
             nc.scalar.activation(dst, src, ACT.Square)
             return y_abs
@@ -166,7 +169,7 @@ def tile_attend_mlpb_relu2_srt_kernel(tc, qT, k_words, k_scales, vT, nb, us, off
 
         def gather(e):
             v_g = keep.tile([P, N], BF16, name="v_g%d" % e)
-            cut = LAST_ON_VECTOR if e == LAST else N
+            cut = ON_VECTOR[e]
             nc.vector.tensor_copy(v_g[:, :cut], v_win[e][:].indirect(offsets[:, :cut // PER_COLUMN]))
             if cut < N:
                 nc.scalar.activation(v_g[:, cut:], v_win[e][:].indirect(offsets[:, cut // PER_COLUMN:]), ACT.Copy)
@@ -215,19 +218,21 @@ def tile_attend_mlpb_relu2_srt_kernel(tc, qT, k_words, k_scales, vT, nb, us, off
         copy_out(v_bf01[:, N:], turn(1, gather(1)))
         quantise_y(1, signed(1, y_abs1))
         y_abs2 = square(2)
-        y_abs3 = square(3)
+        v_ps2 = turn(2, gather(2))
+        y_abs3 = square(3, 2 * WINDOW_BYTES + WINDOW_BYTES // 4)
         v_bf2 = keep.tile([P, N], BF16, name="v_bf2", align_bytes=64)
-        copy_out(v_bf2[:], turn(2, gather(2)))
+        copy_out(v_bf2[:], v_ps2)
         y_bf2 = signed(2, y_abs2)
         v_codes = [placed([P, 2 * P], U32, "v_codes0", 2 * WINDOW_BYTES + WINDOW_BYTES // 2)]
         quantise_values(0, 2, v_bf01[:])
         quantise_y(2, y_bf2)
 
         sums = [psum.tile([P, DV], F32, name="sum%d" % b, tag="acc%d" % b) for b in range(BLOCKS)]
-        ends = [psum.tile([P, P], F32, name="end%d" % b, tag="turn%d" % b) for b in range(2)]
+        ends = {b: psum.tile([P, P], F32, name="end%d" % b, tag="turn%d" % b) for b in range(2)}
+        ends[LAST] = psum.tile([P, 2 * P], F32, name="end3", tag="turn2")
 
         def sums_at(b, lo, hi):
-            return ends[b][:] if b < 2 and lo == 3 * P else sums[b][:, lo:hi]
+            return ends[b][:] if b in ends and hi == DV else sums[b][:, lo:hi]
 
         squares = keep.tile([P, BLOCKS, DV], BF16, name="squares")
         cuts = (0, 2 * P, 3 * P, DV)
@@ -247,9 +252,10 @@ def tile_attend_mlpb_relu2_srt_kernel(tc, qT, k_words, k_scales, vT, nb, us, off
 
         mean_sq = [EPS] * BLOCKS
 
-        def early_sum(b, lo, hi, offset=None):
+        def early_sum(b, lo, hi, offset=None, mean_offset=None):
             sum_sq = sum_squares(b, lo, hi, offset)
-            so_far = keep.tile([P, 1], F32, name="mean_sq%d_%d" % (b, lo))
+            name = "mean_sq%d_%d" % (b, lo)
+            so_far = keep.tile([P, 1], F32, name=name) if mean_offset is None else placed([P, 1], F32, name, mean_offset)
             nc.gpsimd.tensor_scalar(so_far[:], sum_sq[:], 1.0 / DV, mean_sq[b], ALU.mult, ALU.add)
             mean_sq[b] = so_far[:]
 
@@ -266,7 +272,7 @@ def tile_attend_mlpb_relu2_srt_kernel(tc, qT, k_words, k_scales, vT, nb, us, off
         quantise_y(LAST, signed(LAST, y_abs3))
         for b in range(2):
             product(b, cuts[1], cuts[2])
-            early_sum(b, cuts[1], cuts[2])
+            early_sum(b, cuts[1], cuts[2], None, 128 + 64 * b)
         quantise_values(3, 4, v_bf3[:])
         for b in range(2):
             product(b, cuts[2], DV)
@@ -281,7 +287,10 @@ def tile_attend_mlpb_relu2_srt_kernel(tc, qT, k_words, k_scales, vT, nb, us, off
             for i in range(2):
                 cols = slice(i * DV // 2, (i + 1) * DV // 2)
                 for lo, hi in ((cuts[1], cuts[2]), (cuts[2], DV)) if i and b < 2 else ((cols.start, cols.stop),):
-                    nc.vector.tensor_scalar(res[:, lo:hi], sums_at(b, lo, hi), rstd[:], None, ALU.mult)
+                    if i and b == LAST:
+                        nc.scalar.activation(res[:, lo:hi], sums_at(b, lo, hi), ACT.Copy, scale=rstd[:])
+                    else:
+                        nc.vector.tensor_scalar(res[:, lo:hi], sums_at(b, lo, hi), rstd[:], None, ALU.mult)
                 nc.sync.dma_start(out[0, b * P:(b + 1) * P, cols], res[:, cols])
 
         last_sq = [sum_squares(b, cuts[2], DV, 64 * b) for b in range(2)]
@@ -290,4 +299,4 @@ def tile_attend_mlpb_relu2_srt_kernel(tc, qT, k_words, k_scales, vT, nb, us, off
         last_sq = sum_squares(2, 0, DV, 0)
         early_sum(LAST, cuts[0], cuts[1], 64)
         finish(2, last_sq)
-        finish(LAST, sum_squares(LAST, cuts[1], DV))
+        finish(LAST, sum_squares(LAST, cuts[1], DV, 128 + 64))

@@ -227,21 +227,26 @@ def tile_attend_mlpb_relu2_srt_kernel(tc, qT, k_words, k_scales, vT, nb, us, off
         quantise_values(0, 2, v_bf01[:])
         quantise_y(2, y_bf2)
 
+        half = DV // 2
+        cuts = (0, half, 3 * P, DV)
+        tail = LAST * WINDOW_BYTES
         sums = [psum.tile([P, DV], F32, name="sum%d" % b, tag="acc%d" % b) for b in range(BLOCKS)]
-        ends = {b: psum.tile([P, P], F32, name="end%d" % b, tag="turn%d" % b) for b in range(2)}
-        ends[LAST] = psum.tile([P, 2 * P], F32, name="end3", tag="turn2")
+        apart = {}
 
         def sums_at(b, lo, hi):
-            return ends[b][:] if b in ends and hi == DV else sums[b][:, lo:hi]
+            if b in apart and lo >= DV - apart[b].shape[1]:
+                first_apart = DV - apart[b].shape[1]
+                return apart[b][:, lo - first_apart:hi - first_apart]
+            return sums[b][:, lo:hi]
 
         squares = keep.tile([P, BLOCKS, DV], BF16, name="squares")
-        cuts = (0, 2 * P, 3 * P, DV)
-        tail = LAST * WINDOW_BYTES
 
-        def product(b, lo, hi):
+        def product(b, lo, hi, bank=None):
+            if bank is not None:
+                apart[b] = psum.tile([P, DV - lo], F32, name="apart%d" % b, tag="turn%d" % bank)
             rows = slice(b * P, (b + 1) * P)
             nc.tensor.matmul_mx(out=sums_at(b, lo, hi), lhsT=y_codes[:, rows].bitcast(FP8X4), lhsT_scale=y_sc[:, rows],
-                                rhs=v_codes[lo // (2 * P)][:, lo % (2 * P):hi - lo // (2 * P) * 2 * P].bitcast(FP8X4),
+                                rhs=v_codes[lo // half][:, lo % half:hi - lo // half * half].bitcast(FP8X4),
                                 rhs_scale=v_sc[:, lo:hi], start=True, stop=True)
 
         def sum_squares(b, lo, hi, offset=None):
@@ -265,38 +270,70 @@ def tile_attend_mlpb_relu2_srt_kernel(tc, qT, k_words, k_scales, vT, nb, us, off
         v_g3 = gather(LAST)
         for b in range(2):
             early_sum(b, cuts[0], cuts[1], tail + WINDOW_BYTES // 4 + 64 * b)
-        v_bf3 = keep.tile([P, N], BF16, name="v_bf3", align_bytes=64)
+        v_bf3 = placed([P, N], BF16, "v_bf3", 3 * WINDOW_BYTES // 4)
         copy_out(v_bf3[:], turn(LAST, v_g3))
-        v_codes.append(placed([P, 2 * P], U32, "v_codes1", tail + WINDOW_BYTES // 2))
+        v_codes.append(placed([P, half], U32, "v_codes1", tail + WINDOW_BYTES // 2))
         quantise_values(2, 3, v_bf2[:])
         quantise_y(LAST, signed(LAST, y_abs3))
         for b in range(2):
             product(b, cuts[1], cuts[2])
-            early_sum(b, cuts[1], cuts[2], None, 128 + 64 * b)
+            early_sum(b, cuts[1], cuts[2])
+        product(2, cuts[1], cuts[2])
         quantise_values(3, 4, v_bf3[:])
-        for b in range(2):
-            product(b, cuts[2], DV)
-        product(2, cuts[1], DV)
-        product(LAST, cuts[0], cuts[1])
-        product(LAST, cuts[1], DV)
+        product(0, cuts[2], DV, 0)
+        product(LAST, 0, half)
+        for b in (2, 1):
+            product(b, cuts[2], DV, b)
+        product(LAST, half, DV)
 
-        def finish(b, sum_sq):
-            rstd = keep.tile([P, 1], F32, name="rstd%d" % b)
+        def statistics(b, width, offset):
+            stats = placed([P, 6], F32, "stats%d" % b, offset)
+            nc.vector.bn_stats(stats[:], sums[b][:, :width])
+            return stats
+
+        def mean_from(b, width, stats, offset):
+            mean_var = placed([P, 2], F32, "mean_var%d" % b, offset)
+            part_ms = keep.tile([P, 2], F32, name="part_ms%d" % b)
+            nc.vector.bn_aggr(mean_var[:], stats[:])
+            nc.gpsimd.tensor_scalar(part_ms[:, 0:1], mean_var[:, 0:1], mean_var[:, 0:1], mean_var[:, 1:2], ALU.mult, ALU.add)
+            nc.gpsimd.tensor_scalar(part_ms[:, 1:2], part_ms[:, 0:1], width / DV, EPS, ALU.mult, ALU.add)
+            mean_sq[b] = part_ms[:, 1:2]
+
+        stats2 = statistics(2, cuts[2], 3 * WINDOW_BYTES // 4)
+        mean_from(2, cuts[2], stats2, 256)
+
+        def inverse_root(b, sum_sq):
+            rstd = placed([P, 1], F32, "rstd%d" % b, 512 + 64 * b)
             nc.scalar.activation(rstd[:], sum_sq[:], ACT.Abs_reciprocal_sqrt, bias=mean_sq[b], scale=1.0 / DV)
-            res = keep.tile([P, DV], F32, name="res%d" % b)
-            for i in range(2):
-                cols = slice(i * DV // 2, (i + 1) * DV // 2)
-                for lo, hi in ((cuts[1], cuts[2]), (cuts[2], DV)) if i and b < 2 else ((cols.start, cols.stop),):
-                    if i and b == LAST:
-                        nc.scalar.activation(res[:, lo:hi], sums_at(b, lo, hi), ACT.Copy, scale=rstd[:])
-                    else:
-                        nc.vector.tensor_scalar(res[:, lo:hi], sums_at(b, lo, hi), rstd[:], None, ALU.mult)
-                nc.sync.dma_start(out[0, b * P:(b + 1) * P, cols], res[:, cols])
+            return rstd
 
-        last_sq = [sum_squares(b, cuts[2], DV, 64 * b) for b in range(2)]
-        for b in range(2):
-            finish(b, last_sq[b])
-        last_sq = sum_squares(2, 0, DV, 0)
-        early_sum(LAST, cuts[0], cuts[1], 64)
-        finish(2, last_sq)
-        finish(LAST, sum_squares(LAST, cuts[1], DV, 128 + 64))
+        res = [keep.tile([P, DV], F32, name="res%d" % b) for b in range(BLOCKS)]
+
+        def scale_on_vector(b, rstd, lo, hi):
+            nc.vector.tensor_scalar(res[b][:, lo:hi], sums_at(b, lo, hi), rstd[:], None, ALU.mult)
+
+        def scale_on_scalar(b, rstd, lo, hi):
+            nc.scalar.activation(res[b][:, lo:hi], sums_at(b, lo, hi), ACT.Copy, scale=rstd[:])
+
+        def store(b, lo, hi):
+            nc.sync.dma_start(out[0, b * P:(b + 1) * P, lo:hi], res[b][:, lo:hi])
+
+        def finish(b, rstd):
+            (scale_on_scalar if b == LAST else scale_on_vector)(b, rstd, 0, half)
+            store(b, 0, half)
+            if b == LAST:
+                scale_on_scalar(b, rstd, half, DV)
+            else:
+                scale_on_vector(b, rstd, half, cuts[2])
+                (scale_on_scalar if b == 2 else scale_on_vector)(b, rstd, cuts[2], DV)
+            store(b, half, DV)
+
+        rstd0 = inverse_root(0, sum_squares(0, cuts[2], DV, 0))
+        finish(0, rstd0)
+        sum_sq1 = sum_squares(1, cuts[2], DV, 64)
+        sum_sq2 = sum_squares(2, cuts[2], DV, 0)
+        finish(1, inverse_root(1, sum_sq1))
+        rstd2 = inverse_root(2, sum_sq2)
+        sum_sq3 = sum_squares(LAST, 0, DV, 64)
+        finish(2, rstd2)
+        finish(LAST, inverse_root(LAST, sum_sq3))

@@ -264,8 +264,11 @@ def tile_attend_mlpb_relu2_srt_kernel(tc, qT, k_words, k_scales, vT, nb, us, off
             nc.gpsimd.tensor_scalar(so_far[:], sum_sq[:], 1.0 / DV, mean_sq[b], ALU.mult, ALU.add)
             mean_sq[b] = so_far[:]
 
-        for b in range(LAST):
+        for b in range(2):
             product(b, cuts[0], cuts[1])
+        nc.tensor.matmul_mx(out=sums[LAST][:, :half], lhsT=y_codes[:, :P].bitcast(FP8X4), lhsT_scale=y_sc[:, :P],
+                            rhs=v_codes[0][:].bitcast(FP8X4), rhs_scale=v_sc[:, :half], start=True, stop=True)
+        product(2, cuts[0], cuts[1])
 
         v_g3 = gather(LAST)
         for b in range(2):

@@ -176,7 +176,7 @@ def tile_attend_mlpb_relu2_srt_kernel(tc, qT, k_words, k_scales, vT, nb, us, off
             return v_g
 
         def turn(e, v_g):
-            v_ps = psum.tile([P, 2, P], F32, name="v_ps%d" % e, tag="turn%d" % e)
+            v_ps = psum.tile([P, 2, P], F32, name="v_ps%d" % e, tag="turn%d" % (LAST - e))
             for u in range(2):
                 nc.tensor.transpose(v_ps[:, u, :], v_g[:].bitcast(F32)[:, u:N // 2:2], ident[:])
             return v_ps
@@ -208,13 +208,14 @@ def tile_attend_mlpb_relu2_srt_kernel(tc, qT, k_words, k_scales, vT, nb, us, off
             score_pass(dst, t, 1, c, c + P)
             rectify(relu[0][:, t, c:c + P], dst, t)
         v_bf01 = keep.tile([P, 2 * N], BF16, name="v_bf01", align_bytes=64)
-        copy_out(v_bf01[:, :N], turn(0, gather(0)))
+        v_g0 = gather(0)
         quantise_y(0, signed(0, y_abs0))
         y_abs1 = square(1)
         for t in range(PACK):
             for g in range(PASSES):
                 score_pass(scores[t][:, Q_HALF:], t, g, Q_HALF, NQ)
             rectify(relu[1][:, t, :], scores[t][:, Q_HALF:], t)
+        copy_out(v_bf01[:, :N], turn(0, v_g0))
         copy_out(v_bf01[:, N:], turn(1, gather(1)))
         quantise_y(1, signed(1, y_abs1))
         y_abs2 = square(2)
@@ -243,7 +244,7 @@ def tile_attend_mlpb_relu2_srt_kernel(tc, qT, k_words, k_scales, vT, nb, us, off
 
         def product(b, lo, hi, bank=None):
             if bank is not None:
-                apart[b] = psum.tile([P, DV - lo], F32, name="apart%d" % b, tag="turn%d" % bank)
+                apart[b] = psum.tile([P, DV - lo], F32, name="apart%d" % b, tag="turn%d" % (LAST - bank))
             rows = slice(b * P, (b + 1) * P)
             nc.tensor.matmul_mx(out=sums_at(b, lo, hi), lhsT=y_codes[:, rows].bitcast(FP8X4), lhsT_scale=y_sc[:, rows],
                                 rhs=v_codes[lo // half][:, lo % half:hi - lo // half * half].bitcast(FP8X4),

@@ -32,7 +32,7 @@ KS_ROW = 32
 NB_ZEROED_BY_VECTOR = 768
 TINY = 2.0 ** -100
 PER_COLUMN = 16
-ON_VECTOR = (N, N, 352, 288)
+ON_VECTOR = (N, N, 288, 288)
 
 
 def interleaved(dst, src):
@@ -216,17 +216,16 @@ def tile_attend_mlpb_relu2_srt_kernel(tc, qT, k_words, k_scales, vT, nb, us, off
                 score_pass(scores[t][:, Q_HALF:], t, g, Q_HALF, NQ)
             rectify(relu[1][:, t, :], scores[t][:, Q_HALF:], t)
         copy_out(v_bf01[:, :N], turn(0, v_g0))
+        y_abs2 = square(2)
         copy_out(v_bf01[:, N:], turn(1, gather(1)))
         quantise_y(1, signed(1, y_abs1))
-        y_abs2 = square(2)
         v_ps2 = turn(2, gather(2))
         y_abs3 = square(3, 2 * WINDOW_BYTES + WINDOW_BYTES // 4)
         v_bf2 = keep.tile([P, N], BF16, name="v_bf2", align_bytes=64)
         copy_out(v_bf2[:], v_ps2)
-        y_bf2 = signed(2, y_abs2)
         v_codes = [placed([P, 2 * P], U32, "v_codes0", 2 * WINDOW_BYTES + WINDOW_BYTES // 2)]
         quantise_values(0, 2, v_bf01[:])
-        quantise_y(2, y_bf2)
+        quantise_y(2, signed(2, y_abs2))
 
         half = DV // 2
         cuts = (0, half, 3 * P, DV)

from contextlib import ExitStack

import concourse.mybir as mybir
from concourse.masks import make_identity

N, T, D, NQ, DV = 512, 2048, 1024, 512, 512
EPS = 1e-05
FLOPS = 2 * N * D * NQ + 2 * N * NQ * DV
BYTES = 4 * D * NQ + 4 * 128 * T + 32 * T + 4 * DV * T + 4 * T + 4 * N + 2 * 128 * (N // 16) + 4 * NQ * DV

F32 = mybir.dt.float32
BF16 = mybir.dt.bfloat16
I32 = mybir.dt.int32
U32 = mybir.dt.uint32
U16 = mybir.dt.uint16
U8 = mybir.dt.uint8
FP8X4 = mybir.dt.float8_e4m3fn_x4
FP4X4 = mybir.dt.float4_e2m1fn_x4
ACT = mybir.ActivationFunctionType
ALU = mybir.AluOpType

P = 128
PACK = 4
PASSES = D // (P * PACK)
QUADRANTS = 4
BLOCKS = 4
LAST = BLOCKS - 1
WINDOW_BYTES = 4 * T
Q_HALF = NQ // 2
NB_ROW = P - 1
KS_ROW = 32
NB_ZEROED_BY_VECTOR = 768
TINY = 2.0 ** -100
PER_COLUMN = 16
ON_VECTOR = (N, N, 288, 288)


def interleaved(dst, src):
    return dst.rearrange("p (c i) t -> p c t i", i=4), src.rearrange("p t (c i) -> p c t i", i=4)


def tile_attend_mlpb_relu2_srt_kernel(tc, qT, k_words, k_scales, vT, nb, us, offs, out):
    nc = tc.nc
    with ExitStack() as ctx:
        keep = ctx.enter_context(tc.tile_pool(name="keep", bufs=1))
        turns = ctx.enter_context(tc.tile_pool(name="turns", bufs=1))
        psum = ctx.enter_context(tc.psum_pool(name="psum", bufs=1))

        def placed(shape, dtype, name, offset):
            return turns.tile(shape, dtype, name=name, offset=offset, align_bytes=64)

        offsets = keep.tile([P, N // PER_COLUMN], U16, name="offsets")
        ks_win = keep.tile([P, T], U8, name="ks_win")
        nb_win = keep.tile([P, T], F32, name="nb_win")
        us_sb = keep.tile([P, PACK], F32, name="us_sb")
        nc.sync.dma_start(ks_win[KS_ROW:KS_ROW + 32, :].bitcast(I32),
                          k_scales.rearrange("g f t -> f g t").bitcast(I32))
        nc.sync.dma_start(nb_win[NB_ROW:P, :], nb[0:1, :])
        nc.sync.dma_start(us_sb[:], us[0].rearrange("(p j) o -> p (j o)", j=PACK))
        nc.sync.dma_start(offsets[:], offs)
        q_raw = [keep.tile([P, PACK, NQ], F32, name="q_raw%d" % g) for g in range(PASSES)]
        q_rows = qT[0].rearrange("(g p j) q -> g p j q", g=PASSES, j=PACK)
        nc.sync.dma_start(q_raw[0][:], q_rows[0])
        kw_win = keep.tile([P, T], I32, name="kw_win")
        nc.sync.dma_start(kw_win[:], k_words[0].rearrange("p t b -> p (t b)").bitcast(I32))

        k_sc = keep.tile([P, PASSES, N], U8, name="k_sc", align_bytes=64)
        nc.vector.memset(ks_win[0:KS_ROW, :].bitcast(I32), 0)
        nc.vector.memset(ks_win[KS_ROW + 32:P, :].bitcast(I32), 0)
        nc.vector.memset(k_sc[:].rearrange("p g c -> p (g c)").bitcast(I32), 0)
        nc.vector.memset(nb_win[0:NB_ROW, :NB_ZEROED_BY_VECTOR].bitcast(I32), 0)
        nc.gpsimd.memset(nb_win[0:NB_ROW, NB_ZEROED_BY_VECTOR:].bitcast(I32), 0)
        ident = keep.tile([P, P], F32, name="ident")
        make_identity(nc, ident[:])

        ks_g = keep.tile([P, PACK, P], U8, name="ks_g")
        nc.vector.tensor_copy(ks_g[:].rearrange("p t m -> p m t"), ks_win[:].indirect(offsets[:]))
        for quad in range(QUADRANTS):
            row = KS_ROW + 8 * quad
            nc.sync.dma_start(k_sc[32 * quad:32 * quad + 4].rearrange("p g c -> p (g c)").bitcast(I32),
                              ks_g[row:row + 8].rearrange("p t m -> p (t m)").bitcast(I32))

        nc.sync.dma_start(q_raw[1][:], q_rows[1])
        v_win = [placed([P, T], F32, "v_win%d" % e, e * WINDOW_BYTES) for e in range(BLOCKS)]
        for e in range(BLOCKS):
            nc.sync.dma_start(v_win[e][:], vT[e * P:(e + 1) * P, :])

        inv_root = keep.tile([P, PACK], F32, name="inv_root")
        mag = keep.tile([P, PACK], F32, name="mag")
        signs = keep.tile([P, P, PACK], BF16, name="signs")
        nc.vector.scalar_tensor_tensor(mag[:], us_sb[:], -1.0, us_sb[:], ALU.mult, ALU.max)
        positive = keep.tile([P, PACK], F32, name="positive")
        nc.vector.tensor_scalar(positive[:], us_sb[:], 0.0, None, ALU.is_ge)
        nc.scalar.activation(inv_root[:], mag[:], ACT.Abs_reciprocal_sqrt, bias=TINY)
        rough = keep.tile([P, PACK], F32, name="rough")
        step = keep.tile([P, PACK], F32, name="step")
        root = keep.tile([P, PACK], F32, name="root")
        nc.gpsimd.tensor_tensor(rough[:], mag[:], inv_root[:], ALU.mult)
        nc.gpsimd.tensor_tensor(step[:], rough[:], rough[:], ALU.mult)
        nc.gpsimd.tensor_tensor(step[:], mag[:], step[:], ALU.subtract)
        nc.gpsimd.tensor_tensor(step[:], step[:], inv_root[:], ALU.mult)
        nc.gpsimd.tensor_scalar(step[:], step[:], 0.5, 0.0, ALU.mult, ALU.add)
        nc.gpsimd.tensor_tensor(root[:], rough[:], step[:], ALU.add)

        nb_g = keep.tile([P, N], F32, name="nb_g")
        nc.vector.tensor_copy(nb_g[:], nb_win[:].indirect(offsets[:]))
        nb_ps = psum.tile([P, PACK, P], F32, name="nb_ps", tag="turn3")
        for t in range(PACK):
            nc.tensor.transpose(nb_ps[:, t, :], nb_g[:, t:N:PACK], ident[:])
        bias = keep.tile([P, PACK], F32, name="bias")
        for t in range(PACK):
            nc.scalar.activation(bias[:, t:t + 1], nb_ps[:, t, NB_ROW:P], ACT.Copy, scale=root[:, t:t + 1])
        nc.scalar.activation(signs[:], positive[:].unsqueeze(1).to_broadcast([P, P, PACK]), ACT.Copy, bias=-1.0, scale=2.0)

        q_bf = [keep.tile([P, NQ * PACK], BF16, name="q_bf%d" % g, align_bytes=64) for g in range(PASSES)]
        q_codes = [keep.tile([P, NQ], U32, name="q_codes%d" % g, align_bytes=64) for g in range(PASSES)]
        q_sc = [keep.tile([P, NQ], U8, name="q_sc%d" % g, align_bytes=64) for g in range(PASSES)]

        def cast_queries(copy, g, lo, hi):
            dst = q_bf[g][:, lo * PACK:hi * PACK].rearrange("p (c t) -> p c t", t=PACK)
            copy(*interleaved(dst, q_raw[g][:, :, lo:hi]))

        def quantise_queries(g, lo, hi):
            nc.vector.quantize_mx(out=q_codes[g][:, lo:hi].bitcast(FP8X4), scales=q_sc[g][:, lo:hi],
                                  in_=q_bf[g][:, lo * PACK:hi * PACK])

        cast_queries(nc.scalar.copy, 0, 0, Q_HALF)
        cast_queries(nc.vector.tensor_copy, 0, Q_HALF, NQ)
        quantise_queries(0, 0, Q_HALF)
        quantise_queries(0, Q_HALF, NQ)

        kw_g = keep.tile([P, PACK, P], U32, name="kw_g")
        nc.vector.tensor_copy(kw_g[:].rearrange("p t m -> p m t"), kw_win[:].bitcast(U32).indirect(offsets[:]))
        k_codes = [keep.tile([P, N], U16, name="k_codes%d" % g, align_bytes=64) for g in range(PASSES)]
        halves = kw_g[:].rearrange("p t m -> p (t m)").bitcast(U16).rearrange("p (c g) -> p g c", g=2)
        for g in range(PASSES):
            nc.vector.tensor_copy(k_codes[g][:], halves[:, g, :])

        for b in range(BLOCKS):
            cast_queries(nc.scalar.copy if b % 2 else nc.vector.tensor_copy, 1, b * P, (b + 1) * P)
        quantise_queries(1, 0, P)
        quantise_queries(1, P, Q_HALF)
        quantise_queries(1, Q_HALF, NQ)

        scores = [psum.tile([P, NQ], F32, name="score%d" % t, tag="acc%d" % t) for t in range(PACK)]
        spare = [psum.tile([P, P], F32, name="spare%d" % t, tag="turn%d" % t) for t in range(PACK)]

        def score_pass(dst, t, g, lo, hi):
            nc.tensor.matmul_mx(out=dst, lhsT=k_codes[g][:, t * P:(t + 1) * P].bitcast(FP4X4),
                                lhsT_scale=k_sc[:, g, t * P:(t + 1) * P],
                                rhs=q_codes[g][:, lo:hi].bitcast(FP8X4), rhs_scale=q_sc[g][:, lo:hi],
                                start=(g == 0), stop=(g == PASSES - 1))

        def rectify(dst, src, t):
            nc.scalar.activation(dst, src, ACT.Relu, bias=bias[:, t:t + 1], scale=root[:, t:t + 1])

        relu = [keep.tile([P, PACK, Q_HALF], F32, name="relu%d" % h) for h in range(2)]

        def square(b, offset=None):
            name = "y_mag%d" % b
            y_abs = keep.tile([P, P, PACK], BF16, name=name) if offset is None else placed([P, P, PACK], BF16, name, offset)
            dst, src = interleaved(y_abs[:], relu[b // 2][:, :, b % 2 * P:(b % 2 + 1) * P])
            nc.scalar.activation(dst, src, ACT.Square)
            return y_abs

        v_sc = keep.tile([P, DV], U8, name="v_sc", align_bytes=64)
        y_sc = keep.tile([P, NQ], U8, name="y_sc", align_bytes=64)
        y_codes = keep.tile([P, NQ], U32, name="y_codes", align_bytes=64)

        def gather(e):
            v_g = keep.tile([P, N], BF16, name="v_g%d" % e)
            cut = ON_VECTOR[e]
            nc.vector.tensor_copy(v_g[:, :cut], v_win[e][:].indirect(offsets[:, :cut // PER_COLUMN]))
            if cut < N:
                nc.scalar.activation(v_g[:, cut:], v_win[e][:].indirect(offsets[:, cut // PER_COLUMN:]), ACT.Copy)
            return v_g

        def turn(e, v_g):
            v_ps = psum.tile([P, 2, P], F32, name="v_ps%d" % e, tag="turn%d" % (LAST - e))
            for u in range(2):
                nc.tensor.transpose(v_ps[:, u, :], v_g[:].bitcast(F32)[:, u:N // 2:2], ident[:])
            return v_ps

        def copy_out(dst, v_ps):
            nc.scalar.copy(dst.bitcast(F32).rearrange("p (e u) -> p e u", u=2), v_ps[:].rearrange("p u e -> p e u"))

        def quantise_values(lo, hi, v_bf):
            nc.vector.quantize_mx(out=v_codes[lo // 2][:, lo % 2 * P:(hi - lo // 2 * 2) * P].bitcast(FP8X4), scales=v_sc[:, lo * P:hi * P], in_=v_bf)

        def signed(b, y_abs):
            y_bf = placed([P, P, PACK], BF16, "y_bf%d" % b, b * WINDOW_BYTES)
            nc.vector.tensor_tensor(y_bf[:], y_abs[:], signs[:], ALU.mult)
            return y_bf

        def quantise_y(b, y_bf):
            cols = slice(b * P, (b + 1) * P)
            nc.vector.quantize_mx(out=y_codes[:, cols].bitcast(FP8X4), scales=y_sc[:, cols],
                                  in_=y_bf[:].rearrange("p q t -> p (q t)"))

        first = [(t, c, scores[t][:, :P] if c == 0 else spare[t][:]) for c in (0, P) for t in range(PACK)]
        for t, c, dst in first:
            score_pass(dst, t, 0, c, c + P)
        for t, c, dst in first[:PACK]:
            score_pass(dst, t, 1, c, c + P)
            rectify(relu[0][:, t, c:c + P], dst, t)
        y_abs0 = square(0)
        for t, c, dst in first[PACK:]:
            score_pass(dst, t, 1, c, c + P)
            rectify(relu[0][:, t, c:c + P], dst, t)
        v_bf01 = keep.tile([P, 2 * N], BF16, name="v_bf01", align_bytes=64)
        v_g0 = gather(0)
        quantise_y(0, signed(0, y_abs0))
        y_abs1 = square(1)
        for t in range(PACK):
            for g in range(PASSES):
                score_pass(scores[t][:, Q_HALF:], t, g, Q_HALF, NQ)
            rectify(relu[1][:, t, :], scores[t][:, Q_HALF:], t)
        copy_out(v_bf01[:, :N], turn(0, v_g0))
        y_abs2 = square(2)
        copy_out(v_bf01[:, N:], turn(1, gather(1)))
        quantise_y(1, signed(1, y_abs1))
        v_ps2 = turn(2, gather(2))
        y_abs3 = square(3, 2 * WINDOW_BYTES + WINDOW_BYTES // 4)
        v_bf2 = keep.tile([P, N], BF16, name="v_bf2", align_bytes=64)
        copy_out(v_bf2[:], v_ps2)
        v_codes = [placed([P, 2 * P], U32, "v_codes0", 2 * WINDOW_BYTES + WINDOW_BYTES // 2)]
        quantise_values(0, 2, v_bf01[:])
        quantise_y(2, signed(2, y_abs2))

        half = DV // 2
        cuts = (0, half, 3 * P, DV)
        tail = LAST * WINDOW_BYTES
        sums = [psum.tile([P, DV], F32, name="sum%d" % b, tag="acc%d" % b) for b in range(BLOCKS)]
        apart = {}

        def sums_at(b, lo, hi):
            if b in apart and lo >= DV - apart[b].shape[1]:
                first_apart = DV - apart[b].shape[1]
                return apart[b][:, lo - first_apart:hi - first_apart]
            return sums[b][:, lo:hi]

        squares = keep.tile([P, BLOCKS, DV], BF16, name="squares")

        def product(b, lo, hi, bank=None):
            if bank is not None:
                apart[b] = psum.tile([P, DV - lo], F32, name="apart%d" % b, tag="turn%d" % (LAST - bank))
            rows = slice(b * P, (b + 1) * P)
            nc.tensor.matmul_mx(out=sums_at(b, lo, hi), lhsT=y_codes[:, rows].bitcast(FP8X4), lhsT_scale=y_sc[:, rows],
                                rhs=v_codes[lo // half][:, lo % half:hi - lo // half * half].bitcast(FP8X4),
                                rhs_scale=v_sc[:, lo:hi], start=True, stop=True)

        def sum_squares(b, lo, hi, offset=None):
            name = "sum_sq%d_%d" % (b, lo)
            sum_sq = keep.tile([P, 1], F32, name=name) if offset is None else placed([P, 1], F32, name, offset)
            nc.scalar.activation(squares[:, b, lo:hi], sums_at(b, lo, hi), ACT.Square, accum_out=sum_sq[:])
            return sum_sq

        mean_sq = [EPS] * BLOCKS

        def early_sum(b, lo, hi, offset=None, mean_offset=None):
            sum_sq = sum_squares(b, lo, hi, offset)
            name = "mean_sq%d_%d" % (b, lo)
            so_far = keep.tile([P, 1], F32, name=name) if mean_offset is None else placed([P, 1], F32, name, mean_offset)
            nc.gpsimd.tensor_scalar(so_far[:], sum_sq[:], 1.0 / DV, mean_sq[b], ALU.mult, ALU.add)
            mean_sq[b] = so_far[:]

        for b in range(2):
            product(b, cuts[0], cuts[1])
        nc.tensor.matmul_mx(out=sums[LAST][:, :half], lhsT=y_codes[:, :P].bitcast(FP8X4), lhsT_scale=y_sc[:, :P],
                            rhs=v_codes[0][:].bitcast(FP8X4), rhs_scale=v_sc[:, :half], start=True, stop=True)
        product(2, cuts[0], cuts[1])

        v_g3 = gather(LAST)
        for b in range(2):
            early_sum(b, cuts[0], cuts[1], tail + WINDOW_BYTES // 4 + 64 * b)
        v_bf3 = placed([P, N], BF16, "v_bf3", 3 * WINDOW_BYTES // 4)
        copy_out(v_bf3[:], turn(LAST, v_g3))
        v_codes.append(placed([P, half], U32, "v_codes1", tail + WINDOW_BYTES // 2))
        quantise_values(2, 3, v_bf2[:])
        quantise_y(LAST, signed(LAST, y_abs3))
        for b in range(2):
            product(b, cuts[1], cuts[2])
            early_sum(b, cuts[1], cuts[2])
        product(2, cuts[1], cuts[2])
        quantise_values(3, 4, v_bf3[:])
        product(0, cuts[2], DV, 0)
        product(LAST, 0, half)
        for b in (2, 1):
            product(b, cuts[2], DV, b)
        product(LAST, half, DV)

        def statistics(b, width, offset):
            stats = placed([P, 6], F32, "stats%d" % b, offset)
            nc.vector.bn_stats(stats[:], sums[b][:, :width])
            return stats

        def mean_from(b, width, stats, offset):
            mean_var = placed([P, 2], F32, "mean_var%d" % b, offset)
            part_ms = keep.tile([P, 2], F32, name="part_ms%d" % b)
            nc.vector.bn_aggr(mean_var[:], stats[:])
            nc.gpsimd.tensor_scalar(part_ms[:, 0:1], mean_var[:, 0:1], mean_var[:, 0:1], mean_var[:, 1:2], ALU.mult, ALU.add)
            nc.gpsimd.tensor_scalar(part_ms[:, 1:2], part_ms[:, 0:1], width / DV, EPS, ALU.mult, ALU.add)
            mean_sq[b] = part_ms[:, 1:2]

        stats2 = statistics(2, cuts[2], 3 * WINDOW_BYTES // 4)
        mean_from(2, cuts[2], stats2, 256)

        def inverse_root(b, sum_sq):
            rstd = placed([P, 1], F32, "rstd%d" % b, 512 + 64 * b)
            nc.scalar.activation(rstd[:], sum_sq[:], ACT.Abs_reciprocal_sqrt, bias=mean_sq[b], scale=1.0 / DV)
            return rstd

        res = [keep.tile([P, DV], F32, name="res%d" % b) for b in range(BLOCKS)]

        def scale_on_vector(b, rstd, lo, hi):
            nc.vector.tensor_scalar(res[b][:, lo:hi], sums_at(b, lo, hi), rstd[:], None, ALU.mult)

        def scale_on_scalar(b, rstd, lo, hi):
            nc.scalar.activation(res[b][:, lo:hi], sums_at(b, lo, hi), ACT.Copy, scale=rstd[:])

        def store(b, lo, hi):
            nc.sync.dma_start(out[0, b * P:(b + 1) * P, lo:hi], res[b][:, lo:hi])

        def finish(b, rstd):
            (scale_on_scalar if b == LAST else scale_on_vector)(b, rstd, 0, half)
            store(b, 0, half)
            if b == LAST:
                scale_on_scalar(b, rstd, half, DV)
            else:
                scale_on_vector(b, rstd, half, cuts[2])
                (scale_on_scalar if b == 2 else scale_on_vector)(b, rstd, cuts[2], DV)
            store(b, half, DV)

        rstd0 = inverse_root(0, sum_squares(0, cuts[2], DV, 0))
        finish(0, rstd0)
        sum_sq1 = sum_squares(1, cuts[2], DV, 64)
        sum_sq2 = sum_squares(2, cuts[2], DV, 0)
        finish(1, inverse_root(1, sum_sq1))
        rstd2 = inverse_root(2, sum_sq2)
        sum_sq3 = sum_squares(LAST, 0, DV, 64)
        finish(2, rstd2)
        finish(LAST, inverse_root(LAST, sum_sq3))
